import numpy as np
import ml_dtypes


def mxq(x, axis, fmt="e4m3"):
    dtype, down = {"e4m3": (ml_dtypes.float8_e4m3fn, 7), "e5m2": (ml_dtypes.float8_e5m2, 14)}[fmt]
    v = np.moveaxis(np.asarray(x, np.float32).astype(ml_dtypes.bfloat16).astype(np.float64), axis, -1)
    blocks = v.reshape(v.shape[:-1] + (-1, 32))
    amax = np.abs(blocks).max(-1, keepdims=True)
    byte = np.maximum(np.where(amax > 0, np.frexp(amax)[1] - 1 + 127, 0) - down, 1)
    scale = np.exp2(byte - 127.0)
    codes = (blocks / scale).astype(np.float32).astype(dtype).astype(np.float64)
    return np.moveaxis((codes * scale).reshape(v.shape), -1, axis)


WIDE = False


def mx_kscale(k):
    if not WIDE:
        return np.ones(k)
    levels = np.array([10, -10, 5, -5, 0])
    if k % 512:
        return np.exp2(np.random.permutation(np.resize(levels, k // 32))).repeat(32)
    a = np.empty((k // 512, 16))
    for p in range(k // 512):
        a[p, :8] = np.random.permutation(np.resize(levels, 8))
        for g in range(8):
            far = levels[np.abs(levels - a[p, g]) >= 10]
            a[p, g + 8] = far[np.random.randint(len(far))]
    return np.exp2(a.ravel()).repeat(32)


def f64(x):
    return np.asarray(x).astype(np.float64)


def striped(idx):
    return np.tile(idx.reshape(-1, 16).T, (8, 1)).astype(np.uint16)


def unstriped(offs):
    return offs[:16].T.reshape(-1).astype(np.int64)


E2M1 = np.array([0.0, 0.5, 1.0, 1.5, 2.0, 3.0, 4.0, 6.0, -0.0, -0.5, -1.0, -1.5, -2.0, -3.0, -4.0, -6.0])


def pack_weight(w, fmt):
    k, n = w.shape
    w = f64(np.asarray(w, np.float32).astype(ml_dtypes.bfloat16)).reshape(k // 32, 32, n)
    amax = np.abs(w).max(1)
    if fmt == "e4m3":
        byte = np.frexp(amax)[1] - 1 + 127 - 7
    else:
        mant, ex = np.frexp(amax / 6.0)
        byte = np.where(mant > 0.5, ex, ex - 1) + 127
    byte = np.clip(np.where(amax > 0, byte, 1), 1, 254)
    scaled = (w * np.exp2(127.0 - byte)[:, None, :]).reshape(k, n).astype(np.float32)
    by_word = np.ascontiguousarray(scaled.reshape(k // 512, 128, 4, n).transpose(0, 1, 3, 2))
    if fmt == "e4m3":
        words = by_word.astype(ml_dtypes.float8_e4m3fn).view(np.uint8)
    else:
        c = by_word.astype(ml_dtypes.float4_e2m1fn).view(np.uint8) & 0xF
        words = (c[..., 0::2] | (c[..., 1::2] << 4)).reshape(k // 512, 128, 2 * n)
    return np.ascontiguousarray(words), np.ascontiguousarray(byte.astype(np.uint8).reshape(k // 512, 16, n))


def unpack_weight(words, scales, fmt):
    g, _, n = scales.shape
    words = np.ascontiguousarray(words).reshape(g, 128, n, -1)
    if fmt == "e4m3":
        vals = words.view(ml_dtypes.float8_e4m3fn).astype(np.float64)
    else:
        nib = np.empty((g, 128, n, 4), np.uint8)
        nib[..., 0::2] = words & 0xF
        nib[..., 1::2] = words >> 4
        vals = E2M1[nib]
    vals = vals * np.repeat(np.exp2(scales.astype(np.float64) - 127.0), 8, axis=1)[..., None]
    return vals.transpose(0, 1, 3, 2).reshape(g * 512, n)


def gelu(v):
    return 0.5 * v * (1.0 + np.tanh(np.sqrt(2.0 / np.pi) * (v + 0.044715 * v**3)))


K, H, N, T, S, P = 1024, 1024, 512, 2048, 1024, 512

def setup_inputs():
    n = np.random.standard_normal
    s = mx_kscale(K)[:, None]
    u = mx_kscale(H)[:, None]
    tab_words, tab_scales = pack_weight(n((K, T)) * s, "e4m3")
    w1 = n((K, H)) / np.sqrt(K) / s
    w2_words, w2_scales = pack_weight(n((K, H)) / np.sqrt(K) / s * u.T, "e2m1")
    w3_words, w3_scales = pack_weight(0.6 * n((H, N)) / np.sqrt(H) / u, "e4m3")
    return {
        "tab_words": tab_words, "tab_scales": tab_scales,
        "offs": striped(np.random.permutation(T)[:S]),
        "pos1": striped(np.random.permutation(S)[:P]),
        "pos2": striped(np.random.permutation(S)[:P]),
        "pos3": striped(np.random.permutation(S)[:P]),
        "w1": w1.astype(np.float32),
        "w2_words": w2_words, "w2_scales": w2_scales,
        "w3_words": w3_words, "w3_scales": w3_scales,
        "cg": (np.exp(0.3 * n(H)) * u[:, 0]).astype(np.float32),
        "rl": np.exp(0.3 * n(N)).astype(np.float32),
    }

def reference(tab_words, tab_scales, offs, pos1, pos2, pos3, w1, w2_words, w2_scales,
              w3_words, w3_scales, cg, rl):
    v = unpack_weight(tab_words, tab_scales, "e4m3")[:, unstriped(offs)]
    w2 = unpack_weight(w2_words, w2_scales, "e2m1")
    w3 = unpack_weight(w3_words, w3_scales, "e4m3")
    x = mxq(f64(w1), 0, "e4m3").T @ v
    y = w2.T @ v
    z1 = np.abs(x[:, unstriped(pos1)]) * x[:, unstriped(pos2)] * f64(cg)[:, None]
    z2 = y[:, unstriped(pos3)]
    o1 = w3.T @ mxq(z1, 0, "e4m3")
    o2 = w3.T @ mxq(z2, 0, "e4m3")
    return np.tanh(f64(rl)[:, None] * o1 - o2)

@@ -1,0 +1,333 @@
+from contextlib import ExitStack
+
+import concourse.mybir as mybir
+
+K, H, N, T, S, M = 1024, 1024, 512, 2048, 1024, 512
+FLOPS = 2 * K * H * S * 2 + 2 * H * N * M * 2
+
+F32 = mybir.dt.float32
+BF16 = mybir.dt.bfloat16
+I32 = mybir.dt.int32
+U32 = mybir.dt.uint32
+U16 = mybir.dt.uint16
+U8 = mybir.dt.uint8
+E4M3 = mybir.dt.float8_e4m3fn_x4
+E2M1 = mybir.dt.float4_e2m1fn_x4
+ALU = mybir.AluOpType
+ACT = mybir.ActivationFunctionType
+
+P = 128
+PACK = 4
+PASS = P * PACK
+BANK = 512
+CAST = ["g","g","g","g"]
+WEAVE2 = ["s","s"]
+PIECES = [256,256]
+
+
+def tile_list_crack_hedge_tilt_kernel(tc, tab_words, tab_scales, offs, pos1, pos2, pos3, w1,
+                                                w2_words, w2_scales, w3_words, w3_scales, cg, rl, out):
+    nc = tc.nc
+    with ExitStack() as ctx:
+        keep = ctx.enter_context(tc.tile_pool(name="keep", bufs=1))
+        ring = ctx.enter_context(tc.tile_pool(name="ring", bufs=2))
+        psum = ctx.enter_context(tc.psum_pool(name="psum", bufs=1))
+
+        def held(shape, dtype, name):
+            return keep.tile(shape, dtype, name=name, align_bytes=64)
+
+        def bank(b, width=BANK):
+            return psum.tile([P, width], F32, name="bank", tag="bank%d" % b)
+
+        offs_sb = keep.tile([P, S // 16], U16, name="offs_sb")
+        pos1_sb = keep.tile([P, M // 16], U16, name="pos1_sb")
+        pos2_sb = keep.tile([P, M // 16], U16, name="pos2_sb")
+        pos3_sb = keep.tile([P, M // 16], U16, name="pos3_sb")
+        tab_w = [held([P, T], I32, "tab_w%d" % a) for a in range(2)]
+        tab_s = held([P, T], U8, "tab_s")
+        v_w = [held([P, S], I32, "v_w%d" % a) for a in range(2)]
+        v_s = held([P, S], U8, "v_s")
+        v_s1 = held([P, S], U8, "v_s1")
+        w2_raw = held([P, 2 * H * 2], U8, "w2_raw")
+        w2_sraw = held([P, 2 * H], U8, "w2_sraw")
+        w2_w = [held([P, 2 * PASS * 2], U8, "w2_w%d" % b) for b in range(2)]
+        w2_s = [held([P, 2 * PASS], U8, "w2_s%d" % b) for b in range(2)]
+        w1_raw = [[held([P, PACK * PASS], F32, "w1_raw%d%d" % (a, b)) for b in range(2)] for a in range(2)]
+        w1_bf = [[held([P, PACK * PASS], BF16, "w1_bf%d%d" % (a, b)) for b in range(2)] for a in range(2)]
+        w1_w = [[held([P, PASS], U32, "w1_w%d%d" % (a, b)) for b in range(2)] for a in range(2)]
+        w1_s = [[held([P, PASS], U8, "w1_s%d%d" % (a, b)) for b in range(2)] for a in range(2)]
+        w3_w = held([P, 2 * N], I32, "w3_w")
+        w3_s = held([P, N], U8, "w3_s")
+        cg_sb = held([P, 2 * PACK], F32, "cg_sb")
+        cg_ge = held([P, 2 * PACK], F32, "cg_ge")
+        cg_sign = held([P, 2 * PACK], F32, "cg_sign")
+        rl_sb = held([P, N // P], F32, "rl_sb")
+        warm = held([P, 8], F32, "warm")
+        warm2 = held([P, 8], F32, "warm2")
+        o2_sb = [held([P, M], F32, "o2_sb%d" % n) for n in range(N // P)]
+
+        nc.vector.memset(tab_s[:].bitcast(I32), 0)
+        nc.vector.memset(w2_sraw[:].bitcast(I32), 0)
+        nc.vector.memset(warm[:], 0.0)
+        nc.vector.memset(v_s1[:].bitcast(I32), 0)
+        nc.vector.memset(w3_s[:].bitcast(I32), 0)
+
+        def load_words(a):
+            nc.sync.dma_start(tab_w[a][:], tab_words[a].rearrange("p t i -> p (t i)").bitcast(I32))
+
+        def load_w1(a, b):
+            src = w1[PASS * a:PASS * (a + 1), PASS * b:PASS * (b + 1)].rearrange("(p j) c -> p j c", j=PACK)
+            nc.sync.dma_start(w1_raw[a][b][:].rearrange("p (j c) -> p j c", j=PACK), src)
+
+        nc.sync.dma_start(offs_sb[:], offs)
+        load_words(0)
+        for q in range(4):
+            nc.scalar.dma_start(tab_s[32 * q:32 * q + 8, :].bitcast(I32), tab_scales[:, 4 * q:4 * q + 4, :].bitcast(I32))
+        nc.sync.dma_start(w2_raw[:].bitcast(I32).rearrange("p (a c) -> p a c", a=2),
+                          w2_words.bitcast(I32).rearrange("a p c -> p a c"))
+        load_words(1)
+        for q in range(4):
+            nc.scalar.dma_start(w2_sraw[32 * q:32 * q + 4, :].bitcast(I32).rearrange("p (a c) -> p a c", a=2),
+                                w2_scales[:, 4 * q:4 * q + 4, :].bitcast(I32).rearrange("a r c -> r a c"))
+        nc.scalar.activation(warm2[:], warm[:], ACT.Tanh)
+        nc.sync.dma_start(pos3_sb[:], pos3)
+        load_w1(0, 0)
+        load_w1(1, 0)
+        nc.sync.dma_start(cg_sb[:].rearrange("p (b t) -> p b t", b=2), cg.rearrange("(b p t) -> p b t", b=2, t=PACK))
+        nc.sync.dma_start(pos1_sb[:], pos1)
+        nc.sync.dma_start(pos2_sb[:], pos2)
+        load_w1(0, 1)
+        load_w1(1, 1)
+        nc.sync.dma_start(w3_w[:].rearrange("p (a c) -> p a c", a=2),
+                          w3_words.rearrange("a p c i -> p a (c i)").bitcast(I32))
+        for q in range(4):
+            nc.sync.dma_start(w3_s[32 * q:32 * q + 8, :].bitcast(I32), w3_scales[:, 4 * q:4 * q + 4, :].bitcast(I32))
+        with nc.allow_non_contiguous_dma(reason="one ratio for each partition"):
+            nc.sync.dma_start(rl_sb[:], rl.rearrange("(n p) -> p n", p=P))
+
+        nc.gpsimd.tensor_scalar(cg_ge[:], cg_sb[:], 0.0, 2.0, ALU.is_ge, ALU.mult)
+        nc.gpsimd.tensor_scalar(cg_sign[:], cg_ge[:], -1.0, 1.0, ALU.add, ALU.mult)
+
+        def gather_words(a, lo, hi):
+            nc.vector.tensor_copy(v_w[a][:, lo:hi].bitcast(U32),
+                                  tab_w[a][:].bitcast(U32).indirect(offs_sb[:, lo // 16:hi // 16]))
+
+        def order_w2(b):
+            for a in range(2):
+                src = w2_raw[:].bitcast(U16)[:, H * a + PASS * b:H * a + PASS * (b + 1)]
+                dst = w2_w[b][:].bitcast(U16)[:, PASS * a:PASS * (a + 1)]
+                nc.vector.tensor_copy(dst.rearrange("p (t c i) -> p c t i", t=PACK, i=8),
+                                      src.rearrange("p (c i t) -> p c t i", t=PACK, i=8))
+            src = w2_sraw[:].rearrange("p (a b c i t) -> p b a c t i", a=2, b=2, t=PACK, i=16)[:, b]
+            dst = w2_s[b][:].rearrange("p (a t c i) -> p a c t i", a=2, t=PACK, i=16)
+            nc.vector.tensor_copy(dst, src)
+
+        gather_words(0, 0, S)
+        nc.vector.tensor_copy(v_s[:], tab_s[:].indirect(offs_sb[:]))
+        for q in range(4):
+            nc.scalar.dma_start(v_s1[32 * q:32 * q + 4, :].bitcast(I32), v_s[32 * q + 4:32 * q + 8, :].bitcast(I32))
+        order_w2(0)
+        gather_words(1, 0, BANK)
+        gather_words(1, BANK, S)
+        order_w2(1)
+
+        def cast_w1(a, b):
+            dst = w1_bf[a][b][:].rearrange("p (t m j) -> p m j t", t=PACK, j=PACK)
+            src = w1_raw[a][b][:].rearrange("p (j m t) -> p m j t", t=PACK, j=PACK)
+            eng = CAST[2 * b + a]
+            if eng == "g":
+                nc.gpsimd.tensor_scalar(dst, src, 1.0, 0.0, ALU.mult, ALU.add)
+            elif eng == "s":
+                nc.scalar.copy(dst, src)
+            else:
+                nc.vector.tensor_copy(dst, src)
+
+        def quantize_w1(a, b):
+            nc.vector.quantize_mx(out=w1_w[a][b][:].bitcast(E4M3), scales=w1_s[a][b][:], in_=w1_bf[a][b][:])
+
+        def y_pass(acc, b, t, h, a):
+            cols = slice(BANK * h, BANK * (h + 1))
+            c0 = PASS * a + P * t
+            plane = v_s if a == 0 else v_s1
+            nc.tensor.matmul_mx(out=acc[:], lhsT=w2_w[b][:, 2 * c0:2 * (c0 + P)].bitcast(E2M1), lhsT_scale=w2_s[b][:, c0:c0 + P],
+                                rhs=v_w[a][:, cols].bitcast(E4M3), rhs_scale=plane[:, cols], start=(a == 0), stop=(a == 1))
+
+        def x_pass(acc, b, t, h, a):
+            cols = slice(BANK * h, BANK * (h + 1))
+            wc = slice(P * t, P * (t + 1))
+            nc.tensor.matmul_mx(out=acc[:], lhsT=w1_w[a][b][:, wc].bitcast(E4M3), lhsT_scale=w1_s[a][b][:, wc],
+                                rhs=v_w[a][:, cols].bitcast(E4M3), rhs_scale=v_s[4 * a:, cols], start=(a == 0), stop=(a == 1))
+
+        def window():
+            return ring.tile([P, S], F32, name="window", tag="window", bufs=6, align_bytes=64)
+
+        def weave(eng, dst, planes, width):
+            d = dst.rearrange("p (c i t) -> p c t i", t=PACK, i=4)
+            s = planes.rearrange("p (t c i) -> p c t i", t=PACK, i=4)
+            if eng == "g":
+                nc.gpsimd.tensor_scalar(d, s, 1.0, 0.0, ALU.mult, ALU.add)
+            elif eng == "s":
+                nc.scalar.copy(d, s)
+            else:
+                nc.vector.tensor_copy(d, s)
+
+        def quantize_z(name, woven, width):
+            codes = held([P, width], U32, name + "_w")
+            plane = held([P, width], U8, name + "_s")
+            nc.vector.quantize_mx(out=codes[:].bitcast(E4M3), scales=plane[:], in_=woven)
+            return codes, plane
+
+        def o_pass(acc, n, a, z, cols, start, stop):
+            c0 = N * a + P * n
+            nc.tensor.matmul_mx(out=acc[:], lhsT=w3_w[:, c0:c0 + P].bitcast(E4M3), lhsT_scale=w3_s[4 * a:, P * n:P * (n + 1)],
+                                rhs=z[0][:, cols].bitcast(E4M3), rhs_scale=z[1][:, cols], start=start, stop=stop)
+
+        z2_planes = [held([P, PACK * M], BF16, "z2_planes%d" % b) for b in range(2)]
+        z2_woven = [held([P, PACK * M], BF16, "z2_woven%d" % b) for b in range(2)]
+        z2 = [None, None]
+        first = [[bank(2 * t + h) for h in range(2)] for t in range(PACK)]
+        first_win = [window() for t in range(PACK)]
+        for t in range(PACK):
+            for h in range(2):
+                y_pass(first[t][h], 0, t, h, 0)
+        for t in range(PACK):
+            y_pass(first[t][0], 0, t, 0, 1)
+        for t in range(2):
+            nc.scalar.copy(first_win[t][:, 0:BANK], first[t][0][:])
+        for t in range(PACK):
+            y_pass(first[t][1], 0, t, 1, 1)
+
+        for i in range(2 * PACK):
+            b, t = divmod(i, PACK)
+            if b == 0:
+                win = first_win[t]
+                for h in range(1 if t < 2 else 0, 2):
+                    nc.scalar.copy(win[:, BANK * h:BANK * (h + 1)], first[t][h][:])
+            else:
+                win = window()
+                for h in range(2):
+                    acc = bank(2 * t + h)
+                    for a in range(2):
+                        y_pass(acc, b, t, h, a)
+                    nc.scalar.copy(win[:, BANK * h:BANK * (h + 1)], acc[:])
+            nc.vector.tensor_copy(z2_planes[b][:, M * t:M * (t + 1)], win[:].indirect(pos3_sb[:]))
+            if i in [0,1,2,3]:
+                u = [0,1,2,3].index(i)
+                cast_w1(u % 2, u // 2)
+            if i in [3,5,6,7]:
+                u = [3,5,6,7].index(i)
+                quantize_w1(u % 2, u // 2)
+
+        def x_window(b, t):
+            win = window()
+            for h in range(2):
+                acc = bank((2 * t + h) % 4)
+                for a in range(2):
+                    x_pass(acc, b, t, h, a)
+                u = PACK * b + t
+                nc.scalar.activation(win[:, BANK * h:BANK * (h + 1)], acc[:], ACT.Copy, scale=cg_sign[:, u:u + 1])
+            return win
+
+        def pick1(win, b, t, lo, hi):
+            g = ring.tile([P, M], F32, name="crude", tag="crude", bufs=3, align_bytes=64)
+            mag = ring.tile([P, M], F32, name="mag", tag="mag", bufs=3, align_bytes=64)
+            u = PACK * b + t
+            nc.vector.tensor_copy(g[:, 0:hi - lo], win[:].indirect(pos1_sb[:, lo // 16:hi // 16]))
+            nc.scalar.activation(mag[:, 0:hi - lo], g[:, 0:hi - lo], ACT.Abs, scale=cg_sb[:, u:u + 1])
+            return mag
+
+        def pick2(win, mag, planes, t, lo, hi):
+            width = hi - lo
+            nc.vector.tensor_tensor(planes[:, width * t:width * (t + 1)], win[:].indirect(pos2_sb[:, lo // 16:hi // 16]),
+                                    mag[:, 0:width], ALU.mult)
+
+        extra = {"0":["w0"],"1":["z0","w1"],"2":["z1"],"3":["o0"],"4":["W0"],"5":["Z0"]}
+
+        def do_extra(step):
+            for what in extra.get(str(step), []):
+                kind, u = what[0], int(what[1])
+                if kind == "c":
+                    cast_w1(u % 2, u // 2)
+                elif kind == "q":
+                    quantize_w1(u % 2, u // 2)
+                elif kind == "w":
+                    weave(WEAVE2[u], z2_woven[u][:], z2_planes[u][:], M)
+                elif kind == "z":
+                    z2[u] = quantize_z("z2_%d" % u, z2_woven[u][:], M)
+                elif kind == "o":
+                    for n in range(N // P):
+                        acc = bank(4 + n)
+                        for a in range(2):
+                            o_pass(acc, n, a, z2[a], slice(0, M), a == 0, a == 1)
+                        nc.scalar.copy(o2_sb[n][:], acc[:])
+                elif kind == "W":
+                    weave("s", z1_woven0[:], z1_planes0[:], M)
+                elif kind == "Z":
+                    z1_first.append(quantize_z("z1_0", z1_woven0[:], M))
+
+        z1_planes0 = held([P, PACK * M], F32, "z1_planes0")
+        z1_woven0 = held([P, PACK * M], BF16, "z1_woven0")
+        z1_first = []
+        edges = [sum(PIECES[:u]) for u in range(len(PIECES) + 1)]
+        tail_planes = [held([P, PACK * w], F32, "z1_planes1%d" % u) for u, w in enumerate(PIECES)]
+        tail_woven = [held([P, PACK * w], BF16, "z1_woven1%d" % u) for u, w in enumerate(PIECES)]
+
+        steps = [(0, t, 0, M, z1_planes0) for t in range(PACK)]
+        for u in range(len(PIECES)):
+            steps.extend([(1, t, edges[u], edges[u + 1], tail_planes[u]) for t in range(PACK)])
+
+        def finish_a(u):
+            weave(["s","v"][u], tail_woven[u][:], tail_planes[u][:], PIECES[u])
+
+        def finish_b(u):
+            lo, hi = edges[u], edges[u + 1]
+            width = hi - lo
+            z = quantize_z("z1_1%d" % u, tail_woven[u][:], width)
+            accs = []
+            for n in range(N // P):
+                acc = bank((4 if u % 2 == 0 else 0) + n, width)
+                o_pass(acc, n, 0, z1_first[0], slice(lo, hi), True, False)
+                accs.append(acc)
+            for n in range(N // P):
+                o_pass(accs[n], n, 1, z, slice(0, width), False, True)
+            return accs
+
+        def finish_c(u, accs):
+            lo, hi = edges[u], edges[u + 1]
+            width = hi - lo
+            for half in range(2):
+                diff = held([P, 2 * width], F32, "diff%d%d" % (u, half))
+                tilt = held([P, 2 * width], F32, "tilt%d%d" % (u, half))
+                for e in range(2):
+                    n = 2 * half + e
+                    nc.vector.scalar_tensor_tensor(diff[:, width * e:width * (e + 1)], accs[n][:], rl_sb[:, n:n + 1],
+                                                   o2_sb[n][:, lo:hi], ALU.mult, ALU.subtract)
+                nc.scalar.activation(tilt[:], diff[:], ACT.Tanh)
+                dst = out[2 * P * half:2 * P * (half + 1), lo:hi].rearrange("(e p) m -> p e m", p=P)
+                nc.sync.dma_start(dst, tilt[:].rearrange("p (e m) -> p e m", e=2))
+
+        wins = {}
+        wins[(0, 0)] = x_window(0, 0)
+        pending = None
+        accs_of = {}
+        for s, (b, t, lo, hi, planes) in enumerate(steps):
+            if s + 1 < 2 * PACK:
+                nb, nt = divmod(s + 1, PACK)
+                wins[(nb, nt)] = x_window(nb, nt)
+            mag = pick1(wins[(b, t)], b, t, lo, hi)
+            if pending is not None:
+                pick2(*pending)
+            pending = (wins[(b, t)], mag, planes, t, lo, hi)
+            do_extra(s)
+            if s >= 2 * PACK:
+                u, r = divmod(s - 2 * PACK, PACK)
+                if r == 0:
+                    finish_a(u)
+                if r == 1:
+                    accs_of[u] = finish_b(u)
+                if r == 2:
+                    finish_c(u, accs_of[u])
+        pick2(*pending)
+        last = len(PIECES) - 1
+        finish_a(last)
+        finish_c(last, finish_b(last))

@@ -20,9 +20,10 @@ P = 128
 PACK = 4
 PASS = P * PACK
 BANK = 512
-CAST = ["g","g","g","g"]
-WEAVE2 = ["s","s"]
-PIECES = [256,256]
+HALF = 256
+CAST = ["s","v","v","s","s","s","s","s"]
+WEAVE2 = ["s","s","s","v"]
+PIECES = [256,128,128]
 
 
 def tile_list_crack_hedge_tilt_kernel(tc, tab_words, tab_scales, offs, pos1, pos2, pos3, w1,
@@ -44,15 +45,15 @@ def tile_list_crack_hedge_tilt_kernel(tc, tab_words, tab_scales, offs, pos1, pos
         pos2_sb = keep.tile([P, M // 16], U16, name="pos2_sb")
         pos3_sb = keep.tile([P, M // 16], U16, name="pos3_sb")
         tab_w = [held([P, T], I32, "tab_w%d" % a) for a in range(2)]
-        tab_s = held([P, T], U8, "tab_s")
-        v_w = [held([P, S], I32, "v_w%d" % a) for a in range(2)]
+        tab_s = keep.tile([P, T], U8, name="tab_s", tag="tab_s", align_bytes=64)
+        v_w = [held([P, S], I32, "v_w0"), held([P, S], I32, "v_w1")]
         v_s = held([P, S], U8, "v_s")
         v_s1 = held([P, S], U8, "v_s1")
-        w2_raw = held([P, 2 * H * 2], U8, "w2_raw")
+        w2_raw = [held([P, 2 * PASS * 2], U8, "w2_raw%d" % b) for b in range(2)]
         w2_sraw = held([P, 2 * H], U8, "w2_sraw")
         w2_w = [held([P, 2 * PASS * 2], U8, "w2_w%d" % b) for b in range(2)]
         w2_s = [held([P, 2 * PASS], U8, "w2_s%d" % b) for b in range(2)]
-        w1_raw = [[held([P, PACK * PASS], F32, "w1_raw%d%d" % (a, b)) for b in range(2)] for a in range(2)]
+        w1_raw = [held([P, PACK * HALF], F32, "w1_raw%d" % u) for u in range(8)]
         w1_bf = [[held([P, PACK * PASS], BF16, "w1_bf%d%d" % (a, b)) for b in range(2)] for a in range(2)]
         w1_w = [[held([P, PASS], U32, "w1_w%d%d" % (a, b)) for b in range(2)] for a in range(2)]
         w1_s = [[held([P, PASS], U8, "w1_s%d%d" % (a, b)) for b in range(2)] for a in range(2)]
@@ -75,35 +76,44 @@ def tile_list_crack_hedge_tilt_kernel(tc, tab_words, tab_scales, offs, pos1, pos
         def load_words(a):
             nc.sync.dma_start(tab_w[a][:], tab_words[a].rearrange("p t i -> p (t i)").bitcast(I32))
 
-        def load_w1(a, b):
-            src = w1[PASS * a:PASS * (a + 1), PASS * b:PASS * (b + 1)].rearrange("(p j) c -> p j c", j=PACK)
-            nc.sync.dma_start(w1_raw[a][b][:].rearrange("p (j c) -> p j c", j=PACK), src)
+        def load_w1(u):
+            b, a, e = u // 4, (u // 2) % 2, u % 2
+            c0 = PASS * b + HALF * e
+            src = w1[PASS * a:PASS * (a + 1), c0:c0 + HALF].rearrange("(p j) c -> p j c", j=PACK)
+            nc.sync.dma_start(w1_raw[u][:].rearrange("p (j c) -> p j c", j=PACK), src)
 
+        def load_w2(b):
+            nc.sync.dma_start(w2_raw[b][:].bitcast(I32).rearrange("p (a c) -> p a c", a=2),
+                              w2_words[:, :, 2 * PASS * b:2 * PASS * (b + 1)].bitcast(I32).rearrange("a p c -> p a c"))
+
+        small = nc.sync
         nc.sync.dma_start(offs_sb[:], offs)
+        load_w2(0)
+        for q in range(4):
+            nc.sync.dma_start(tab_s[32 * q:32 * q + 8, :].bitcast(I32), tab_scales[:, 4 * q:4 * q + 4, :].bitcast(I32))
+        nc.scalar.activation(warm2[:], warm[:], ACT.Tanh)
         load_words(0)
         for q in range(4):
-            nc.scalar.dma_start(tab_s[32 * q:32 * q + 8, :].bitcast(I32), tab_scales[:, 4 * q:4 * q + 4, :].bitcast(I32))
-        nc.sync.dma_start(w2_raw[:].bitcast(I32).rearrange("p (a c) -> p a c", a=2),
-                          w2_words.bitcast(I32).rearrange("a p c -> p a c"))
+            nc.sync.dma_start(w2_sraw[32 * q:32 * q + 4, :].bitcast(I32).rearrange("p (a c) -> p a c", a=2),
+                            w2_scales[:, 4 * q:4 * q + 4, :].bitcast(I32).rearrange("a r c -> r a c"))
+        for u in range(1):
+            load_w1(u)
         load_words(1)
-        for q in range(4):
-            nc.scalar.dma_start(w2_sraw[32 * q:32 * q + 4, :].bitcast(I32).rearrange("p (a c) -> p a c", a=2),
-                                w2_scales[:, 4 * q:4 * q + 4, :].bitcast(I32).rearrange("a r c -> r a c"))
-        nc.scalar.activation(warm2[:], warm[:], ACT.Tanh)
+        load_w2(1)
         nc.sync.dma_start(pos3_sb[:], pos3)
-        load_w1(0, 0)
-        load_w1(1, 0)
-        nc.sync.dma_start(cg_sb[:].rearrange("p (b t) -> p b t", b=2), cg.rearrange("(b p t) -> p b t", b=2, t=PACK))
+        for u in range(1, 4):
+            load_w1(u)
         nc.sync.dma_start(pos1_sb[:], pos1)
         nc.sync.dma_start(pos2_sb[:], pos2)
-        load_w1(0, 1)
-        load_w1(1, 1)
+        small.dma_start(cg_sb[:].rearrange("p (b t) -> p b t", b=2), cg.rearrange("(b p t) -> p b t", b=2, t=PACK))
+        for u in range(4, 8):
+            load_w1(u)
         nc.sync.dma_start(w3_w[:].rearrange("p (a c) -> p a c", a=2),
                           w3_words.rearrange("a p c i -> p a (c i)").bitcast(I32))
         for q in range(4):
-            nc.sync.dma_start(w3_s[32 * q:32 * q + 8, :].bitcast(I32), w3_scales[:, 4 * q:4 * q + 4, :].bitcast(I32))
+            small.dma_start(w3_s[32 * q:32 * q + 8, :].bitcast(I32), w3_scales[:, 4 * q:4 * q + 4, :].bitcast(I32))
         with nc.allow_non_contiguous_dma(reason="one ratio for each partition"):
-            nc.sync.dma_start(rl_sb[:], rl.rearrange("(n p) -> p n", p=P))
+            small.dma_start(rl_sb[:], rl.rearrange("(n p) -> p n", p=P))
 
         nc.gpsimd.tensor_scalar(cg_ge[:], cg_sb[:], 0.0, 2.0, ALU.is_ge, ALU.mult)
         nc.gpsimd.tensor_scalar(cg_sign[:], cg_ge[:], -1.0, 1.0, ALU.add, ALU.mult)
@@ -113,30 +123,27 @@ def tile_list_crack_hedge_tilt_kernel(tc, tab_words, tab_scales, offs, pos1, pos
                                   tab_w[a][:].bitcast(U32).indirect(offs_sb[:, lo // 16:hi // 16]))
 
         def order_w2(b):
-            for a in range(2):
-                src = w2_raw[:].bitcast(U16)[:, H * a + PASS * b:H * a + PASS * (b + 1)]
-                dst = w2_w[b][:].bitcast(U16)[:, PASS * a:PASS * (a + 1)]
-                nc.vector.tensor_copy(dst.rearrange("p (t c i) -> p c t i", t=PACK, i=8),
-                                      src.rearrange("p (c i t) -> p c t i", t=PACK, i=8))
+            nc.vector.tensor_copy(w2_w[b][:].bitcast(U16).rearrange("p (a t c i) -> p a c t i", a=2, t=PACK, i=8),
+                                  w2_raw[b][:].bitcast(U16).rearrange("p (a c i t) -> p a c t i", a=2, t=PACK, i=8))
             src = w2_sraw[:].rearrange("p (a b c i t) -> p b a c t i", a=2, b=2, t=PACK, i=16)[:, b]
             dst = w2_s[b][:].rearrange("p (a t c i) -> p a c t i", a=2, t=PACK, i=16)
             nc.vector.tensor_copy(dst, src)
 
-        gather_words(0, 0, S)
         nc.vector.tensor_copy(v_s[:], tab_s[:].indirect(offs_sb[:]))
-        for q in range(4):
-            nc.scalar.dma_start(v_s1[32 * q:32 * q + 4, :].bitcast(I32), v_s[32 * q + 4:32 * q + 8, :].bitcast(I32))
+        nc.scalar.dma_start(v_s1[0:100, :].bitcast(I32), v_s[4:104, :].bitcast(I32))
         order_w2(0)
+        gather_words(0, 0, BANK)
+        gather_words(0, BANK, S)
         gather_words(1, 0, BANK)
         gather_words(1, BANK, S)
-        order_w2(1)
 
-        def cast_w1(a, b):
-            dst = w1_bf[a][b][:].rearrange("p (t m j) -> p m j t", t=PACK, j=PACK)
-            src = w1_raw[a][b][:].rearrange("p (j m t) -> p m j t", t=PACK, j=PACK)
-            eng = CAST[2 * b + a]
+        def cast_w1(u):
+            b, a, e = u // 4, (u // 2) % 2, u % 2
+            eng = CAST[u]
+            dst = w1_bf[a][b][:].rearrange("p (t e m j) -> p e m j t", t=PACK, e=2, j=PACK)[:, e]
+            src = w1_raw[u][:].rearrange("p (j m t) -> p m j t", t=PACK, j=PACK)
             if eng == "g":
-                nc.gpsimd.tensor_scalar(dst, src, 1.0, 0.0, ALU.mult, ALU.add)
+                nc.gpsimd.tensor_scalar(dst.rearrange("p m j t -> p t m j"), src.rearrange("p m j t -> p t m j"), 1.0, 0.0, ALU.mult, ALU.add)
             elif eng == "s":
                 nc.scalar.copy(dst, src)
             else:
@@ -159,17 +166,20 @@ def tile_list_crack_hedge_tilt_kernel(tc, tab_words, tab_scales, offs, pos1, pos
                                 rhs=v_w[a][:, cols].bitcast(E4M3), rhs_scale=v_s[4 * a:, cols], start=(a == 0), stop=(a == 1))
 
         def window():
-            return ring.tile([P, S], F32, name="window", tag="window", bufs=6, align_bytes=64)
+            return ring.tile([P, S], F32, name="window", tag="window", bufs=7, align_bytes=64)
 
-        def weave(eng, dst, planes, width):
-            d = dst.rearrange("p (c i t) -> p c t i", t=PACK, i=4)
-            s = planes.rearrange("p (t c i) -> p c t i", t=PACK, i=4)
+        def weave(eng, woven, planes, e, parts):
             if eng == "g":
+                d = woven.rearrange("p (e m t) -> p e m t", e=parts, t=PACK)[:, e]
+                s = planes.rearrange("p (t e m) -> p e m t", e=parts, t=PACK)[:, e]
                 nc.gpsimd.tensor_scalar(d, s, 1.0, 0.0, ALU.mult, ALU.add)
-            elif eng == "s":
-                nc.scalar.copy(d, s)
             else:
-                nc.vector.tensor_copy(d, s)
+                d = woven.rearrange("p (e c i t) -> p e c t i", e=parts, t=PACK, i=4)[:, e]
+                s = planes.rearrange("p (t e c i) -> p e c t i", e=parts, t=PACK, i=4)[:, e]
+                if eng == "s":
+                    nc.scalar.copy(d, s)
+                else:
+                    nc.vector.tensor_copy(d, s)
 
         def quantize_z(name, woven, width):
             codes = held([P, width], U32, name + "_w")
@@ -185,24 +195,47 @@ def tile_list_crack_hedge_tilt_kernel(tc, tab_words, tab_scales, offs, pos1, pos
         z2_planes = [held([P, PACK * M], BF16, "z2_planes%d" % b) for b in range(2)]
         z2_woven = [held([P, PACK * M], BF16, "z2_woven%d" % b) for b in range(2)]
         z2 = [None, None]
-        first = [[bank(2 * t + h) for h in range(2)] for t in range(PACK)]
-        first_win = [window() for t in range(PACK)]
-        for t in range(PACK):
-            for h in range(2):
+        extra = {"h":["c0","c1","q0","c2","p1"],"y3":["c3"],"y4":["q1"],"y7":["c4"],"x0":["c5"],"x1":["q2","c6"],"x2":["c7"],"x3":["q3","w0"],"x4":["w1"],"x5":["z0","w2","W0"],"x6":["w3","W1"],"x7":["z1","Z0","o0","o1","o2","o3"],"x8":[]}
+
+        def do_extra(step):
+            for what in extra.get(str(step), []):
+                kind, u = what[0], int(what[1])
+                if kind == "c":
+                    cast_w1(u)
+                elif kind == "q":
+                    quantize_w1(u % 2, u // 2)
+                elif kind == "p":
+                    order_w2(u)
+                elif kind == "w":
+                    weave(WEAVE2[u], z2_woven[u // 2][:], z2_planes[u // 2][:], u % 2, 2)
+                elif kind == "z":
+                    z2[u] = quantize_z("z2_%d" % u, z2_woven[u][:], M)
+                elif kind == "o":
+                    acc = bank(4 + u)
+                    for a in range(2):
+                        o_pass(acc, u, a, z2[a], slice(0, M), a == 0, a == 1)
+                    nc.scalar.copy(o2_sb[u][:], acc[:])
+                elif kind == "W":
+                    weave("s", z1_woven0[:], z1_planes0[:], u, 2)
+                elif kind == "Z":
+                    z1_first.append(quantize_z("z1_0", z1_woven0[:], M))
+
+        do_extra("h")
+        FIRST = 2
+        first = [[bank(2 * t + h) for h in range(2)] for t in range(FIRST)]
+        first_win = [window() for t in range(FIRST)]
+        for h in range(2):
+            for t in range(FIRST):
                 y_pass(first[t][h], 0, t, h, 0)
-        for t in range(PACK):
-            y_pass(first[t][0], 0, t, 0, 1)
-        for t in range(2):
-            nc.scalar.copy(first_win[t][:, 0:BANK], first[t][0][:])
-        for t in range(PACK):
-            y_pass(first[t][1], 0, t, 1, 1)
+        for h in range(2):
+            for t in range(FIRST):
+                y_pass(first[t][h], 0, t, h, 1)
+                nc.scalar.copy(first_win[t][:, BANK * h:BANK * (h + 1)], first[t][h][:])
 
         for i in range(2 * PACK):
             b, t = divmod(i, PACK)
-            if b == 0:
+            if i < FIRST:
                 win = first_win[t]
-                for h in range(1 if t < 2 else 0, 2):
-                    nc.scalar.copy(win[:, BANK * h:BANK * (h + 1)], first[t][h][:])
             else:
                 win = window()
                 for h in range(2):
@@ -211,12 +244,7 @@ def tile_list_crack_hedge_tilt_kernel(tc, tab_words, tab_scales, offs, pos1, pos
                         y_pass(acc, b, t, h, a)
                     nc.scalar.copy(win[:, BANK * h:BANK * (h + 1)], acc[:])
             nc.vector.tensor_copy(z2_planes[b][:, M * t:M * (t + 1)], win[:].indirect(pos3_sb[:]))
-            if i in [0,1,2,3]:
-                u = [0,1,2,3].index(i)
-                cast_w1(u % 2, u // 2)
-            if i in [3,5,6,7]:
-                u = [3,5,6,7].index(i)
-                quantize_w1(u % 2, u // 2)
+            do_extra("y%d" % i)
 
         def x_window(b, t):
             win = window()
@@ -228,42 +256,20 @@ def tile_list_crack_hedge_tilt_kernel(tc, tab_words, tab_scales, offs, pos1, pos
                 nc.scalar.activation(win[:, BANK * h:BANK * (h + 1)], acc[:], ACT.Copy, scale=cg_sign[:, u:u + 1])
             return win
 
-        def pick1(win, b, t, lo, hi):
+        def pick1(win, lo, hi):
             g = ring.tile([P, M], F32, name="crude", tag="crude", bufs=3, align_bytes=64)
-            mag = ring.tile([P, M], F32, name="mag", tag="mag", bufs=3, align_bytes=64)
-            u = PACK * b + t
             nc.vector.tensor_copy(g[:, 0:hi - lo], win[:].indirect(pos1_sb[:, lo // 16:hi // 16]))
-            nc.scalar.activation(mag[:, 0:hi - lo], g[:, 0:hi - lo], ACT.Abs, scale=cg_sb[:, u:u + 1])
-            return mag
+            return g
 
-        def pick2(win, mag, planes, t, lo, hi):
+        def pick2(win, g, planes, b, t, lo, hi):
             width = hi - lo
-            nc.vector.tensor_tensor(planes[:, width * t:width * (t + 1)], win[:].indirect(pos2_sb[:, lo // 16:hi // 16]),
-                                    mag[:, 0:width], ALU.mult)
-
-        extra = {"0":["w0"],"1":["z0","w1"],"2":["z1"],"3":["o0"],"4":["W0"],"5":["Z0"]}
-
-        def do_extra(step):
-            for what in extra.get(str(step), []):
-                kind, u = what[0], int(what[1])
-                if kind == "c":
-                    cast_w1(u % 2, u // 2)
-                elif kind == "q":
-                    quantize_w1(u % 2, u // 2)
-                elif kind == "w":
-                    weave(WEAVE2[u], z2_woven[u][:], z2_planes[u][:], M)
-                elif kind == "z":
-                    z2[u] = quantize_z("z2_%d" % u, z2_woven[u][:], M)
-                elif kind == "o":
-                    for n in range(N // P):
-                        acc = bank(4 + n)
-                        for a in range(2):
-                            o_pass(acc, n, a, z2[a], slice(0, M), a == 0, a == 1)
-                        nc.scalar.copy(o2_sb[n][:], acc[:])
-                elif kind == "W":
-                    weave("s", z1_woven0[:], z1_planes0[:], M)
-                elif kind == "Z":
-                    z1_first.append(quantize_z("z1_0", z1_woven0[:], M))
+            u = PACK * b + t
+            mag = g
+            nc.scalar.activation(mag[:, 0:width], g[:, 0:width], ACT.Abs, scale=cg_sb[:, u:u + 1])
+            for tile, c0, c1 in planes:
+                w = c1 - c0
+                nc.vector.tensor_tensor(tile[:, w * t:w * (t + 1)], win[:].indirect(pos2_sb[:, c0 // 16:c1 // 16]),
+                                        mag[:, c0 - lo:c1 - lo], ALU.mult)
 
         z1_planes0 = held([P, PACK * M], F32, "z1_planes0")
         z1_woven0 = held([P, PACK * M], BF16, "z1_woven0")
@@ -272,12 +278,17 @@ def tile_list_crack_hedge_tilt_kernel(tc, tab_words, tab_scales, offs, pos1, pos
         tail_planes = [held([P, PACK * w], F32, "z1_planes1%d" % u) for u, w in enumerate(PIECES)]
         tail_woven = [held([P, PACK * w], BF16, "z1_woven1%d" % u) for u, w in enumerate(PIECES)]
 
-        steps = [(0, t, 0, M, z1_planes0) for t in range(PACK)]
+        SPLIT = 3
+        steps = [(0, t, 0, M, [(z1_planes0, 0, M)]) for t in range(PACK)]
+        every = [(tail_planes[u], edges[u], edges[u + 1]) for u in range(len(PIECES))]
+        steps.extend([(1, t, 0, M, every) for t in range(SPLIT)])
+        done_at = []
         for u in range(len(PIECES)):
-            steps.extend([(1, t, edges[u], edges[u + 1], tail_planes[u]) for t in range(PACK)])
+            steps.extend([(1, t, edges[u], edges[u + 1], [every[u]]) for t in range(SPLIT, PACK)])
+            done_at.append(len(steps) - 1)
 
         def finish_a(u):
-            weave(["s","v"][u], tail_woven[u][:], tail_planes[u][:], PIECES[u])
+            weave(["s","v","v"][u], tail_woven[u][:], tail_planes[u][:], 0, 1)
 
         def finish_b(u):
             lo, hi = edges[u], edges[u + 1]
@@ -306,28 +317,29 @@ def tile_list_crack_hedge_tilt_kernel(tc, tab_words, tab_scales, offs, pos1, pos
                 dst = out[2 * P * half:2 * P * (half + 1), lo:hi].rearrange("(e p) m -> p e m", p=P)
                 nc.sync.dma_start(dst, tilt[:].rearrange("p (e m) -> p e m", e=2))
 
+        AHEAD = 0
+        LAG = 1
         wins = {}
-        wins[(0, 0)] = x_window(0, 0)
-        pending = None
+        for s in range(AHEAD):
+            wins[divmod(s, PACK)] = x_window(*divmod(s, PACK))
+        crude = {}
         accs_of = {}
-        for s, (b, t, lo, hi, planes) in enumerate(steps):
-            if s + 1 < 2 * PACK:
-                nb, nt = divmod(s + 1, PACK)
-                wins[(nb, nt)] = x_window(nb, nt)
-            mag = pick1(wins[(b, t)], b, t, lo, hi)
-            if pending is not None:
-                pick2(*pending)
-            pending = (wins[(b, t)], mag, planes, t, lo, hi)
-            do_extra(s)
-            if s >= 2 * PACK:
-                u, r = divmod(s - 2 * PACK, PACK)
+        total = len(steps)
+        for s in range(total + LAG + 3):
+            if s + AHEAD < 2 * PACK:
+                wins[divmod(s + AHEAD, PACK)] = x_window(*divmod(s + AHEAD, PACK))
+            if s < total:
+                b, t, lo, hi, planes = steps[s]
+                crude[s] = pick1(wins[(b, t)], lo, hi)
+            if 0 <= s - LAG < total:
+                b, t, lo, hi, planes = steps[s - LAG]
+                pick2(wins[(b, t)], crude[s - LAG], planes, b, t, lo, hi)
+            do_extra("x%d" % s)
+            for u in range(len(PIECES)):
+                r = s - LAG - done_at[u]
                 if r == 0:
                     finish_a(u)
                 if r == 1:
                     accs_of[u] = finish_b(u)
                 if r == 2:
                     finish_c(u, accs_of[u])
-        pick2(*pending)
-        last = len(PIECES) - 1
-        finish_a(last)
-        finish_c(last, finish_b(last))

@@ -20,14 +20,17 @@ P = 128
 PACK = 4
 PASS = P * PACK
 BANK = 512
-HALF = 256
-CAST = ["s","v","v","s","s","s","s","s"]
-WEAVE2 = ["s","s","s","v"]
-PIECES = [256,128,128]
+TILES = H // P
+N_TILES = N // P
+STAGE_BANKS = 4
+WINDOWS = 8
+PIECES = [256, 128, 128]
+DIESEL_ON_SCALAR = (1, 3, 5, 7)
+CRUDE_ON_VECTOR = (2, 3)
 
 
 def tile_list_crack_hedge_tilt_kernel(tc, tab_words, tab_scales, offs, pos1, pos2, pos3, w1,
-                                                w2_words, w2_scales, w3_words, w3_scales, cg, rl, out):
+                                                    w2_words, w2_scales, w3_words, w3_scales, cg, rl, out):
     nc = tc.nc
     with ExitStack() as ctx:
         keep = ctx.enter_context(tc.tile_pool(name="keep", bufs=1))
@@ -37,309 +40,273 @@ def tile_list_crack_hedge_tilt_kernel(tc, tab_words, tab_scales, offs, pos1, pos
         def held(shape, dtype, name):
             return keep.tile(shape, dtype, name=name, align_bytes=64)
 
-        def bank(b, width=BANK):
-            return psum.tile([P, width], F32, name="bank", tag="bank%d" % b)
+        def bank(b):
+            return psum.tile([P, BANK], F32, name="bank", tag="bank%d" % b)
+
+        def window():
+            return ring.tile([P, S], F32, name="window", tag="window", bufs=WINDOWS, align_bytes=64)
 
         offs_sb = keep.tile([P, S // 16], U16, name="offs_sb")
         pos1_sb = keep.tile([P, M // 16], U16, name="pos1_sb")
         pos2_sb = keep.tile([P, M // 16], U16, name="pos2_sb")
         pos3_sb = keep.tile([P, M // 16], U16, name="pos3_sb")
         tab_w = [held([P, T], I32, "tab_w%d" % a) for a in range(2)]
-        tab_s = keep.tile([P, T], U8, name="tab_s", tag="tab_s", align_bytes=64)
-        v_w = [held([P, S], I32, "v_w0"), held([P, S], I32, "v_w1")]
+        tab_s = held([P, T], U8, "tab_s")
+        v_w = [held([P, S], I32, "v_w%d" % a) for a in range(2)]
         v_s = held([P, S], U8, "v_s")
         v_s1 = held([P, S], U8, "v_s1")
-        w2_raw = [held([P, 2 * PASS * 2], U8, "w2_raw%d" % b) for b in range(2)]
-        w2_sraw = held([P, 2 * H], U8, "w2_sraw")
-        w2_w = [held([P, 2 * PASS * 2], U8, "w2_w%d" % b) for b in range(2)]
-        w2_s = [held([P, 2 * PASS], U8, "w2_s%d" % b) for b in range(2)]
-        w1_raw = [held([P, PACK * HALF], F32, "w1_raw%d" % u) for u in range(8)]
-        w1_bf = [[held([P, PACK * PASS], BF16, "w1_bf%d%d" % (a, b)) for b in range(2)] for a in range(2)]
-        w1_w = [[held([P, PASS], U32, "w1_w%d%d" % (a, b)) for b in range(2)] for a in range(2)]
-        w1_s = [[held([P, PASS], U8, "w1_s%d%d" % (a, b)) for b in range(2)] for a in range(2)]
+        w2_w = [held([P, 2 * 2 * PASS], U8, "w2_w%d" % b) for b in range(2)]
+        w2_s = held([P, 2 * H], U8, "w2_s")
+        w1_raw = [[held([P, PACK * PASS], F32, "w1_raw%d%d" % (b, a)) for a in range(2)] for b in range(2)]
+        w1_w = [[held([P, PASS], U32, "w1_w%d%d" % (b, a)) for a in range(2)] for b in range(2)]
+        w1_s = [[held([P, PASS], U8, "w1_s%d%d" % (b, a)) for a in range(2)] for b in range(2)]
         w3_w = held([P, 2 * N], I32, "w3_w")
         w3_s = held([P, N], U8, "w3_s")
-        cg_sb = held([P, 2 * PACK], F32, "cg_sb")
-        cg_ge = held([P, 2 * PACK], F32, "cg_ge")
-        cg_sign = held([P, 2 * PACK], F32, "cg_sign")
-        rl_sb = held([P, N // P], F32, "rl_sb")
-        warm = held([P, 8], F32, "warm")
-        warm2 = held([P, 8], F32, "warm2")
-        o2_sb = [held([P, M], F32, "o2_sb%d" % n) for n in range(N // P)]
+        cg_sb = held([P, TILES], F32, "cg_sb")
+        cg_ge = held([P, TILES], F32, "cg_ge")
+        cg_sign = held([P, TILES], F32, "cg_sign")
+        rl_sb = held([P, N_TILES], F32, "rl_sb")
 
         nc.vector.memset(tab_s[:].bitcast(I32), 0)
-        nc.vector.memset(w2_sraw[:].bitcast(I32), 0)
-        nc.vector.memset(warm[:], 0.0)
+        nc.vector.memset(w2_s[:].bitcast(I32), 0)
         nc.vector.memset(v_s1[:].bitcast(I32), 0)
         nc.vector.memset(w3_s[:].bitcast(I32), 0)
 
         def load_words(a):
             nc.sync.dma_start(tab_w[a][:], tab_words[a].rearrange("p t i -> p (t i)").bitcast(I32))
 
-        def load_w1(u):
-            b, a, e = u // 4, (u // 2) % 2, u % 2
-            c0 = PASS * b + HALF * e
-            src = w1[PASS * a:PASS * (a + 1), c0:c0 + HALF].rearrange("(p j) c -> p j c", j=PACK)
-            nc.sync.dma_start(w1_raw[u][:].rearrange("p (j c) -> p j c", j=PACK), src)
+        def load_w1(b, a):
+            src = w1[PASS * a:PASS * (a + 1), PASS * b:PASS * (b + 1)].rearrange("(p j) c -> p j c", j=PACK)
+            nc.sync.dma_start(w1_raw[b][a][:].rearrange("p (j c) -> p j c", j=PACK), src)
 
         def load_w2(b):
-            nc.sync.dma_start(w2_raw[b][:].bitcast(I32).rearrange("p (a c) -> p a c", a=2),
+            nc.sync.dma_start(w2_w[b][:].bitcast(I32).rearrange("p (a c) -> p a c", a=2),
                               w2_words[:, :, 2 * PASS * b:2 * PASS * (b + 1)].bitcast(I32).rearrange("a p c -> p a c"))
 
-        small = nc.sync
         nc.sync.dma_start(offs_sb[:], offs)
         load_w2(0)
         for q in range(4):
             nc.sync.dma_start(tab_s[32 * q:32 * q + 8, :].bitcast(I32), tab_scales[:, 4 * q:4 * q + 4, :].bitcast(I32))
-        nc.scalar.activation(warm2[:], warm[:], ACT.Tanh)
         load_words(0)
         for q in range(4):
-            nc.sync.dma_start(w2_sraw[32 * q:32 * q + 4, :].bitcast(I32).rearrange("p (a c) -> p a c", a=2),
-                            w2_scales[:, 4 * q:4 * q + 4, :].bitcast(I32).rearrange("a r c -> r a c"))
-        for u in range(1):
-            load_w1(u)
+            nc.sync.dma_start(w2_s[32 * q:32 * q + 4, :].bitcast(I32).rearrange("p (a c) -> p a c", a=2),
+                              w2_scales[:, 4 * q:4 * q + 4, :].bitcast(I32).rearrange("a r c -> r a c"))
         load_words(1)
-        load_w2(1)
+        nc.vector.tensor_copy(v_s[:], tab_s[:].indirect(offs_sb[:]))
+        nc.sync.dma_start(v_s1[0:100, :].bitcast(I32), v_s[4:104, :].bitcast(I32))
+        load_w1(0, 0)
         nc.sync.dma_start(pos3_sb[:], pos3)
-        for u in range(1, 4):
-            load_w1(u)
+        load_w1(0, 1)
+        load_w2(1)
+        load_w1(1, 0)
+        nc.sync.dma_start(cg_sb[:].rearrange("p (b t) -> p b t", b=2), cg.rearrange("(b p t) -> p b t", b=2, t=PACK))
         nc.sync.dma_start(pos1_sb[:], pos1)
         nc.sync.dma_start(pos2_sb[:], pos2)
-        small.dma_start(cg_sb[:].rearrange("p (b t) -> p b t", b=2), cg.rearrange("(b p t) -> p b t", b=2, t=PACK))
-        for u in range(4, 8):
-            load_w1(u)
+        load_w1(1, 1)
         nc.sync.dma_start(w3_w[:].rearrange("p (a c) -> p a c", a=2),
                           w3_words.rearrange("a p c i -> p a (c i)").bitcast(I32))
         for q in range(4):
-            small.dma_start(w3_s[32 * q:32 * q + 8, :].bitcast(I32), w3_scales[:, 4 * q:4 * q + 4, :].bitcast(I32))
+            nc.sync.dma_start(w3_s[32 * q:32 * q + 8, :].bitcast(I32), w3_scales[:, 4 * q:4 * q + 4, :].bitcast(I32))
         with nc.allow_non_contiguous_dma(reason="one ratio for each partition"):
-            small.dma_start(rl_sb[:], rl.rearrange("(n p) -> p n", p=P))
+            nc.sync.dma_start(rl_sb[:], rl.rearrange("(n p) -> p n", p=P))
 
         nc.gpsimd.tensor_scalar(cg_ge[:], cg_sb[:], 0.0, 2.0, ALU.is_ge, ALU.mult)
         nc.gpsimd.tensor_scalar(cg_sign[:], cg_ge[:], -1.0, 1.0, ALU.add, ALU.mult)
 
-        def gather_words(a, lo, hi):
-            nc.vector.tensor_copy(v_w[a][:, lo:hi].bitcast(U32),
-                                  tab_w[a][:].bitcast(U32).indirect(offs_sb[:, lo // 16:hi // 16]))
+        for a in range(2):
+            for h in range(2):
+                nc.vector.tensor_copy(v_w[a][:, BANK * h:BANK * (h + 1)].bitcast(U32),
+                                      tab_w[a][:].bitcast(U32).indirect(offs_sb[:, BANK * h // 16:BANK * (h + 1) // 16]))
 
-        def order_w2(b):
-            nc.vector.tensor_copy(w2_w[b][:].bitcast(U16).rearrange("p (a t c i) -> p a c t i", a=2, t=PACK, i=8),
-                                  w2_raw[b][:].bitcast(U16).rearrange("p (a c i t) -> p a c t i", a=2, t=PACK, i=8))
-            src = w2_sraw[:].rearrange("p (a b c i t) -> p b a c t i", a=2, b=2, t=PACK, i=16)[:, b]
-            dst = w2_s[b][:].rearrange("p (a t c i) -> p a c t i", a=2, t=PACK, i=16)
-            nc.vector.tensor_copy(dst, src)
-
-        nc.vector.tensor_copy(v_s[:], tab_s[:].indirect(offs_sb[:]))
-        nc.scalar.dma_start(v_s1[0:100, :].bitcast(I32), v_s[4:104, :].bitcast(I32))
-        order_w2(0)
-        gather_words(0, 0, BANK)
-        gather_words(0, BANK, S)
-        gather_words(1, 0, BANK)
-        gather_words(1, BANK, S)
-
-        def cast_w1(u):
-            b, a, e = u // 4, (u // 2) % 2, u % 2
-            eng = CAST[u]
-            dst = w1_bf[a][b][:].rearrange("p (t e m j) -> p e m j t", t=PACK, e=2, j=PACK)[:, e]
-            src = w1_raw[u][:].rearrange("p (j m t) -> p m j t", t=PACK, j=PACK)
-            if eng == "g":
-                nc.gpsimd.tensor_scalar(dst.rearrange("p m j t -> p t m j"), src.rearrange("p m j t -> p t m j"), 1.0, 0.0, ALU.mult, ALU.add)
-            elif eng == "s":
-                nc.scalar.copy(dst, src)
+        def pick(on_scalar, dst, win, places):
+            if on_scalar:
+                nc.scalar.activation(dst, win[:].indirect(places), ACT.Copy)
             else:
-                nc.vector.tensor_copy(dst, src)
+                nc.vector.tensor_copy(dst, win[:].indirect(places))
 
-        def quantize_w1(a, b):
-            nc.vector.quantize_mx(out=w1_w[a][b][:].bitcast(E4M3), scales=w1_s[a][b][:], in_=w1_bf[a][b][:])
-
-        def y_pass(acc, b, t, h, a):
-            cols = slice(BANK * h, BANK * (h + 1))
-            c0 = PASS * a + P * t
-            plane = v_s if a == 0 else v_s1
-            nc.tensor.matmul_mx(out=acc[:], lhsT=w2_w[b][:, 2 * c0:2 * (c0 + P)].bitcast(E2M1), lhsT_scale=w2_s[b][:, c0:c0 + P],
-                                rhs=v_w[a][:, cols].bitcast(E4M3), rhs_scale=plane[:, cols], start=(a == 0), stop=(a == 1))
-
-        def x_pass(acc, b, t, h, a):
-            cols = slice(BANK * h, BANK * (h + 1))
-            wc = slice(P * t, P * (t + 1))
-            nc.tensor.matmul_mx(out=acc[:], lhsT=w1_w[a][b][:, wc].bitcast(E4M3), lhsT_scale=w1_s[a][b][:, wc],
-                                rhs=v_w[a][:, cols].bitcast(E4M3), rhs_scale=v_s[4 * a:, cols], start=(a == 0), stop=(a == 1))
-
-        def window():
-            return ring.tile([P, S], F32, name="window", tag="window", bufs=7, align_bytes=64)
-
-        def weave(eng, woven, planes, e, parts):
-            if eng == "g":
-                d = woven.rearrange("p (e m t) -> p e m t", e=parts, t=PACK)[:, e]
-                s = planes.rearrange("p (t e m) -> p e m t", e=parts, t=PACK)[:, e]
-                nc.gpsimd.tensor_scalar(d, s, 1.0, 0.0, ALU.mult, ALU.add)
-            else:
-                d = woven.rearrange("p (e c i t) -> p e c t i", e=parts, t=PACK, i=4)[:, e]
-                s = planes.rearrange("p (t e c i) -> p e c t i", e=parts, t=PACK, i=4)[:, e]
-                if eng == "s":
-                    nc.scalar.copy(d, s)
-                else:
-                    nc.vector.tensor_copy(d, s)
-
-        def quantize_z(name, woven, width):
+        def quantize(name, woven, width):
             codes = held([P, width], U32, name + "_w")
             plane = held([P, width], U8, name + "_s")
-            nc.vector.quantize_mx(out=codes[:].bitcast(E4M3), scales=plane[:], in_=woven)
+            nc.vector.quantize_mx(out=codes[:].bitcast(E4M3), scales=plane[:], in_=woven[:])
             return codes, plane
+
+        w1_bf = {}
+
+        def round_w1(b, a):
+            w1_bf[b, a] = ring.tile([P, PACK * PASS], BF16, name="w1_bf", tag="w1_bf", align_bytes=64)
+            nc.vector.tensor_copy(w1_bf[b, a][:].rearrange("p (t m j) -> p m j t", t=PACK, j=PACK),
+                                  w1_raw[b][a][:].rearrange("p (j m t) -> p m j t", t=PACK, j=PACK))
+
+        def quantize_w1(b, a):
+            nc.vector.quantize_mx(out=w1_w[b][a][:].bitcast(E4M3), scales=w1_s[b][a][:], in_=w1_bf[b, a][:])
+
+        def y_pass(acc, i, h, a):
+            b, t = divmod(i, PACK)
+            cols = slice(BANK * h, BANK * (h + 1))
+            c0 = PASS * a + P * t
+            s0 = H * a + P * i
+            plane = v_s if a == 0 else v_s1
+            nc.tensor.matmul_mx(out=acc[:], lhsT=w2_w[b][:, 2 * c0:2 * (c0 + P)].bitcast(E2M1), lhsT_scale=w2_s[:, s0:s0 + P],
+                                rhs=v_w[a][:, cols].bitcast(E4M3), rhs_scale=plane[:, cols], start=(a == 0), stop=(a == 1))
+
+        def x_pass(acc, i, h, a):
+            b, t = divmod(i, PACK)
+            cols = slice(BANK * h, BANK * (h + 1))
+            wc = slice(P * t, P * (t + 1))
+            nc.tensor.matmul_mx(out=acc[:], lhsT=w1_w[b][a][:, wc].bitcast(E4M3), lhsT_scale=w1_s[b][a][:, wc],
+                                rhs=v_w[a][:, cols].bitcast(E4M3), rhs_scale=v_s[4 * a:, cols], start=(a == 0), stop=(a == 1))
 
         def o_pass(acc, n, a, z, cols, start, stop):
             c0 = N * a + P * n
-            nc.tensor.matmul_mx(out=acc[:], lhsT=w3_w[:, c0:c0 + P].bitcast(E4M3), lhsT_scale=w3_s[4 * a:, P * n:P * (n + 1)],
+            nc.tensor.matmul_mx(out=acc, lhsT=w3_w[:, c0:c0 + P].bitcast(E4M3), lhsT_scale=w3_s[4 * a:, P * n:P * (n + 1)],
                                 rhs=z[0][:, cols].bitcast(E4M3), rhs_scale=z[1][:, cols], start=start, stop=stop)
 
-        z2_planes = [held([P, PACK * M], BF16, "z2_planes%d" % b) for b in range(2)]
-        z2_woven = [held([P, PACK * M], BF16, "z2_woven%d" % b) for b in range(2)]
-        z2 = [None, None]
-        extra = {"h":["c0","c1","q0","c2","p1"],"y3":["c3"],"y4":["q1"],"y7":["c4"],"x0":["c5"],"x1":["q2","c6"],"x2":["c7"],"x3":["q3","w0"],"x4":["w1"],"x5":["z0","w2","W0"],"x6":["w3","W1"],"x7":["z1","Z0","o0","o1","o2","o3"],"x8":[]}
+        z2_rows = [held([P, PACK * M], BF16, "z2_rows%d" % b) for b in range(2)]
 
-        def do_extra(step):
-            for what in extra.get(str(step), []):
-                kind, u = what[0], int(what[1])
-                if kind == "c":
-                    cast_w1(u)
-                elif kind == "q":
-                    quantize_w1(u % 2, u // 2)
-                elif kind == "p":
-                    order_w2(u)
-                elif kind == "w":
-                    weave(WEAVE2[u], z2_woven[u // 2][:], z2_planes[u // 2][:], u % 2, 2)
-                elif kind == "z":
-                    z2[u] = quantize_z("z2_%d" % u, z2_woven[u][:], M)
-                elif kind == "o":
-                    acc = bank(4 + u)
-                    for a in range(2):
-                        o_pass(acc, u, a, z2[a], slice(0, M), a == 0, a == 1)
-                    nc.scalar.copy(o2_sb[u][:], acc[:])
-                elif kind == "W":
-                    weave("s", z1_woven0[:], z1_planes0[:], u, 2)
-                elif kind == "Z":
-                    z1_first.append(quantize_z("z1_0", z1_woven0[:], M))
-
-        do_extra("h")
-        FIRST = 2
-        first = [[bank(2 * t + h) for h in range(2)] for t in range(FIRST)]
-        first_win = [window() for t in range(FIRST)]
-        for h in range(2):
-            for t in range(FIRST):
-                y_pass(first[t][h], 0, t, h, 0)
-        for h in range(2):
-            for t in range(FIRST):
-                y_pass(first[t][h], 0, t, h, 1)
-                nc.scalar.copy(first_win[t][:, BANK * h:BANK * (h + 1)], first[t][h][:])
-
-        for i in range(2 * PACK):
+        def pick_diesel(i, win):
             b, t = divmod(i, PACK)
-            if i < FIRST:
-                win = first_win[t]
-            else:
-                win = window()
-                for h in range(2):
-                    acc = bank(2 * t + h)
-                    for a in range(2):
-                        y_pass(acc, b, t, h, a)
-                    nc.scalar.copy(win[:, BANK * h:BANK * (h + 1)], acc[:])
-            nc.vector.tensor_copy(z2_planes[b][:, M * t:M * (t + 1)], win[:].indirect(pos3_sb[:]))
-            do_extra("y%d" % i)
+            picked = held([P, M], BF16, "diesel%d" % i)
+            pick(i in DIESEL_ON_SCALAR, picked[:], win, pos3_sb[:])
+            nc.sync.dma_start(z2_rows[b][32 * t:32 * (t + 1), :].bitcast(I32).rearrange("p (j c) -> p j c", j=PACK),
+                              picked[:].bitcast(I32))
 
-        def x_window(b, t):
+        first = [[bank(2 * i + h) for h in range(2)] for i in range(2)]
+        y_win = [window() for i in range(2)]
+        for h in range(2):
+            for i in range(2):
+                y_pass(first[i][h], i, h, 0)
+        for h in range(2):
+            for i in range(2):
+                y_pass(first[i][h], i, h, 1)
+                nc.scalar.copy(y_win[i][:, BANK * h:BANK * (h + 1)], first[i][h][:])
+        for i in range(2, TILES + 1):
+            if i < TILES:
+                y_win.append(window())
+                for h in range(2):
+                    acc = bank((2 * i + h) % STAGE_BANKS)
+                    for a in range(2):
+                        y_pass(acc, i, h, a)
+                    nc.scalar.copy(y_win[i][:, BANK * h:BANK * (h + 1)], acc[:])
+            if i % 2 == 0:
+                round_w1(*divmod(i // 2 - 1, 2))
+                pick_diesel(i - 2, y_win[i - 2])
+                quantize_w1(*divmod(i // 2 - 1, 2))
+                pick_diesel(i - 1, y_win[i - 1])
+
+        crude = [held([P, PACK * M], F32, "crude%d" % b) for b in range(2)]
+        petrol = [held([P, PACK * M], F32, "petrol%d" % b) for b in range(2)]
+
+        def x_window(i):
             win = window()
             for h in range(2):
-                acc = bank((2 * t + h) % 4)
+                acc = bank((2 * i + h) % STAGE_BANKS)
                 for a in range(2):
-                    x_pass(acc, b, t, h, a)
-                u = PACK * b + t
-                nc.scalar.activation(win[:, BANK * h:BANK * (h + 1)], acc[:], ACT.Copy, scale=cg_sign[:, u:u + 1])
+                    x_pass(acc, i, h, a)
+                nc.scalar.activation(win[:, BANK * h:BANK * (h + 1)], acc[:], ACT.Copy, scale=cg_sign[:, i:i + 1])
             return win
 
-        def pick1(win, lo, hi):
-            g = ring.tile([P, M], F32, name="crude", tag="crude", bufs=3, align_bytes=64)
-            nc.vector.tensor_copy(g[:, 0:hi - lo], win[:].indirect(pos1_sb[:, lo // 16:hi // 16]))
-            return g
+        def pick_crude(i, win, lo, hi):
+            b, t = divmod(i, PACK)
+            pick(i not in CRUDE_ON_VECTOR, crude[b][:, M * t + lo:M * t + hi], win, pos1_sb[:, lo // 16:hi // 16])
 
-        def pick2(win, g, planes, b, t, lo, hi):
-            width = hi - lo
-            u = PACK * b + t
-            mag = g
-            nc.scalar.activation(mag[:, 0:width], g[:, 0:width], ACT.Abs, scale=cg_sb[:, u:u + 1])
-            for tile, c0, c1 in planes:
-                w = c1 - c0
-                nc.vector.tensor_tensor(tile[:, w * t:w * (t + 1)], win[:].indirect(pos2_sb[:, c0 // 16:c1 // 16]),
-                                        mag[:, c0 - lo:c1 - lo], ALU.mult)
+        def pick_petrol(i, win, lo, hi):
+            b, t = divmod(i, PACK)
+            pick(False, petrol[b][:, M * t + lo:M * t + hi], win, pos2_sb[:, lo // 16:hi // 16])
 
-        z1_planes0 = held([P, PACK * M], F32, "z1_planes0")
-        z1_woven0 = held([P, PACK * M], BF16, "z1_woven0")
-        z1_first = []
+        def size_of_crude(i, lo, hi):
+            b, t = divmod(i, PACK)
+            values = crude[b][:, M * t + lo:M * t + hi]
+            nc.scalar.activation(values, values, ACT.Abs, scale=cg_sb[:, i:i + 1])
+
+        def weave_z1(b, lo, hi):
+            woven = held([P, PACK * (hi - lo)], BF16, "z1_woven%d_%d" % (b, lo))
+            def walk(planes):
+                return planes[:].rearrange("p (t m) -> p t m", t=PACK)[:, :, lo:hi].rearrange("p t (c i) -> p c t i", i=2)
+            nc.vector.tensor_tensor(woven[:].rearrange("p (c i t) -> p c t i", t=PACK, i=2), walk(crude[b]), walk(petrol[b]), ALU.mult)
+            return woven
+
+        def weave_z2(b):
+            woven = held([P, PACK * M], BF16, "z2_woven%d" % b)
+            nc.vector.tensor_copy(woven[:].rearrange("p (c i t) -> p c t i", t=PACK, i=4),
+                                  z2_rows[b][:].rearrange("p (t c i) -> p c t i", t=PACK, i=4))
+            return woven
+
+        woven2 = []
+        z2 = []
+        o2_banks = []
+        x_win = [x_window(0)]
+        for i in range(TILES - 1):
+            x_win.append(x_window(i + 1))
+            pick_crude(i, x_win[i], 0, M)
+            pick_petrol(i, x_win[i], 0, M)
+            if i < 2:
+                woven2.append(weave_z2(i))
+            if 1 <= i < 3:
+                z2.append(quantize("z2_%d" % (i - 1), woven2[i - 1], M))
+            if i == 3:
+                for n in range(N_TILES):
+                    o2_banks.append(bank(STAGE_BANKS + n))
+                    for a in range(2):
+                        o_pass(o2_banks[n][:], n, a, z2[a], slice(0, M), a == 0, a == 1)
+            if i >= 1:
+                size_of_crude(i - 1, 0, M)
+            if i == PACK:
+                z1_first_woven = weave_z1(0, 0, M)
+            if i == PACK + 1:
+                z1_first = quantize("z1_0", z1_first_woven, M)
+
+        last = TILES - 1
         edges = [sum(PIECES[:u]) for u in range(len(PIECES) + 1)]
-        tail_planes = [held([P, PACK * w], F32, "z1_planes1%d" % u) for u, w in enumerate(PIECES)]
-        tail_woven = [held([P, PACK * w], BF16, "z1_woven1%d" % u) for u, w in enumerate(PIECES)]
+        spans = [(edges[u], edges[u + 1]) for u in range(len(PIECES))]
+        size_of_crude(last - 1, 0, M)
+        for lo, hi in spans:
+            pick_crude(last, x_win[last], lo, hi)
+            pick_petrol(last, x_win[last], lo, hi)
+        for lo, hi in spans:
+            size_of_crude(last, lo, hi)
 
-        SPLIT = 3
-        steps = [(0, t, 0, M, [(z1_planes0, 0, M)]) for t in range(PACK)]
-        every = [(tail_planes[u], edges[u], edges[u + 1]) for u in range(len(PIECES))]
-        steps.extend([(1, t, 0, M, every) for t in range(SPLIT)])
-        done_at = []
-        for u in range(len(PIECES)):
-            steps.extend([(1, t, edges[u], edges[u + 1], [every[u]]) for t in range(SPLIT, PACK)])
-            done_at.append(len(steps) - 1)
-
-        def finish_a(u):
-            weave(["s","v","v"][u], tail_woven[u][:], tail_planes[u][:], 0, 1)
-
-        def finish_b(u):
-            lo, hi = edges[u], edges[u + 1]
+        o1 = []
+        free_banks = list(range(STAGE_BANKS))
+        for lo, hi in spans:
             width = hi - lo
-            z = quantize_z("z1_1%d" % u, tail_woven[u][:], width)
-            accs = []
-            for n in range(N // P):
-                acc = bank((4 if u % 2 == 0 else 0) + n, width)
-                o_pass(acc, n, 0, z1_first[0], slice(lo, hi), True, False)
-                accs.append(acc)
-            for n in range(N // P):
-                o_pass(accs[n], n, 1, z, slice(0, width), False, True)
-            return accs
+            share = BANK // width
+            banks = [bank(free_banks.pop(0)) for g in range(N_TILES // share)]
+            o1.append([banks[n // share][:, width * (n % share):width * (n % share + 1)] for n in range(N_TILES)])
+            for n in range(N_TILES):
+                o_pass(o1[-1][n], n, 0, z1_first, slice(lo, hi), n % share == 0, False)
 
-        def finish_c(u, accs):
-            lo, hi = edges[u], edges[u + 1]
+        o2 = [held([P, M], F32, "o2_%d" % n) for n in range(N_TILES)]
+        for half in range(2):
+            for n in range(N_TILES):
+                cols = slice(M // 2 * half, M // 2 * (half + 1))
+                nc.scalar.copy(o2[n][:, cols], o2_banks[n][:, cols])
+
+        woven1 = {}
+
+        def second_pass(u):
+            lo, hi = spans[u]
+            share = BANK // (hi - lo)
+            z = quantize("z1_1%d" % u, woven1[u], hi - lo)
+            for n in range(N_TILES):
+                o_pass(o1[u][n], n, 1, z, slice(0, hi - lo), False, n % share == share - 1)
+
+        def finish(u):
+            lo, hi = spans[u]
             width = hi - lo
             for half in range(2):
-                diff = held([P, 2 * width], F32, "diff%d%d" % (u, half))
                 tilt = held([P, 2 * width], F32, "tilt%d%d" % (u, half))
                 for e in range(2):
                     n = 2 * half + e
-                    nc.vector.scalar_tensor_tensor(diff[:, width * e:width * (e + 1)], accs[n][:], rl_sb[:, n:n + 1],
-                                                   o2_sb[n][:, lo:hi], ALU.mult, ALU.subtract)
-                nc.scalar.activation(tilt[:], diff[:], ACT.Tanh)
+                    nc.vector.scalar_tensor_tensor(tilt[:, width * e:width * (e + 1)], o1[u][n], rl_sb[:, n:n + 1],
+                                                   o2[n][:, lo:hi], ALU.mult, ALU.subtract)
+                nc.scalar.activation(tilt[:], tilt[:], ACT.Tanh)
                 dst = out[2 * P * half:2 * P * (half + 1), lo:hi].rearrange("(e p) m -> p e m", p=P)
                 nc.sync.dma_start(dst, tilt[:].rearrange("p (e m) -> p e m", e=2))
 
-        AHEAD = 0
-        LAG = 1
-        wins = {}
-        for s in range(AHEAD):
-            wins[divmod(s, PACK)] = x_window(*divmod(s, PACK))
-        crude = {}
-        accs_of = {}
-        total = len(steps)
-        for s in range(total + LAG + 3):
-            if s + AHEAD < 2 * PACK:
-                wins[divmod(s + AHEAD, PACK)] = x_window(*divmod(s + AHEAD, PACK))
-            if s < total:
-                b, t, lo, hi, planes = steps[s]
-                crude[s] = pick1(wins[(b, t)], lo, hi)
-            if 0 <= s - LAG < total:
-                b, t, lo, hi, planes = steps[s - LAG]
-                pick2(wins[(b, t)], crude[s - LAG], planes, b, t, lo, hi)
-            do_extra("x%d" % s)
-            for u in range(len(PIECES)):
-                r = s - LAG - done_at[u]
-                if r == 0:
-                    finish_a(u)
-                if r == 1:
-                    accs_of[u] = finish_b(u)
-                if r == 2:
-                    finish_c(u, accs_of[u])
+        for s in range(len(PIECES) + 3):
+            if s < len(PIECES):
+                woven1[s] = weave_z1(1, *spans[s])
+            if 0 <= s - 1 < len(PIECES):
+                second_pass(s - 1)
+            if 0 <= s - 2 < len(PIECES):
+                finish(s - 2)

@@ -25,8 +25,8 @@ N_TILES = N // P
 STAGE_BANKS = 4
 WINDOWS = 8
 PIECES = [256, 128, 128]
-DIESEL_ON_SCALAR = (1, 3, 5, 7)
-CRUDE_ON_VECTOR = (2, 3)
+DIESEL_ON_SCALAR = ()
+CRUDE_ON_VECTOR = (3,)
 
 
 def tile_list_crack_hedge_tilt_kernel(tc, tab_words, tab_scales, offs, pos1, pos2, pos3, w1,
@@ -45,6 +45,9 @@ def tile_list_crack_hedge_tilt_kernel(tc, tab_words, tab_scales, offs, pos1, pos
 
         def window():
             return ring.tile([P, S], F32, name="window", tag="window", bufs=WINDOWS, align_bytes=64)
+
+        def rounded():
+            return keep.tile([P, PACK * PASS], BF16, name="rounded", tag="rounded", align_bytes=64)
 
         offs_sb = keep.tile([P, S // 16], U16, name="offs_sb")
         pos1_sb = keep.tile([P, M // 16], U16, name="pos1_sb")
@@ -133,9 +136,14 @@ def tile_list_crack_hedge_tilt_kernel(tc, tab_words, tab_scales, offs, pos1, pos
         w1_bf = {}
 
         def round_w1(b, a):
-            w1_bf[b, a] = ring.tile([P, PACK * PASS], BF16, name="w1_bf", tag="w1_bf", align_bytes=64)
-            nc.vector.tensor_copy(w1_bf[b, a][:].rearrange("p (t m j) -> p m j t", t=PACK, j=PACK),
-                                  w1_raw[b][a][:].rearrange("p (j m t) -> p m j t", t=PACK, j=PACK))
+            w1_bf[b, a] = rounded()
+            if (b, a) == (0, 0):
+                nc.vector.tensor_copy(w1_bf[b, a][:].rearrange("p (t m j) -> p m j t", t=PACK, j=PACK),
+                                      w1_raw[b][a][:].rearrange("p (j m t) -> p m j t", t=PACK, j=PACK))
+            else:
+                nc.gpsimd.tensor_scalar(w1_bf[b, a][:].rearrange("p (t m j) -> p m t j", t=PACK, j=PACK),
+                                        w1_raw[b][a][:].rearrange("p (j m t) -> p m t j", t=PACK, j=PACK),
+                                        1.0, 0.0, ALU.mult, ALU.add)
 
         def quantize_w1(b, a):
             nc.vector.quantize_mx(out=w1_w[b][a][:].bitcast(E4M3), scales=w1_s[b][a][:], in_=w1_bf[b, a][:])
@@ -189,8 +197,8 @@ def tile_list_crack_hedge_tilt_kernel(tc, tab_words, tab_scales, offs, pos1, pos
                     nc.scalar.copy(y_win[i][:, BANK * h:BANK * (h + 1)], acc[:])
             if i % 2 == 0:
                 round_w1(*divmod(i // 2 - 1, 2))
-                pick_diesel(i - 2, y_win[i - 2])
                 quantize_w1(*divmod(i // 2 - 1, 2))
+                pick_diesel(i - 2, y_win[i - 2])
                 pick_diesel(i - 1, y_win[i - 1])
 
         crude = [held([P, PACK * M], F32, "crude%d" % b) for b in range(2)]
@@ -226,7 +234,7 @@ def tile_list_crack_hedge_tilt_kernel(tc, tab_words, tab_scales, offs, pos1, pos
             return woven
 
         def weave_z2(b):
-            woven = held([P, PACK * M], BF16, "z2_woven%d" % b)
+            woven = rounded()
             nc.vector.tensor_copy(woven[:].rearrange("p (c i t) -> p c t i", t=PACK, i=4),
                                   z2_rows[b][:].rearrange("p (t c i) -> p c t i", t=PACK, i=4))
             return woven
@@ -239,11 +247,11 @@ def tile_list_crack_hedge_tilt_kernel(tc, tab_words, tab_scales, offs, pos1, pos
             x_win.append(x_window(i + 1))
             pick_crude(i, x_win[i], 0, M)
             pick_petrol(i, x_win[i], 0, M)
-            if i < 2:
-                woven2.append(weave_z2(i))
-            if 1 <= i < 3:
-                z2.append(quantize("z2_%d" % (i - 1), woven2[i - 1], M))
-            if i == 3:
+            if 3 <= i < 5:
+                z2.append(quantize("z2_%d" % (i - 3), woven2[i - 3], M))
+            if 2 <= i < 4:
+                woven2.append(weave_z2(i - 2))
+            if i == 4:
                 for n in range(N_TILES):
                     o2_banks.append(bank(STAGE_BANKS + n))
                     for a in range(2):

@@ -25,8 +25,10 @@ N_TILES = N // P
 STAGE_BANKS = 4
 WINDOWS = 8
 PIECES = [256, 128, 128]
-DIESEL_ON_SCALAR = ()
-CRUDE_ON_VECTOR = (3,)
+DIESEL_ON_SCALAR = (1, 3, 5, 7)
+CRUDE_ON_VECTOR = (1, 2, 3)
+WHOLE = 7
+W2_EDGES = [0, 2 * P, 4 * P, H]
 
 
 def tile_list_crack_hedge_tilt_kernel(tc, tab_words, tab_scales, offs, pos1, pos2, pos3, w1,
@@ -47,7 +49,7 @@ def tile_list_crack_hedge_tilt_kernel(tc, tab_words, tab_scales, offs, pos1, pos
             return ring.tile([P, S], F32, name="window", tag="window", bufs=WINDOWS, align_bytes=64)
 
         def rounded():
-            return keep.tile([P, PACK * PASS], BF16, name="rounded", tag="rounded", align_bytes=64)
+            return keep.tile([P, 2 * PACK * PASS], BF16, name="rounded", tag="rounded", align_bytes=64)
 
         offs_sb = keep.tile([P, S // 16], U16, name="offs_sb")
         pos1_sb = keep.tile([P, M // 16], U16, name="pos1_sb")
@@ -58,11 +60,10 @@ def tile_list_crack_hedge_tilt_kernel(tc, tab_words, tab_scales, offs, pos1, pos
         v_w = [held([P, S], I32, "v_w%d" % a) for a in range(2)]
         v_s = held([P, S], U8, "v_s")
         v_s1 = held([P, S], U8, "v_s1")
-        w2_w = [held([P, 2 * 2 * PASS], U8, "w2_w%d" % b) for b in range(2)]
+        w2_cols = list(zip(W2_EDGES, W2_EDGES[1:]))
+        w2_w = [held([P, 2 * 2 * (hi - lo)], U8, "w2_w%d" % lo) for lo, hi in w2_cols]
         w2_s = held([P, 2 * H], U8, "w2_s")
         w1_raw = [[held([P, PACK * PASS], F32, "w1_raw%d%d" % (b, a)) for a in range(2)] for b in range(2)]
-        w1_w = [[held([P, PASS], U32, "w1_w%d%d" % (b, a)) for a in range(2)] for b in range(2)]
-        w1_s = [[held([P, PASS], U8, "w1_s%d%d" % (b, a)) for a in range(2)] for b in range(2)]
         w3_w = held([P, 2 * N], I32, "w3_w")
         w3_s = held([P, N], U8, "w3_s")
         cg_sb = held([P, TILES], F32, "cg_sb")
@@ -82,9 +83,10 @@ def tile_list_crack_hedge_tilt_kernel(tc, tab_words, tab_scales, offs, pos1, pos
             src = w1[PASS * a:PASS * (a + 1), PASS * b:PASS * (b + 1)].rearrange("(p j) c -> p j c", j=PACK)
             nc.sync.dma_start(w1_raw[b][a][:].rearrange("p (j c) -> p j c", j=PACK), src)
 
-        def load_w2(b):
-            nc.sync.dma_start(w2_w[b][:].bitcast(I32).rearrange("p (a c) -> p a c", a=2),
-                              w2_words[:, :, 2 * PASS * b:2 * PASS * (b + 1)].bitcast(I32).rearrange("a p c -> p a c"))
+        def load_w2(g):
+            lo, hi = w2_cols[g]
+            nc.sync.dma_start(w2_w[g][:].bitcast(I32).rearrange("p (a c) -> p a c", a=2),
+                              w2_words[:, :, 2 * lo:2 * hi].bitcast(I32).rearrange("a p c -> p a c"))
 
         nc.sync.dma_start(offs_sb[:], offs)
         load_w2(0)
@@ -97,14 +99,15 @@ def tile_list_crack_hedge_tilt_kernel(tc, tab_words, tab_scales, offs, pos1, pos
         load_words(1)
         nc.vector.tensor_copy(v_s[:], tab_s[:].indirect(offs_sb[:]))
         nc.sync.dma_start(v_s1[0:100, :].bitcast(I32), v_s[4:104, :].bitcast(I32))
+        load_w2(1)
         load_w1(0, 0)
         nc.sync.dma_start(pos3_sb[:], pos3)
+        load_w2(2)
         load_w1(0, 1)
-        load_w2(1)
-        load_w1(1, 0)
         nc.sync.dma_start(cg_sb[:].rearrange("p (b t) -> p b t", b=2), cg.rearrange("(b p t) -> p b t", b=2, t=PACK))
         nc.sync.dma_start(pos1_sb[:], pos1)
         nc.sync.dma_start(pos2_sb[:], pos2)
+        load_w1(1, 0)
         load_w1(1, 1)
         nc.sync.dma_start(w3_w[:].rearrange("p (a c) -> p a c", a=2),
                           w3_words.rearrange("a p c i -> p a (c i)").bitcast(I32))
@@ -113,8 +116,8 @@ def tile_list_crack_hedge_tilt_kernel(tc, tab_words, tab_scales, offs, pos1, pos
         with nc.allow_non_contiguous_dma(reason="one ratio for each partition"):
             nc.sync.dma_start(rl_sb[:], rl.rearrange("(n p) -> p n", p=P))
 
-        nc.gpsimd.tensor_scalar(cg_ge[:], cg_sb[:], 0.0, 2.0, ALU.is_ge, ALU.mult)
-        nc.gpsimd.tensor_scalar(cg_sign[:], cg_ge[:], -1.0, 1.0, ALU.add, ALU.mult)
+        nc.vector.tensor_scalar(cg_ge[:], cg_sb[:], 0.0, 2.0, ALU.is_ge, ALU.mult)
+        nc.vector.tensor_scalar(cg_sign[:], cg_ge[:], -1.0, 1.0, ALU.add, ALU.mult)
 
         for a in range(2):
             for h in range(2):
@@ -127,41 +130,36 @@ def tile_list_crack_hedge_tilt_kernel(tc, tab_words, tab_scales, offs, pos1, pos
             else:
                 nc.vector.tensor_copy(dst, win[:].indirect(places))
 
-        def quantize(name, woven, width):
+        def quantize(name, woven):
+            width = woven.shape[1] // PACK
             codes = held([P, width], U32, name + "_w")
             plane = held([P, width], U8, name + "_s")
-            nc.vector.quantize_mx(out=codes[:].bitcast(E4M3), scales=plane[:], in_=woven[:])
+            nc.vector.quantize_mx(out=codes[:].bitcast(E4M3), scales=plane[:], in_=woven)
             return codes, plane
 
-        w1_bf = {}
-
-        def round_w1(b, a):
-            w1_bf[b, a] = rounded()
-            if (b, a) == (0, 0):
-                nc.vector.tensor_copy(w1_bf[b, a][:].rearrange("p (t m j) -> p m j t", t=PACK, j=PACK),
+        def round_w1(b):
+            both = rounded()
+            for a in range(2):
+                dst = both[:, PACK * PASS * a:PACK * PASS * (a + 1)]
+                nc.vector.tensor_copy(dst.rearrange("p (t m j) -> p m j t", t=PACK, j=PACK),
                                       w1_raw[b][a][:].rearrange("p (j m t) -> p m j t", t=PACK, j=PACK))
-            else:
-                nc.gpsimd.tensor_scalar(w1_bf[b, a][:].rearrange("p (t m j) -> p m t j", t=PACK, j=PACK),
-                                        w1_raw[b][a][:].rearrange("p (j m t) -> p m t j", t=PACK, j=PACK),
-                                        1.0, 0.0, ALU.mult, ALU.add)
-
-        def quantize_w1(b, a):
-            nc.vector.quantize_mx(out=w1_w[b][a][:].bitcast(E4M3), scales=w1_s[b][a][:], in_=w1_bf[b, a][:])
+            return both
 
         def y_pass(acc, i, h, a):
-            b, t = divmod(i, PACK)
+            g = sum(1 for edge in W2_EDGES[1:] if edge <= P * i)
+            lo, hi = w2_cols[g]
             cols = slice(BANK * h, BANK * (h + 1))
-            c0 = PASS * a + P * t
+            c0 = (hi - lo) * a + P * i - lo
             s0 = H * a + P * i
             plane = v_s if a == 0 else v_s1
-            nc.tensor.matmul_mx(out=acc[:], lhsT=w2_w[b][:, 2 * c0:2 * (c0 + P)].bitcast(E2M1), lhsT_scale=w2_s[:, s0:s0 + P],
+            nc.tensor.matmul_mx(out=acc[:], lhsT=w2_w[g][:, 2 * c0:2 * (c0 + P)].bitcast(E2M1), lhsT_scale=w2_s[:, s0:s0 + P],
                                 rhs=v_w[a][:, cols].bitcast(E4M3), rhs_scale=plane[:, cols], start=(a == 0), stop=(a == 1))
 
         def x_pass(acc, i, h, a):
             b, t = divmod(i, PACK)
             cols = slice(BANK * h, BANK * (h + 1))
-            wc = slice(P * t, P * (t + 1))
-            nc.tensor.matmul_mx(out=acc[:], lhsT=w1_w[b][a][:, wc].bitcast(E4M3), lhsT_scale=w1_s[b][a][:, wc],
+            wc = slice(PASS * a + P * t, PASS * a + P * (t + 1))
+            nc.tensor.matmul_mx(out=acc[:], lhsT=w1_q[b][0][:, wc].bitcast(E4M3), lhsT_scale=w1_q[b][1][:, wc],
                                 rhs=v_w[a][:, cols].bitcast(E4M3), rhs_scale=v_s[4 * a:, cols], start=(a == 0), stop=(a == 1))
 
         def o_pass(acc, n, a, z, cols, start, stop):
@@ -178,6 +176,7 @@ def tile_list_crack_hedge_tilt_kernel(tc, tab_words, tab_scales, offs, pos1, pos
             nc.sync.dma_start(z2_rows[b][32 * t:32 * (t + 1), :].bitcast(I32).rearrange("p (j c) -> p j c", j=PACK),
                               picked[:].bitcast(I32))
 
+        w1_q = []
         first = [[bank(2 * i + h) for h in range(2)] for i in range(2)]
         y_win = [window() for i in range(2)]
         for h in range(2):
@@ -195,14 +194,14 @@ def tile_list_crack_hedge_tilt_kernel(tc, tab_words, tab_scales, offs, pos1, pos
                     for a in range(2):
                         y_pass(acc, i, h, a)
                     nc.scalar.copy(y_win[i][:, BANK * h:BANK * (h + 1)], acc[:])
+            if i % PACK == 2:
+                w1_q.append(quantize("w1_%d" % (i // PACK), round_w1(i // PACK)[:]))
             if i % 2 == 0:
-                round_w1(*divmod(i // 2 - 1, 2))
-                quantize_w1(*divmod(i // 2 - 1, 2))
                 pick_diesel(i - 2, y_win[i - 2])
                 pick_diesel(i - 1, y_win[i - 1])
 
         crude = [held([P, PACK * M], F32, "crude%d" % b) for b in range(2)]
-        petrol = [held([P, PACK * M], F32, "petrol%d" % b) for b in range(2)]
+        petrol = [held([P, PACK * M], F32, "petrol0")]
 
         def x_window(i):
             win = window()
@@ -226,52 +225,40 @@ def tile_list_crack_hedge_tilt_kernel(tc, tab_words, tab_scales, offs, pos1, pos
             values = crude[b][:, M * t + lo:M * t + hi]
             nc.scalar.activation(values, values, ACT.Abs, scale=cg_sb[:, i:i + 1])
 
-        def weave_z1(b, lo, hi):
-            woven = held([P, PACK * (hi - lo)], BF16, "z1_woven%d_%d" % (b, lo))
+        def weave_z1(engine, woven, b, lo, hi):
             def walk(planes):
                 return planes[:].rearrange("p (t m) -> p t m", t=PACK)[:, :, lo:hi].rearrange("p t (c i) -> p c t i", i=2)
-            nc.vector.tensor_tensor(woven[:].rearrange("p (c i t) -> p c t i", t=PACK, i=2), walk(crude[b]), walk(petrol[b]), ALU.mult)
+            engine.tensor_tensor(woven.rearrange("p (c i t) -> p c t i", t=PACK, i=2), walk(crude[b]), walk(petrol[b]), ALU.mult)
             return woven
 
-        def weave_z2(b):
-            woven = rounded()
-            nc.vector.tensor_copy(woven[:].rearrange("p (c i t) -> p c t i", t=PACK, i=4),
-                                  z2_rows[b][:].rearrange("p (t c i) -> p c t i", t=PACK, i=4))
-            return woven
+        def weave_z2():
+            both = rounded()
+            for b in range(2):
+                nc.gpsimd.tensor_scalar(both[:, PACK * M * b:PACK * M * (b + 1)].rearrange("p (m t) -> p m t", t=PACK),
+                                        z2_rows[b][:].rearrange("p (t m) -> p m t", t=PACK), 1.0, 0.0, ALU.mult, ALU.add)
+            return both
 
-        woven2 = []
-        z2 = []
         o2_banks = []
         x_win = [x_window(0)]
-        for i in range(TILES - 1):
+        for i in range(WHOLE):
             x_win.append(x_window(i + 1))
-            pick_crude(i, x_win[i], 0, M)
-            pick_petrol(i, x_win[i], 0, M)
-            if 3 <= i < 5:
-                z2.append(quantize("z2_%d" % (i - 3), woven2[i - 3], M))
-            if 2 <= i < 4:
-                woven2.append(weave_z2(i - 2))
-            if i == 4:
+            if i == 3:
+                z2 = quantize("z2", weave_z2()[:])
                 for n in range(N_TILES):
                     o2_banks.append(bank(STAGE_BANKS + n))
                     for a in range(2):
-                        o_pass(o2_banks[n][:], n, a, z2[a], slice(0, M), a == 0, a == 1)
+                        o_pass(o2_banks[n][:], n, a, z2, slice(M * a, M * (a + 1)), a == 0, a == 1)
+                petrol.append(keep.tile([P, PACK * M], F32, name="petrol1", tag="rounded", align_bytes=64))
+            if i == PACK + 1:
+                z1_first = quantize("z1_0", weave_z1(nc.vector, held([P, PACK * M], BF16, "z1_woven")[:], 0, 0, M))
+            pick_crude(i, x_win[i], 0, M)
+            pick_petrol(i, x_win[i], 0, M)
             if i >= 1:
                 size_of_crude(i - 1, 0, M)
-            if i == PACK:
-                z1_first_woven = weave_z1(0, 0, M)
-            if i == PACK + 1:
-                z1_first = quantize("z1_0", z1_first_woven, M)
 
-        last = TILES - 1
+        size_of_crude(WHOLE - 1, 0, M)
         edges = [sum(PIECES[:u]) for u in range(len(PIECES) + 1)]
         spans = [(edges[u], edges[u + 1]) for u in range(len(PIECES))]
-        size_of_crude(last - 1, 0, M)
-        for lo, hi in spans:
-            pick_crude(last, x_win[last], lo, hi)
-            pick_petrol(last, x_win[last], lo, hi)
-        for lo, hi in spans:
-            size_of_crude(last, lo, hi)
 
         o1 = []
         free_banks = list(range(STAGE_BANKS))
@@ -284,17 +271,24 @@ def tile_list_crack_hedge_tilt_kernel(tc, tab_words, tab_scales, offs, pos1, pos
                 o_pass(o1[-1][n], n, 0, z1_first, slice(lo, hi), n % share == 0, False)
 
         o2 = [held([P, M], F32, "o2_%d" % n) for n in range(N_TILES)]
-        for half in range(2):
-            for n in range(N_TILES):
-                cols = slice(M // 2 * half, M // 2 * (half + 1))
-                nc.scalar.copy(o2[n][:, cols], o2_banks[n][:, cols])
 
-        woven1 = {}
+        def picks(u):
+            lo, hi = spans[u]
+            for i in range(WHOLE, TILES):
+                pick_crude(i, x_win[i], lo, hi)
+                pick_petrol(i, x_win[i], lo, hi)
+            for i in range(WHOLE, TILES):
+                size_of_crude(i, lo, hi)
+
+        def empty_o2(half):
+            cols = slice(M // 2 * half, M // 2 * (half + 1))
+            for n in range(N_TILES):
+                nc.scalar.copy(o2[n][:, cols], o2_banks[n][:, cols])
 
         def second_pass(u):
             lo, hi = spans[u]
             share = BANK // (hi - lo)
-            z = quantize("z1_1%d" % u, woven1[u], hi - lo)
+            z = quantize("z1_1%d" % u, woven1[u])
             for n in range(N_TILES):
                 o_pass(o1[u][n], n, 1, z, slice(0, hi - lo), False, n % share == share - 1)
 
@@ -311,9 +305,14 @@ def tile_list_crack_hedge_tilt_kernel(tc, tab_words, tab_scales, offs, pos1, pos
                 dst = out[2 * P * half:2 * P * (half + 1), lo:hi].rearrange("(e p) m -> p e m", p=P)
                 nc.sync.dma_start(dst, tilt[:].rearrange("p (e m) -> p e m", e=2))
 
-        for s in range(len(PIECES) + 3):
+        for u in range(len(PIECES)):
+            picks(u)
+        for half in range(2):
+            empty_o2(half)
+        woven1 = []
+        for s in range(len(PIECES) + 2):
             if s < len(PIECES):
-                woven1[s] = weave_z1(1, *spans[s])
+                woven1.append(weave_z1(nc.vector, held([P, PACK * PIECES[s]], BF16, "z1_woven%d" % s)[:], 1, *spans[s]))
             if 0 <= s - 1 < len(PIECES):
                 second_pass(s - 1)
             if 0 <= s - 2 < len(PIECES):

@@ -25,8 +25,9 @@ N_TILES = N // P
 STAGE_BANKS = 4
 WINDOWS = 8
 PIECES = [256, 128, 128]
-DIESEL_ON_SCALAR = (1, 3, 5, 7)
+DIESEL_ON_SCALAR = (1, 3, 5)
 CRUDE_ON_VECTOR = (1, 2, 3)
+PETROL_ON_SCALAR = (7,)
 WHOLE = 7
 W2_EDGES = [0, 2 * P, 4 * P, H]
 
@@ -58,8 +59,8 @@ def tile_list_crack_hedge_tilt_kernel(tc, tab_words, tab_scales, offs, pos1, pos
         tab_w = [held([P, T], I32, "tab_w%d" % a) for a in range(2)]
         tab_s = held([P, T], U8, "tab_s")
         v_w = [held([P, S], I32, "v_w%d" % a) for a in range(2)]
-        v_s = held([P, S], U8, "v_s")
-        v_s1 = held([P, S], U8, "v_s1")
+        picked_s = held([P, S], U8, "picked_s")
+        v_s = held([P, 2 * S], U8, "v_s")
         w2_cols = list(zip(W2_EDGES, W2_EDGES[1:]))
         w2_w = [held([P, 2 * 2 * (hi - lo)], U8, "w2_w%d" % lo) for lo, hi in w2_cols]
         w2_s = held([P, 2 * H], U8, "w2_s")
@@ -71,9 +72,10 @@ def tile_list_crack_hedge_tilt_kernel(tc, tab_words, tab_scales, offs, pos1, pos
         cg_sign = held([P, TILES], F32, "cg_sign")
         rl_sb = held([P, N_TILES], F32, "rl_sb")
 
-        nc.vector.memset(tab_s[:].bitcast(I32), 0)
         nc.vector.memset(w2_s[:].bitcast(I32), 0)
-        nc.vector.memset(v_s1[:].bitcast(I32), 0)
+        nc.vector.memset(tab_s[32:64, :].bitcast(I32), 0)
+        nc.vector.memset(tab_s[64:128, :].bitcast(I32), 0)
+        nc.vector.memset(v_s[:].bitcast(I32), 0)
         nc.vector.memset(w3_s[:].bitcast(I32), 0)
 
         def load_words(a):
@@ -83,38 +85,33 @@ def tile_list_crack_hedge_tilt_kernel(tc, tab_words, tab_scales, offs, pos1, pos
             src = w1[PASS * a:PASS * (a + 1), PASS * b:PASS * (b + 1)].rearrange("(p j) c -> p j c", j=PACK)
             nc.sync.dma_start(w1_raw[b][a][:].rearrange("p (j c) -> p j c", j=PACK), src)
 
-        def load_w2(g):
+        def load_w2(queue, g):
             lo, hi = w2_cols[g]
-            nc.sync.dma_start(w2_w[g][:].bitcast(I32).rearrange("p (a c) -> p a c", a=2),
+            queue.dma_start(w2_w[g][:].bitcast(I32).rearrange("p (a c) -> p a c", a=2),
                               w2_words[:, :, 2 * lo:2 * hi].bitcast(I32).rearrange("a p c -> p a c"))
 
         nc.sync.dma_start(offs_sb[:], offs)
-        load_w2(0)
-        for q in range(4):
-            nc.sync.dma_start(tab_s[32 * q:32 * q + 8, :].bitcast(I32), tab_scales[:, 4 * q:4 * q + 4, :].bitcast(I32))
+        nc.sync.dma_start(tab_s[0:32, :].bitcast(I32), tab_scales.bitcast(I32).rearrange("a s c -> s a c"))
         load_words(0)
+        load_w2(nc.scalar, 0)
         for q in range(4):
-            nc.sync.dma_start(w2_s[32 * q:32 * q + 4, :].bitcast(I32).rearrange("p (a c) -> p a c", a=2),
+            nc.scalar.dma_start(w2_s[32 * q:32 * q + 4, :].bitcast(I32).rearrange("p (a c) -> p a c", a=2),
                               w2_scales[:, 4 * q:4 * q + 4, :].bitcast(I32).rearrange("a r c -> r a c"))
         load_words(1)
-        nc.vector.tensor_copy(v_s[:], tab_s[:].indirect(offs_sb[:]))
-        nc.sync.dma_start(v_s1[0:100, :].bitcast(I32), v_s[4:104, :].bitcast(I32))
-        load_w2(1)
+        nc.vector.tensor_copy(picked_s[:], tab_s[:].indirect(offs_sb[:]))
+        for q in range(4):
+            nc.sync.dma_start(v_s[32 * q:32 * q + 4, :].bitcast(I32).rearrange("p (a c) -> p a c", a=2),
+                              picked_s[8 * q:8 * q + 8, :].bitcast(I32))
+        load_w2(nc.sync, 1)
         load_w1(0, 0)
         nc.sync.dma_start(pos3_sb[:], pos3)
-        load_w2(2)
+        load_w2(nc.sync, 2)
         load_w1(0, 1)
         nc.sync.dma_start(cg_sb[:].rearrange("p (b t) -> p b t", b=2), cg.rearrange("(b p t) -> p b t", b=2, t=PACK))
         nc.sync.dma_start(pos1_sb[:], pos1)
         nc.sync.dma_start(pos2_sb[:], pos2)
         load_w1(1, 0)
         load_w1(1, 1)
-        nc.sync.dma_start(w3_w[:].rearrange("p (a c) -> p a c", a=2),
-                          w3_words.rearrange("a p c i -> p a (c i)").bitcast(I32))
-        for q in range(4):
-            nc.sync.dma_start(w3_s[32 * q:32 * q + 8, :].bitcast(I32), w3_scales[:, 4 * q:4 * q + 4, :].bitcast(I32))
-        with nc.allow_non_contiguous_dma(reason="one ratio for each partition"):
-            nc.sync.dma_start(rl_sb[:], rl.rearrange("(n p) -> p n", p=P))
 
         nc.vector.tensor_scalar(cg_ge[:], cg_sb[:], 0.0, 2.0, ALU.is_ge, ALU.mult)
         nc.vector.tensor_scalar(cg_sign[:], cg_ge[:], -1.0, 1.0, ALU.add, ALU.mult)
@@ -151,16 +148,15 @@ def tile_list_crack_hedge_tilt_kernel(tc, tab_words, tab_scales, offs, pos1, pos
             cols = slice(BANK * h, BANK * (h + 1))
             c0 = (hi - lo) * a + P * i - lo
             s0 = H * a + P * i
-            plane = v_s if a == 0 else v_s1
             nc.tensor.matmul_mx(out=acc[:], lhsT=w2_w[g][:, 2 * c0:2 * (c0 + P)].bitcast(E2M1), lhsT_scale=w2_s[:, s0:s0 + P],
-                                rhs=v_w[a][:, cols].bitcast(E4M3), rhs_scale=plane[:, cols], start=(a == 0), stop=(a == 1))
+                                rhs=v_w[a][:, cols].bitcast(E4M3), rhs_scale=v_s[:, S * a + BANK * h:S * a + BANK * (h + 1)], start=(a == 0), stop=(a == 1))
 
         def x_pass(acc, i, h, a):
             b, t = divmod(i, PACK)
             cols = slice(BANK * h, BANK * (h + 1))
             wc = slice(PASS * a + P * t, PASS * a + P * (t + 1))
             nc.tensor.matmul_mx(out=acc[:], lhsT=w1_q[b][0][:, wc].bitcast(E4M3), lhsT_scale=w1_q[b][1][:, wc],
-                                rhs=v_w[a][:, cols].bitcast(E4M3), rhs_scale=v_s[4 * a:, cols], start=(a == 0), stop=(a == 1))
+                                rhs=v_w[a][:, cols].bitcast(E4M3), rhs_scale=v_s[:, S * a + BANK * h:S * a + BANK * (h + 1)], start=(a == 0), stop=(a == 1))
 
         def o_pass(acc, n, a, z, cols, start, stop):
             c0 = N * a + P * n
@@ -182,7 +178,6 @@ def tile_list_crack_hedge_tilt_kernel(tc, tab_words, tab_scales, offs, pos1, pos
         for h in range(2):
             for i in range(2):
                 y_pass(first[i][h], i, h, 0)
-        for h in range(2):
             for i in range(2):
                 y_pass(first[i][h], i, h, 1)
                 nc.scalar.copy(y_win[i][:, BANK * h:BANK * (h + 1)], first[i][h][:])
@@ -199,6 +194,13 @@ def tile_list_crack_hedge_tilt_kernel(tc, tab_words, tab_scales, offs, pos1, pos
             if i % 2 == 0:
                 pick_diesel(i - 2, y_win[i - 2])
                 pick_diesel(i - 1, y_win[i - 1])
+
+        nc.sync.dma_start(w3_w[:].rearrange("p (a c) -> p a c", a=2),
+                          w3_words.rearrange("a p c i -> p a (c i)").bitcast(I32))
+        for q in range(4):
+            nc.sync.dma_start(w3_s[32 * q:32 * q + 8, :].bitcast(I32), w3_scales[:, 4 * q:4 * q + 4, :].bitcast(I32))
+        with nc.allow_non_contiguous_dma(reason="one ratio for each partition"):
+            nc.sync.dma_start(rl_sb[:], rl.rearrange("(n p) -> p n", p=P))
 
         crude = [held([P, PACK * M], F32, "crude%d" % b) for b in range(2)]
         petrol = [held([P, PACK * M], F32, "petrol0")]
@@ -218,7 +220,7 @@ def tile_list_crack_hedge_tilt_kernel(tc, tab_words, tab_scales, offs, pos1, pos
 
         def pick_petrol(i, win, lo, hi):
             b, t = divmod(i, PACK)
-            pick(False, petrol[b][:, M * t + lo:M * t + hi], win, pos2_sb[:, lo // 16:hi // 16])
+            pick(i in PETROL_ON_SCALAR, petrol[b][:, M * t + lo:M * t + hi], win, pos2_sb[:, lo // 16:hi // 16])
 
         def size_of_crude(i, lo, hi):
             b, t = divmod(i, PACK)

@@ -25,9 +25,10 @@ N_TILES = N // P
 STAGE_BANKS = 4
 WINDOWS = 8
 PIECES = [256, 128, 128]
-DIESEL_ON_SCALAR = (1, 3, 5)
-CRUDE_ON_VECTOR = (1, 2, 3)
+DIESEL_ON_SCALAR = (1,)
+CRUDE_ON_VECTOR = (2, 3, 4)
 PETROL_ON_SCALAR = (7,)
+SHARED = 37 * 1024
 WHOLE = 7
 W2_EDGES = [0, 2 * P, 4 * P, H]
 
@@ -38,6 +39,7 @@ def tile_list_crack_hedge_tilt_kernel(tc, tab_words, tab_scales, offs, pos1, pos
     with ExitStack() as ctx:
         keep = ctx.enter_context(tc.tile_pool(name="keep", bufs=1))
         ring = ctx.enter_context(tc.tile_pool(name="ring", bufs=2))
+        shared = ctx.enter_context(tc.tile_pool(name="shared", bufs=1))
         psum = ctx.enter_context(tc.psum_pool(name="psum", bufs=1))
 
         def held(shape, dtype, name):
@@ -49,8 +51,8 @@ def tile_list_crack_hedge_tilt_kernel(tc, tab_words, tab_scales, offs, pos1, pos
         def window():
             return ring.tile([P, S], F32, name="window", tag="window", bufs=WINDOWS, align_bytes=64)
 
-        def rounded():
-            return keep.tile([P, 2 * PACK * PASS], BF16, name="rounded", tag="rounded", align_bytes=64)
+        def placed(shape, dtype, name, offset):
+            return shared.tile(shape, dtype, name=name, align_bytes=64, offset=offset)
 
         offs_sb = keep.tile([P, S // 16], U16, name="offs_sb")
         pos1_sb = keep.tile([P, M // 16], U16, name="pos1_sb")
@@ -103,18 +105,18 @@ def tile_list_crack_hedge_tilt_kernel(tc, tab_words, tab_scales, offs, pos1, pos
             nc.sync.dma_start(v_s[32 * q:32 * q + 4, :].bitcast(I32).rearrange("p (a c) -> p a c", a=2),
                               picked_s[8 * q:8 * q + 8, :].bitcast(I32))
         load_w2(nc.sync, 1)
+        nc.sync.dma_start(cg_sb[:].rearrange("p (b t) -> p b t", b=2), cg.rearrange("(b p t) -> p b t", b=2, t=PACK))
         load_w1(0, 0)
         nc.sync.dma_start(pos3_sb[:], pos3)
         load_w2(nc.sync, 2)
         load_w1(0, 1)
-        nc.sync.dma_start(cg_sb[:].rearrange("p (b t) -> p b t", b=2), cg.rearrange("(b p t) -> p b t", b=2, t=PACK))
         nc.sync.dma_start(pos1_sb[:], pos1)
         nc.sync.dma_start(pos2_sb[:], pos2)
         load_w1(1, 0)
         load_w1(1, 1)
 
-        nc.vector.tensor_scalar(cg_ge[:], cg_sb[:], 0.0, 2.0, ALU.is_ge, ALU.mult)
-        nc.vector.tensor_scalar(cg_sign[:], cg_ge[:], -1.0, 1.0, ALU.add, ALU.mult)
+        nc.gpsimd.tensor_scalar(cg_ge[:], cg_sb[:], 0.0, 2.0, ALU.is_ge, ALU.mult)
+        nc.gpsimd.tensor_scalar(cg_sign[:], cg_ge[:], -1.0, 1.0, ALU.add, ALU.mult)
 
         for a in range(2):
             for h in range(2):
@@ -135,11 +137,16 @@ def tile_list_crack_hedge_tilt_kernel(tc, tab_words, tab_scales, offs, pos1, pos
             return codes, plane
 
         def round_w1(b):
-            both = rounded()
+            both = placed([P, (SHARED + 5 * 1024 * (1 - b)) // 2], BF16, "w1_rounded%d" % b, 0)[:, 0:2 * PACK * PASS]
             for a in range(2):
                 dst = both[:, PACK * PASS * a:PACK * PASS * (a + 1)]
-                nc.vector.tensor_copy(dst.rearrange("p (t m j) -> p m j t", t=PACK, j=PACK),
-                                      w1_raw[b][a][:].rearrange("p (j m t) -> p m j t", t=PACK, j=PACK))
+                if b == 0:
+                    nc.vector.tensor_copy(dst.rearrange("p (t m j) -> p m j t", t=PACK, j=PACK),
+                                          w1_raw[b][a][:].rearrange("p (j m t) -> p m j t", t=PACK, j=PACK))
+                else:
+                    nc.gpsimd.tensor_scalar(dst.rearrange("p (t m j) -> p m t j", t=PACK, j=PACK),
+                                            w1_raw[b][a][:].rearrange("p (j m t) -> p m t j", t=PACK, j=PACK),
+                                            1.0, 0.0, ALU.mult, ALU.add)
             return both
 
         def y_pass(acc, i, h, a):
@@ -167,7 +174,10 @@ def tile_list_crack_hedge_tilt_kernel(tc, tab_words, tab_scales, offs, pos1, pos
 
         def pick_diesel(i, win):
             b, t = divmod(i, PACK)
-            picked = held([P, M], BF16, "diesel%d" % i)
+            if i < 2:
+                picked = held([P, M], BF16, "diesel%d" % i)
+            else:
+                picked = placed([P, M], BF16, "diesel%d" % i, SHARED + 1024 * (TILES - 2 - i))
             pick(i in DIESEL_ON_SCALAR, picked[:], win, pos3_sb[:])
             nc.sync.dma_start(z2_rows[b][32 * t:32 * (t + 1), :].bitcast(I32).rearrange("p (j c) -> p j c", j=PACK),
                               picked[:].bitcast(I32))
@@ -190,7 +200,7 @@ def tile_list_crack_hedge_tilt_kernel(tc, tab_words, tab_scales, offs, pos1, pos
                         y_pass(acc, i, h, a)
                     nc.scalar.copy(y_win[i][:, BANK * h:BANK * (h + 1)], acc[:])
             if i % PACK == 2:
-                w1_q.append(quantize("w1_%d" % (i // PACK), round_w1(i // PACK)[:]))
+                w1_q.append(quantize("w1_%d" % (i // PACK), round_w1(i // PACK)))
             if i % 2 == 0:
                 pick_diesel(i - 2, y_win[i - 2])
                 pick_diesel(i - 1, y_win[i - 1])
@@ -202,8 +212,8 @@ def tile_list_crack_hedge_tilt_kernel(tc, tab_words, tab_scales, offs, pos1, pos
         with nc.allow_non_contiguous_dma(reason="one ratio for each partition"):
             nc.sync.dma_start(rl_sb[:], rl.rearrange("(n p) -> p n", p=P))
 
-        crude = [held([P, PACK * M], F32, "crude%d" % b) for b in range(2)]
-        petrol = [held([P, PACK * M], F32, "petrol0")]
+        crude = [placed([P, PACK * M], F32, "crude0", 20480)]
+        petrol = [placed([P, PACK * M], F32, "petrol0", 28672)]
 
         def x_window(i):
             win = window()
@@ -234,7 +244,7 @@ def tile_list_crack_hedge_tilt_kernel(tc, tab_words, tab_scales, offs, pos1, pos
             return woven
 
         def weave_z2():
-            both = rounded()
+            both = placed([P, 2 * PACK * M], BF16, "z2_woven", 6144)
             for b in range(2):
                 nc.gpsimd.tensor_scalar(both[:, PACK * M * b:PACK * M * (b + 1)].rearrange("p (m t) -> p m t", t=PACK),
                                         z2_rows[b][:].rearrange("p (t m) -> p m t", t=PACK), 1.0, 0.0, ALU.mult, ALU.add)
@@ -250,9 +260,10 @@ def tile_list_crack_hedge_tilt_kernel(tc, tab_words, tab_scales, offs, pos1, pos
                     o2_banks.append(bank(STAGE_BANKS + n))
                     for a in range(2):
                         o_pass(o2_banks[n][:], n, a, z2, slice(M * a, M * (a + 1)), a == 0, a == 1)
-                petrol.append(keep.tile([P, PACK * M], F32, name="petrol1", tag="rounded", align_bytes=64))
+                petrol.append(placed([P, PACK * M], F32, "petrol1", 0))
+                crude.append(placed([P, PACK * M], F32, "crude1", 12288))
             if i == PACK + 1:
-                z1_first = quantize("z1_0", weave_z1(nc.vector, held([P, PACK * M], BF16, "z1_woven")[:], 0, 0, M))
+                z1_first = quantize("z1_0", weave_z1(nc.gpsimd, placed([P, PACK * M], BF16, "z1_woven", 8192)[:], 0, 0, M))
             pick_crude(i, x_win[i], 0, M)
             pick_petrol(i, x_win[i], 0, M)
             if i >= 1:

@@ -26,9 +26,10 @@ STAGE_BANKS = 4
 WINDOWS = 8
 PIECES = [256, 128, 128]
 DIESEL_ON_SCALAR = (1,)
-CRUDE_ON_VECTOR = (2, 3, 4)
-PETROL_ON_SCALAR = (7,)
-SHARED = 37 * 1024
+CRUDE_ON_VECTOR = (3, 4, 5)
+PETROL_SPLIT = 256
+SHARED = 36 * 1024
+EARLY_DIESEL = 2
 WHOLE = 7
 W2_EDGES = [0, 2 * P, 4 * P, H]
 
@@ -129,15 +130,18 @@ def tile_list_crack_hedge_tilt_kernel(tc, tab_words, tab_scales, offs, pos1, pos
             else:
                 nc.vector.tensor_copy(dst, win[:].indirect(places))
 
-        def quantize(name, woven):
+        def quantize(name, woven, parts=1):
             width = woven.shape[1] // PACK
             codes = held([P, width], U32, name + "_w")
             plane = held([P, width], U8, name + "_s")
-            nc.vector.quantize_mx(out=codes[:].bitcast(E4M3), scales=plane[:], in_=woven)
+            step = width // parts
+            for c0 in range(0, width, step):
+                nc.vector.quantize_mx(out=codes[:, c0:c0 + step].bitcast(E4M3), scales=plane[:, c0:c0 + step],
+                                      in_=woven[:, PACK * c0:PACK * (c0 + step)])
             return codes, plane
 
         def round_w1(b):
-            both = placed([P, (SHARED + 5 * 1024 * (1 - b)) // 2], BF16, "w1_rounded%d" % b, 0)[:, 0:2 * PACK * PASS]
+            both = placed([P, (SHARED + 6 * 1024 * (1 - b)) // 2], BF16, "w1_rounded%d" % b, 0)[:, 0:2 * PACK * PASS]
             for a in range(2):
                 dst = both[:, PACK * PASS * a:PACK * PASS * (a + 1)]
                 if b == 0:
@@ -174,10 +178,10 @@ def tile_list_crack_hedge_tilt_kernel(tc, tab_words, tab_scales, offs, pos1, pos
 
         def pick_diesel(i, win):
             b, t = divmod(i, PACK)
-            if i < 2:
+            if i < EARLY_DIESEL:
                 picked = held([P, M], BF16, "diesel%d" % i)
             else:
-                picked = placed([P, M], BF16, "diesel%d" % i, SHARED + 1024 * (TILES - 2 - i))
+                picked = placed([P, M], BF16, "diesel%d" % i, SHARED + 1024 * (TILES - 1 - i))
             pick(i in DIESEL_ON_SCALAR, picked[:], win, pos3_sb[:])
             nc.sync.dma_start(z2_rows[b][32 * t:32 * (t + 1), :].bitcast(I32).rearrange("p (j c) -> p j c", j=PACK),
                               picked[:].bitcast(I32))
@@ -200,7 +204,7 @@ def tile_list_crack_hedge_tilt_kernel(tc, tab_words, tab_scales, offs, pos1, pos
                         y_pass(acc, i, h, a)
                     nc.scalar.copy(y_win[i][:, BANK * h:BANK * (h + 1)], acc[:])
             if i % PACK == 2:
-                w1_q.append(quantize("w1_%d" % (i // PACK), round_w1(i // PACK)))
+                w1_q.append(quantize("w1_%d" % (i // PACK), round_w1(i // PACK), 2 - i // PACK))
             if i % 2 == 0:
                 pick_diesel(i - 2, y_win[i - 2])
                 pick_diesel(i - 1, y_win[i - 1])
@@ -230,7 +234,7 @@ def tile_list_crack_hedge_tilt_kernel(tc, tab_words, tab_scales, offs, pos1, pos
 
         def pick_petrol(i, win, lo, hi):
             b, t = divmod(i, PACK)
-            pick(i in PETROL_ON_SCALAR, petrol[b][:, M * t + lo:M * t + hi], win, pos2_sb[:, lo // 16:hi // 16])
+            pick(i == TILES - 1 and lo >= PETROL_SPLIT, petrol[b][:, M * t + lo:M * t + hi], win, pos2_sb[:, lo // 16:hi // 16])
 
         def size_of_crude(i, lo, hi):
             b, t = divmod(i, PACK)
@@ -253,6 +257,8 @@ def tile_list_crack_hedge_tilt_kernel(tc, tab_words, tab_scales, offs, pos1, pos
         o2_banks = []
         x_win = [x_window(0)]
         for i in range(WHOLE):
+            if i == PACK:
+                size_of_crude(i - 1, 0, M)
             x_win.append(x_window(i + 1))
             if i == 3:
                 z2 = quantize("z2", weave_z2()[:])
@@ -266,7 +272,7 @@ def tile_list_crack_hedge_tilt_kernel(tc, tab_words, tab_scales, offs, pos1, pos
                 z1_first = quantize("z1_0", weave_z1(nc.gpsimd, placed([P, PACK * M], BF16, "z1_woven", 8192)[:], 0, 0, M))
             pick_crude(i, x_win[i], 0, M)
             pick_petrol(i, x_win[i], 0, M)
-            if i >= 1:
+            if i >= 1 and i != PACK:
                 size_of_crude(i - 1, 0, M)
 
         size_of_crude(WHOLE - 1, 0, M)
@@ -308,15 +314,15 @@ def tile_list_crack_hedge_tilt_kernel(tc, tab_words, tab_scales, offs, pos1, pos
         def finish(u):
             lo, hi = spans[u]
             width = hi - lo
-            for half in range(2):
-                tilt = held([P, 2 * width], F32, "tilt%d%d" % (u, half))
-                for e in range(2):
-                    n = 2 * half + e
+            groups = [(0, 1), (2, 3)] if u + 1 < len(PIECES) else [(0, 1), (2,), (3,)]
+            for group in groups:
+                tilt = held([P, len(group) * width], F32, "tilt%d%d" % (u, group[0]))
+                for e, n in enumerate(group):
                     nc.vector.scalar_tensor_tensor(tilt[:, width * e:width * (e + 1)], o1[u][n], rl_sb[:, n:n + 1],
                                                    o2[n][:, lo:hi], ALU.mult, ALU.subtract)
                 nc.scalar.activation(tilt[:], tilt[:], ACT.Tanh)
-                dst = out[2 * P * half:2 * P * (half + 1), lo:hi].rearrange("(e p) m -> p e m", p=P)
-                nc.sync.dma_start(dst, tilt[:].rearrange("p (e m) -> p e m", e=2))
+                dst = out[P * group[0]:P * (group[-1] + 1), lo:hi].rearrange("(e p) m -> p e m", p=P)
+                nc.sync.dma_start(dst, tilt[:].rearrange("p (e m) -> p e m", e=len(group)))
 
         for u in range(len(PIECES)):
             picks(u)

@@ -27,7 +27,7 @@ WINDOWS = 8
 PIECES = [256, 128, 128]
 DIESEL_ON_SCALAR = (1,)
 CRUDE_ON_VECTOR = (3, 4, 5)
-PETROL_SPLIT = 256
+PETROL_SPLIT = 0
 SHARED = 36 * 1024
 EARLY_DIESEL = 2
 WHOLE = 7
@@ -199,7 +199,7 @@ def tile_list_crack_hedge_tilt_kernel(tc, tab_words, tab_scales, offs, pos1, pos
             if i < TILES:
                 y_win.append(window())
                 for h in range(2):
-                    acc = bank((2 * i + h) % STAGE_BANKS)
+                    acc = bank((2 * i + h) % (2 * STAGE_BANKS))
                     for a in range(2):
                         y_pass(acc, i, h, a)
                     nc.scalar.copy(y_win[i][:, BANK * h:BANK * (h + 1)], acc[:])
@@ -222,7 +222,7 @@ def tile_list_crack_hedge_tilt_kernel(tc, tab_words, tab_scales, offs, pos1, pos
         def x_window(i):
             win = window()
             for h in range(2):
-                acc = bank((2 * i + h) % STAGE_BANKS)
+                acc = bank((2 * i + h) % (2 * STAGE_BANKS))
                 for a in range(2):
                     x_pass(acc, i, h, a)
                 nc.scalar.activation(win[:, BANK * h:BANK * (h + 1)], acc[:], ACT.Copy, scale=cg_sign[:, i:i + 1])
@@ -262,10 +262,6 @@ def tile_list_crack_hedge_tilt_kernel(tc, tab_words, tab_scales, offs, pos1, pos
             x_win.append(x_window(i + 1))
             if i == 3:
                 z2 = quantize("z2", weave_z2()[:])
-                for n in range(N_TILES):
-                    o2_banks.append(bank(STAGE_BANKS + n))
-                    for a in range(2):
-                        o_pass(o2_banks[n][:], n, a, z2, slice(M * a, M * (a + 1)), a == 0, a == 1)
                 petrol.append(placed([P, PACK * M], F32, "petrol1", 0))
                 crude.append(placed([P, PACK * M], F32, "crude1", 12288))
             if i == PACK + 1:
@@ -278,6 +274,11 @@ def tile_list_crack_hedge_tilt_kernel(tc, tab_words, tab_scales, offs, pos1, pos
         size_of_crude(WHOLE - 1, 0, M)
         edges = [sum(PIECES[:u]) for u in range(len(PIECES) + 1)]
         spans = [(edges[u], edges[u + 1]) for u in range(len(PIECES))]
+
+        for n in range(N_TILES):
+            o2_banks.append(bank(STAGE_BANKS + n))
+            for a in range(2):
+                o_pass(o2_banks[n][:], n, a, z2, slice(M * a, M * (a + 1)), a == 0, a == 1)
 
         o1 = []
         free_banks = list(range(STAGE_BANKS))

@@ -25,11 +25,12 @@ N_TILES = N // P
 STAGE_BANKS = 4
 WINDOWS = 8
 PIECES = [256, 128, 128]
-DIESEL_ON_SCALAR = (1,)
+DIESEL_ON_SCALAR = (6, 7)
 CRUDE_ON_VECTOR = (3, 4, 5)
-PETROL_SPLIT = 0
+PETROL_SPLIT = 256
 SHARED = 36 * 1024
 EARLY_DIESEL = 2
+DIESEL_BYTES = 6 * 1024
 WHOLE = 7
 W2_EDGES = [0, 2 * P, 4 * P, H]
 
@@ -140,18 +141,17 @@ def tile_list_crack_hedge_tilt_kernel(tc, tab_words, tab_scales, offs, pos1, pos
                                       in_=woven[:, PACK * c0:PACK * (c0 + step)])
             return codes, plane
 
-        def round_w1(b):
-            both = placed([P, (SHARED + 6 * 1024 * (1 - b)) // 2], BF16, "w1_rounded%d" % b, 0)[:, 0:2 * PACK * PASS]
-            for a in range(2):
-                dst = both[:, PACK * PASS * a:PACK * PASS * (a + 1)]
-                if b == 0:
-                    nc.vector.tensor_copy(dst.rearrange("p (t m j) -> p m j t", t=PACK, j=PACK),
-                                          w1_raw[b][a][:].rearrange("p (j m t) -> p m j t", t=PACK, j=PACK))
-                else:
-                    nc.gpsimd.tensor_scalar(dst.rearrange("p (t m j) -> p m t j", t=PACK, j=PACK),
-                                            w1_raw[b][a][:].rearrange("p (j m t) -> p m t j", t=PACK, j=PACK),
-                                            1.0, 0.0, ALU.mult, ALU.add)
-            return both
+        def round_w1(b, a):
+            start, stop = {(0, 0): (0, 4096), (0, 1): (4096, 8192), (1, 0): (8192, SHARED + DIESEL_BYTES), (1, 1): (0, SHARED)}[b, a]
+            dst = placed([P, (stop - start) // 2], BF16, "w1_rounded%d%d" % (b, a), start)[:, 0:PACK * PASS]
+            if (b, a) == (1, 1):
+                nc.gpsimd.tensor_scalar(dst.rearrange("p (t m j) -> p m t j", t=PACK, j=PACK),
+                                        w1_raw[b][a][:].rearrange("p (j m t) -> p m t j", t=PACK, j=PACK),
+                                        1.0, 0.0, ALU.mult, ALU.add)
+            else:
+                nc.vector.tensor_copy(dst.rearrange("p (t m j) -> p m j t", t=PACK, j=PACK),
+                                      w1_raw[b][a][:].rearrange("p (j m t) -> p m j t", t=PACK, j=PACK))
+            return dst
 
         def y_pass(acc, i, h, a):
             g = sum(1 for edge in W2_EDGES[1:] if edge <= P * i)
@@ -165,8 +165,8 @@ def tile_list_crack_hedge_tilt_kernel(tc, tab_words, tab_scales, offs, pos1, pos
         def x_pass(acc, i, h, a):
             b, t = divmod(i, PACK)
             cols = slice(BANK * h, BANK * (h + 1))
-            wc = slice(PASS * a + P * t, PASS * a + P * (t + 1))
-            nc.tensor.matmul_mx(out=acc[:], lhsT=w1_q[b][0][:, wc].bitcast(E4M3), lhsT_scale=w1_q[b][1][:, wc],
+            wc = slice(P * t, P * (t + 1))
+            nc.tensor.matmul_mx(out=acc[:], lhsT=w1_q[b, a][0][:, wc].bitcast(E4M3), lhsT_scale=w1_q[b, a][1][:, wc],
                                 rhs=v_w[a][:, cols].bitcast(E4M3), rhs_scale=v_s[:, S * a + BANK * h:S * a + BANK * (h + 1)], start=(a == 0), stop=(a == 1))
 
         def o_pass(acc, n, a, z, cols, start, stop):
@@ -186,7 +186,7 @@ def tile_list_crack_hedge_tilt_kernel(tc, tab_words, tab_scales, offs, pos1, pos
             nc.sync.dma_start(z2_rows[b][32 * t:32 * (t + 1), :].bitcast(I32).rearrange("p (j c) -> p j c", j=PACK),
                               picked[:].bitcast(I32))
 
-        w1_q = []
+        w1_q = {}
         first = [[bank(2 * i + h) for h in range(2)] for i in range(2)]
         y_win = [window() for i in range(2)]
         for h in range(2):
@@ -203,8 +203,12 @@ def tile_list_crack_hedge_tilt_kernel(tc, tab_words, tab_scales, offs, pos1, pos
                     for a in range(2):
                         y_pass(acc, i, h, a)
                     nc.scalar.copy(y_win[i][:, BANK * h:BANK * (h + 1)], acc[:])
-            if i % PACK == 2:
-                w1_q.append(quantize("w1_%d" % (i // PACK), round_w1(i // PACK), 2 - i // PACK))
+            if i == 2:
+                groups = [(b, a) for b in range(2) for a in range(2)]
+                rounded = [round_w1(b, a) for b, a in groups[:3]]
+                for group, values in zip(groups, rounded):
+                    w1_q[group] = quantize("w1_%d%d" % group, values)
+                w1_q[groups[3]] = quantize("w1_11", round_w1(*groups[3]))
             if i % 2 == 0:
                 pick_diesel(i - 2, y_win[i - 2])
                 pick_diesel(i - 1, y_win[i - 1])

@@ -25,8 +25,8 @@ N_TILES = N // P
 STAGE_BANKS = 4
 WINDOWS = 8
 PIECES = [256, 128, 128]
-DIESEL_ON_SCALAR = (6, 7)
-CRUDE_ON_VECTOR = (3, 4, 5)
+DIESEL_ON_SCALAR = (5, 6, 7)
+CRUDE_ON_VECTOR = (2, 3, 4, 5)
 PETROL_SPLIT = 256
 SHARED = 36 * 1024
 EARLY_DIESEL = 2

@@ -20,19 +20,26 @@ P = 128
 PACK = 4
 PASS = P * PACK
 BANK = 512
+BANKS = 8
 TILES = H // P
 N_TILES = N // P
-STAGE_BANKS = 4
-WINDOWS = 8
+LAST = TILES - 1
+WINDOWS = TILES
 PIECES = [256, 128, 128]
-DIESEL_ON_SCALAR = (5, 6, 7)
-CRUDE_ON_VECTOR = (2, 3, 4, 5)
-PETROL_SPLIT = 256
-SHARED = 36 * 1024
-EARLY_DIESEL = 2
-DIESEL_BYTES = 6 * 1024
-WHOLE = 7
 W2_EDGES = [0, 2 * P, 4 * P, H]
+
+Y_AHEAD = 2
+Y_ON_SCALAR = 5
+P1_ON_VECTOR = range(2, 6)
+P2_SPLIT = 256
+
+KB = 1024
+AT_W1_EARLY = 9 * KB
+AT_W1_LAST = 20 * KB
+AT_Y_PICKED = 9 * KB
+AT_X_PICKED = [23 * KB, 0]
+AT_Z2 = 15 * KB
+AT_Z1 = 16 * KB
 
 
 def tile_list_crack_hedge_tilt_kernel(tc, tab_words, tab_scales, offs, pos1, pos2, pos3, w1,
@@ -40,21 +47,21 @@ def tile_list_crack_hedge_tilt_kernel(tc, tab_words, tab_scales, offs, pos1, pos
     nc = tc.nc
     with ExitStack() as ctx:
         keep = ctx.enter_context(tc.tile_pool(name="keep", bufs=1))
-        ring = ctx.enter_context(tc.tile_pool(name="ring", bufs=2))
-        shared = ctx.enter_context(tc.tile_pool(name="shared", bufs=1))
+        ring = ctx.enter_context(tc.tile_pool(name="ring", bufs=WINDOWS))
+        staged = ctx.enter_context(tc.tile_pool(name="staged", bufs=1))
         psum = ctx.enter_context(tc.psum_pool(name="psum", bufs=1))
 
         def held(shape, dtype, name):
             return keep.tile(shape, dtype, name=name, align_bytes=64)
 
-        def bank(b):
-            return psum.tile([P, BANK], F32, name="bank", tag="bank%d" % b)
+        def placed(shape, dtype, name, offset):
+            return staged.tile(shape, dtype, name=name, align_bytes=64, offset=offset)
+
+        def bank(index):
+            return psum.tile([P, BANK], F32, name="bank", tag="bank%d" % index)
 
         def window():
-            return ring.tile([P, S], F32, name="window", tag="window", bufs=WINDOWS, align_bytes=64)
-
-        def placed(shape, dtype, name, offset):
-            return shared.tile(shape, dtype, name=name, align_bytes=64, offset=offset)
+            return ring.tile([P, S], F32, name="window", tag="window", align_bytes=64)
 
         offs_sb = keep.tile([P, S // 16], U16, name="offs_sb")
         pos1_sb = keep.tile([P, M // 16], U16, name="pos1_sb")
@@ -63,7 +70,7 @@ def tile_list_crack_hedge_tilt_kernel(tc, tab_words, tab_scales, offs, pos1, pos
         tab_w = [held([P, T], I32, "tab_w%d" % a) for a in range(2)]
         tab_s = held([P, T], U8, "tab_s")
         v_w = [held([P, S], I32, "v_w%d" % a) for a in range(2)]
-        picked_s = held([P, S], U8, "picked_s")
+        gathered_s = held([P, S], U8, "gathered_s")
         v_s = held([P, 2 * S], U8, "v_s")
         w2_cols = list(zip(W2_EDGES, W2_EDGES[1:]))
         w2_w = [held([P, 2 * 2 * (hi - lo)], U8, "w2_w%d" % lo) for lo, hi in w2_cols]
@@ -72,7 +79,7 @@ def tile_list_crack_hedge_tilt_kernel(tc, tab_words, tab_scales, offs, pos1, pos
         w3_w = held([P, 2 * N], I32, "w3_w")
         w3_s = held([P, N], U8, "w3_s")
         cg_sb = held([P, TILES], F32, "cg_sb")
-        cg_ge = held([P, TILES], F32, "cg_ge")
+        cg_step = held([P, TILES], F32, "cg_step")
         cg_sign = held([P, TILES], F32, "cg_sign")
         rl_sb = held([P, N_TILES], F32, "rl_sb")
 
@@ -89,10 +96,10 @@ def tile_list_crack_hedge_tilt_kernel(tc, tab_words, tab_scales, offs, pos1, pos
             src = w1[PASS * a:PASS * (a + 1), PASS * b:PASS * (b + 1)].rearrange("(p j) c -> p j c", j=PACK)
             nc.sync.dma_start(w1_raw[b][a][:].rearrange("p (j c) -> p j c", j=PACK), src)
 
-        def load_w2(queue, g):
-            lo, hi = w2_cols[g]
-            queue.dma_start(w2_w[g][:].bitcast(I32).rearrange("p (a c) -> p a c", a=2),
-                              w2_words[:, :, 2 * lo:2 * hi].bitcast(I32).rearrange("a p c -> p a c"))
+        def load_w2(queue, part):
+            lo, hi = w2_cols[part]
+            queue.dma_start(w2_w[part][:].bitcast(I32).rearrange("p (a c) -> p a c", a=2),
+                            w2_words[:, :, 2 * lo:2 * hi].bitcast(I32).rearrange("a p c -> p a c"))
 
         nc.sync.dma_start(offs_sb[:], offs)
         nc.sync.dma_start(tab_s[0:32, :].bitcast(I32), tab_scales.bitcast(I32).rearrange("a s c -> s a c"))
@@ -100,12 +107,12 @@ def tile_list_crack_hedge_tilt_kernel(tc, tab_words, tab_scales, offs, pos1, pos
         load_w2(nc.scalar, 0)
         for q in range(4):
             nc.scalar.dma_start(w2_s[32 * q:32 * q + 4, :].bitcast(I32).rearrange("p (a c) -> p a c", a=2),
-                              w2_scales[:, 4 * q:4 * q + 4, :].bitcast(I32).rearrange("a r c -> r a c"))
+                                w2_scales[:, 4 * q:4 * q + 4, :].bitcast(I32).rearrange("a s c -> s a c"))
         load_words(1)
-        nc.vector.tensor_copy(picked_s[:], tab_s[:].indirect(offs_sb[:]))
+        nc.vector.tensor_copy(gathered_s[:], tab_s[:].indirect(offs_sb[:]))
         for q in range(4):
             nc.sync.dma_start(v_s[32 * q:32 * q + 4, :].bitcast(I32).rearrange("p (a c) -> p a c", a=2),
-                              picked_s[8 * q:8 * q + 8, :].bitcast(I32))
+                              gathered_s[8 * q:8 * q + 8, :].bitcast(I32))
         load_w2(nc.sync, 1)
         nc.sync.dma_start(cg_sb[:].rearrange("p (b t) -> p b t", b=2), cg.rearrange("(b p t) -> p b t", b=2, t=PACK))
         load_w1(0, 0)
@@ -117,8 +124,8 @@ def tile_list_crack_hedge_tilt_kernel(tc, tab_words, tab_scales, offs, pos1, pos
         load_w1(1, 0)
         load_w1(1, 1)
 
-        nc.gpsimd.tensor_scalar(cg_ge[:], cg_sb[:], 0.0, 2.0, ALU.is_ge, ALU.mult)
-        nc.gpsimd.tensor_scalar(cg_sign[:], cg_ge[:], -1.0, 1.0, ALU.add, ALU.mult)
+        nc.gpsimd.tensor_scalar(cg_step[:], cg_sb[:], 0.0, 2.0, ALU.is_ge, ALU.mult)
+        nc.gpsimd.tensor_scalar(cg_sign[:], cg_step[:], -1.0, 1.0, ALU.add, ALU.mult)
 
         for a in range(2):
             for h in range(2):
@@ -131,87 +138,88 @@ def tile_list_crack_hedge_tilt_kernel(tc, tab_words, tab_scales, offs, pos1, pos
             else:
                 nc.vector.tensor_copy(dst, win[:].indirect(places))
 
-        def quantize(name, woven, parts=1):
-            width = woven.shape[1] // PACK
+        def quantize(name, values):
+            width = values.shape[1] // PACK
             codes = held([P, width], U32, name + "_w")
             plane = held([P, width], U8, name + "_s")
-            step = width // parts
-            for c0 in range(0, width, step):
-                nc.vector.quantize_mx(out=codes[:, c0:c0 + step].bitcast(E4M3), scales=plane[:, c0:c0 + step],
-                                      in_=woven[:, PACK * c0:PACK * (c0 + step)])
+            nc.vector.quantize_mx(out=codes[:].bitcast(E4M3), scales=plane[:], in_=values)
             return codes, plane
 
-        def round_w1(b, a):
-            start, stop = {(0, 0): (0, 4096), (0, 1): (4096, 8192), (1, 0): (8192, SHARED + DIESEL_BYTES), (1, 1): (0, SHARED)}[b, a]
-            dst = placed([P, (stop - start) // 2], BF16, "w1_rounded%d%d" % (b, a), start)[:, 0:PACK * PASS]
-            if (b, a) == (1, 1):
-                nc.gpsimd.tensor_scalar(dst.rearrange("p (t m j) -> p m t j", t=PACK, j=PACK),
-                                        w1_raw[b][a][:].rearrange("p (j m t) -> p m t j", t=PACK, j=PACK),
-                                        1.0, 0.0, ALU.mult, ALU.add)
-            else:
-                nc.vector.tensor_copy(dst.rearrange("p (t m j) -> p m j t", t=PACK, j=PACK),
+        def prepare_w1():
+            parts = [(b, a) for b in range(2) for a in range(2)]
+            size = PACK * PASS
+            early = placed([P, 3 * size], BF16, "w1_early", AT_W1_EARLY)
+            for e, (b, a) in enumerate(parts[:3]):
+                nc.vector.tensor_copy(early[:, size * e:size * (e + 1)].rearrange("p (t m j) -> p m j t", t=PACK, j=PACK),
                                       w1_raw[b][a][:].rearrange("p (j m t) -> p m j t", t=PACK, j=PACK))
-            return dst
+            operands = {}
+            for e, part in enumerate(parts[:3]):
+                operands[part] = quantize("w1_%d%d" % part, early[:, size * e:size * (e + 1)])
+            b, a = parts[3]
+            last = placed([P, size], BF16, "w1_last", AT_W1_LAST)
+            nc.gpsimd.tensor_scalar(last[:].rearrange("p (t m j) -> p m t j", t=PACK, j=PACK),
+                                    w1_raw[b][a][:].rearrange("p (j m t) -> p m t j", t=PACK, j=PACK),
+                                    1.0, 0.0, ALU.mult, ALU.add)
+            operands[b, a] = quantize("w1_%d%d" % (b, a), last[:])
+            return operands
+
+        def table_operand(h, a):
+            return dict(rhs=v_w[a][:, BANK * h:BANK * (h + 1)].bitcast(E4M3),
+                        rhs_scale=v_s[:, S * a + BANK * h:S * a + BANK * (h + 1)], start=(a == 0), stop=(a == 1))
 
         def y_pass(acc, i, h, a):
-            g = sum(1 for edge in W2_EDGES[1:] if edge <= P * i)
-            lo, hi = w2_cols[g]
-            cols = slice(BANK * h, BANK * (h + 1))
-            c0 = (hi - lo) * a + P * i - lo
-            s0 = H * a + P * i
-            nc.tensor.matmul_mx(out=acc[:], lhsT=w2_w[g][:, 2 * c0:2 * (c0 + P)].bitcast(E2M1), lhsT_scale=w2_s[:, s0:s0 + P],
-                                rhs=v_w[a][:, cols].bitcast(E4M3), rhs_scale=v_s[:, S * a + BANK * h:S * a + BANK * (h + 1)], start=(a == 0), stop=(a == 1))
+            part = sum(1 for edge in W2_EDGES[1:] if edge <= P * i)
+            lo, hi = w2_cols[part]
+            word = (hi - lo) * a + P * i - lo
+            byte = H * a + P * i
+            nc.tensor.matmul_mx(out=acc[:], lhsT=w2_w[part][:, 2 * word:2 * (word + P)].bitcast(E2M1),
+                                lhsT_scale=w2_s[:, byte:byte + P], **table_operand(h, a))
 
         def x_pass(acc, i, h, a):
             b, t = divmod(i, PACK)
-            cols = slice(BANK * h, BANK * (h + 1))
-            wc = slice(P * t, P * (t + 1))
-            nc.tensor.matmul_mx(out=acc[:], lhsT=w1_q[b, a][0][:, wc].bitcast(E4M3), lhsT_scale=w1_q[b, a][1][:, wc],
-                                rhs=v_w[a][:, cols].bitcast(E4M3), rhs_scale=v_s[:, S * a + BANK * h:S * a + BANK * (h + 1)], start=(a == 0), stop=(a == 1))
+            codes, plane = w1_mx[b, a]
+            nc.tensor.matmul_mx(out=acc[:], lhsT=codes[:, P * t:P * (t + 1)].bitcast(E4M3),
+                                lhsT_scale=plane[:, P * t:P * (t + 1)], **table_operand(h, a))
 
-        def o_pass(acc, n, a, z, cols, start, stop):
-            c0 = N * a + P * n
-            nc.tensor.matmul_mx(out=acc, lhsT=w3_w[:, c0:c0 + P].bitcast(E4M3), lhsT_scale=w3_s[4 * a:, P * n:P * (n + 1)],
-                                rhs=z[0][:, cols].bitcast(E4M3), rhs_scale=z[1][:, cols], start=start, stop=stop)
+        def o_pass(acc, n, b, z, cols, start, stop):
+            word = N * b + P * n
+            codes, plane = z
+            nc.tensor.matmul_mx(out=acc, lhsT=w3_w[:, word:word + P].bitcast(E4M3), lhsT_scale=w3_s[4 * b:, P * n:P * (n + 1)],
+                                rhs=codes[:, cols].bitcast(E4M3), rhs_scale=plane[:, cols], start=start, stop=stop)
 
         z2_rows = [held([P, PACK * M], BF16, "z2_rows%d" % b) for b in range(2)]
 
-        def pick_diesel(i, win):
-            b, t = divmod(i, PACK)
-            if i < EARLY_DIESEL:
-                picked = held([P, M], BF16, "diesel%d" % i)
+        def pick_y(i):
+            b, quarter = divmod(i, PACK)
+            if i < Y_AHEAD:
+                picked = held([P, M], BF16, "y_picked%d" % i)
             else:
-                picked = placed([P, M], BF16, "diesel%d" % i, SHARED + 1024 * (TILES - 1 - i))
-            pick(i in DIESEL_ON_SCALAR, picked[:], win, pos3_sb[:])
-            nc.sync.dma_start(z2_rows[b][32 * t:32 * (t + 1), :].bitcast(I32).rearrange("p (j c) -> p j c", j=PACK),
+                picked = placed([P, M], BF16, "y_picked%d" % i, AT_Y_PICKED + KB * (LAST - i))
+            pick(i >= Y_ON_SCALAR, picked[:], y_win[i], pos3_sb[:])
+            nc.sync.dma_start(z2_rows[b][32 * quarter:32 * (quarter + 1), :].bitcast(I32).rearrange("p (j c) -> p j c", j=PACK),
                               picked[:].bitcast(I32))
 
-        w1_q = {}
-        first = [[bank(2 * i + h) for h in range(2)] for i in range(2)]
+        first_banks = [[bank(2 * i + h) for h in range(2)] for i in range(2)]
         y_win = [window() for i in range(2)]
         for h in range(2):
             for i in range(2):
-                y_pass(first[i][h], i, h, 0)
+                y_pass(first_banks[i][h], i, h, 0)
             for i in range(2):
-                y_pass(first[i][h], i, h, 1)
-                nc.scalar.copy(y_win[i][:, BANK * h:BANK * (h + 1)], first[i][h][:])
+                y_pass(first_banks[i][h], i, h, 1)
+                nc.scalar.copy(y_win[i][:, BANK * h:BANK * (h + 1)], first_banks[i][h][:])
         for i in range(2, TILES + 1):
             if i < TILES:
                 y_win.append(window())
                 for h in range(2):
-                    acc = bank((2 * i + h) % (2 * STAGE_BANKS))
+                    acc = bank((2 * i + h) % BANKS)
                     for a in range(2):
                         y_pass(acc, i, h, a)
                     nc.scalar.copy(y_win[i][:, BANK * h:BANK * (h + 1)], acc[:])
             if i == 2:
-                groups = [(b, a) for b in range(2) for a in range(2)]
-                rounded = [round_w1(b, a) for b, a in groups[:3]]
-                for group, values in zip(groups, rounded):
-                    w1_q[group] = quantize("w1_%d%d" % group, values)
-                w1_q[groups[3]] = quantize("w1_11", round_w1(*groups[3]))
+                w1_mx = prepare_w1()
             if i % 2 == 0:
-                pick_diesel(i - 2, y_win[i - 2])
-                pick_diesel(i - 1, y_win[i - 1])
+                pick_y(i - 2)
+                pick_y(i - 1)
 
         nc.sync.dma_start(w3_w[:].rearrange("p (a c) -> p a c", a=2),
                           w3_words.rearrange("a p c i -> p a (c i)").bitcast(I32))
@@ -220,72 +228,71 @@ def tile_list_crack_hedge_tilt_kernel(tc, tab_words, tab_scales, offs, pos1, pos
         with nc.allow_non_contiguous_dma(reason="one ratio for each partition"):
             nc.sync.dma_start(rl_sb[:], rl.rearrange("(n p) -> p n", p=P))
 
-        crude = [placed([P, PACK * M], F32, "crude0", 20480)]
-        petrol = [placed([P, PACK * M], F32, "petrol0", 28672)]
+        def picked_tile(b):
+            both = placed([P, 2 * PACK * M], F32, "x_picked%d" % b, AT_X_PICKED[b])
+            return both[:, 0:PACK * M], both[:, PACK * M:2 * PACK * M]
 
         def x_window(i):
             win = window()
             for h in range(2):
-                acc = bank((2 * i + h) % (2 * STAGE_BANKS))
+                acc = bank((2 * i + h) % BANKS)
                 for a in range(2):
                     x_pass(acc, i, h, a)
                 nc.scalar.activation(win[:, BANK * h:BANK * (h + 1)], acc[:], ACT.Copy, scale=cg_sign[:, i:i + 1])
             return win
 
-        def pick_crude(i, win, lo, hi):
+        def pick_x(i, lo, hi):
             b, t = divmod(i, PACK)
-            pick(i not in CRUDE_ON_VECTOR, crude[b][:, M * t + lo:M * t + hi], win, pos1_sb[:, lo // 16:hi // 16])
+            x1, x2 = x_picked[b]
+            pick(i not in P1_ON_VECTOR, x1[:, M * t + lo:M * t + hi], x_win[i], pos1_sb[:, lo // 16:hi // 16])
+            pick(i == LAST and lo >= P2_SPLIT, x2[:, M * t + lo:M * t + hi], x_win[i], pos2_sb[:, lo // 16:hi // 16])
 
-        def pick_petrol(i, win, lo, hi):
+        def scaled_abs(i, lo, hi):
             b, t = divmod(i, PACK)
-            pick(i == TILES - 1 and lo >= PETROL_SPLIT, petrol[b][:, M * t + lo:M * t + hi], win, pos2_sb[:, lo // 16:hi // 16])
-
-        def size_of_crude(i, lo, hi):
-            b, t = divmod(i, PACK)
-            values = crude[b][:, M * t + lo:M * t + hi]
+            values = x_picked[b][0][:, M * t + lo:M * t + hi]
             nc.scalar.activation(values, values, ACT.Abs, scale=cg_sb[:, i:i + 1])
 
-        def weave_z1(engine, woven, b, lo, hi):
-            def walk(planes):
-                return planes[:].rearrange("p (t m) -> p t m", t=PACK)[:, :, lo:hi].rearrange("p t (c i) -> p c t i", i=2)
-            engine.tensor_tensor(woven.rearrange("p (c i t) -> p c t i", t=PACK, i=2), walk(crude[b]), walk(petrol[b]), ALU.mult)
-            return woven
+        def form_z1(engine, dst, b, lo, hi):
+            def walk(tiles):
+                return tiles.rearrange("p (t m) -> p t m", t=PACK)[:, :, lo:hi].rearrange("p t (c i) -> p c t i", i=2)
+            x1, x2 = x_picked[b]
+            engine.tensor_tensor(dst.rearrange("p (c i t) -> p c t i", t=PACK, i=2), walk(x1), walk(x2), ALU.mult)
+            return dst
 
         def weave_z2():
-            both = placed([P, 2 * PACK * M], BF16, "z2_woven", 6144)
+            both = placed([P, 2 * PACK * M], BF16, "z2_woven", AT_Z2)
             for b in range(2):
                 nc.gpsimd.tensor_scalar(both[:, PACK * M * b:PACK * M * (b + 1)].rearrange("p (m t) -> p m t", t=PACK),
                                         z2_rows[b][:].rearrange("p (t m) -> p m t", t=PACK), 1.0, 0.0, ALU.mult, ALU.add)
-            return both
+            return both[:]
+
+        x_picked = [picked_tile(0)]
+        x_win = [x_window(0)]
+        for i in range(LAST):
+            if i == PACK:
+                scaled_abs(i - 1, 0, M)
+            x_win.append(x_window(i + 1))
+            if i == PACK - 1:
+                z2 = quantize("z2", weave_z2())
+                x_picked.append(picked_tile(1))
+            if i == PACK + 1:
+                z1_first = quantize("z1_0", form_z1(nc.gpsimd, placed([P, PACK * M], BF16, "z1_first", AT_Z1)[:], 0, 0, M))
+            pick_x(i, 0, M)
+            if i >= 1 and i != PACK:
+                scaled_abs(i - 1, 0, M)
+        scaled_abs(LAST - 1, 0, M)
+
+        edges = [sum(PIECES[:u]) for u in range(len(PIECES) + 1)]
+        spans = list(zip(edges, edges[1:]))
 
         o2_banks = []
-        x_win = [x_window(0)]
-        for i in range(WHOLE):
-            if i == PACK:
-                size_of_crude(i - 1, 0, M)
-            x_win.append(x_window(i + 1))
-            if i == 3:
-                z2 = quantize("z2", weave_z2()[:])
-                petrol.append(placed([P, PACK * M], F32, "petrol1", 0))
-                crude.append(placed([P, PACK * M], F32, "crude1", 12288))
-            if i == PACK + 1:
-                z1_first = quantize("z1_0", weave_z1(nc.gpsimd, placed([P, PACK * M], BF16, "z1_woven", 8192)[:], 0, 0, M))
-            pick_crude(i, x_win[i], 0, M)
-            pick_petrol(i, x_win[i], 0, M)
-            if i >= 1 and i != PACK:
-                size_of_crude(i - 1, 0, M)
-
-        size_of_crude(WHOLE - 1, 0, M)
-        edges = [sum(PIECES[:u]) for u in range(len(PIECES) + 1)]
-        spans = [(edges[u], edges[u + 1]) for u in range(len(PIECES))]
-
         for n in range(N_TILES):
-            o2_banks.append(bank(STAGE_BANKS + n))
-            for a in range(2):
-                o_pass(o2_banks[n][:], n, a, z2, slice(M * a, M * (a + 1)), a == 0, a == 1)
+            o2_banks.append(bank(BANKS - N_TILES + n))
+            for b in range(2):
+                o_pass(o2_banks[n][:], n, b, z2, slice(M * b, M * (b + 1)), b == 0, b == 1)
 
         o1 = []
-        free_banks = list(range(STAGE_BANKS))
+        free_banks = list(range(BANKS - N_TILES))
         for lo, hi in spans:
             width = hi - lo
             share = BANK // width
@@ -296,25 +303,12 @@ def tile_list_crack_hedge_tilt_kernel(tc, tab_words, tab_scales, offs, pos1, pos
 
         o2 = [held([P, M], F32, "o2_%d" % n) for n in range(N_TILES)]
 
-        def picks(u):
-            lo, hi = spans[u]
-            for i in range(WHOLE, TILES):
-                pick_crude(i, x_win[i], lo, hi)
-                pick_petrol(i, x_win[i], lo, hi)
-            for i in range(WHOLE, TILES):
-                size_of_crude(i, lo, hi)
-
-        def empty_o2(half):
-            cols = slice(M // 2 * half, M // 2 * (half + 1))
-            for n in range(N_TILES):
-                nc.scalar.copy(o2[n][:, cols], o2_banks[n][:, cols])
-
-        def second_pass(u):
+        def close_o1(u):
             lo, hi = spans[u]
             share = BANK // (hi - lo)
-            z = quantize("z1_1%d" % u, woven1[u])
+            z1_piece = quantize("z1_1%d" % u, z1_second[u])
             for n in range(N_TILES):
-                o_pass(o1[u][n], n, 1, z, slice(0, hi - lo), False, n % share == share - 1)
+                o_pass(o1[u][n], n, 1, z1_piece, slice(0, hi - lo), False, n % share == share - 1)
 
         def finish(u):
             lo, hi = spans[u]
@@ -329,15 +323,18 @@ def tile_list_crack_hedge_tilt_kernel(tc, tab_words, tab_scales, offs, pos1, pos
                 dst = out[P * group[0]:P * (group[-1] + 1), lo:hi].rearrange("(e p) m -> p e m", p=P)
                 nc.sync.dma_start(dst, tilt[:].rearrange("p (e m) -> p e m", e=len(group)))
 
-        for u in range(len(PIECES)):
-            picks(u)
+        for lo, hi in spans:
+            pick_x(LAST, lo, hi)
+            scaled_abs(LAST, lo, hi)
         for half in range(2):
-            empty_o2(half)
-        woven1 = []
+            cols = slice(M // 2 * half, M // 2 * (half + 1))
+            for n in range(N_TILES):
+                nc.scalar.copy(o2[n][:, cols], o2_banks[n][:, cols])
+        z1_second = []
         for s in range(len(PIECES) + 2):
             if s < len(PIECES):
-                woven1.append(weave_z1(nc.vector, held([P, PACK * PIECES[s]], BF16, "z1_woven%d" % s)[:], 1, *spans[s]))
+                z1_second.append(form_z1(nc.vector, held([P, PACK * PIECES[s]], BF16, "z1_second%d" % s)[:], 1, *spans[s]))
             if 0 <= s - 1 < len(PIECES):
-                second_pass(s - 1)
+                close_o1(s - 1)
             if 0 <= s - 2 < len(PIECES):
                 finish(s - 2)

@@ -26,20 +26,21 @@ N_TILES = N // P
 LAST = TILES - 1
 WINDOWS = TILES
 PIECES = [256, 128, 128]
-W2_EDGES = [0, 2 * P, 4 * P, H]
+W2_EDGES = [0, 2 * P, 4 * P, 6 * P, H]
 
-Y_AHEAD = 2
-Y_ON_SCALAR = 5
-P1_ON_VECTOR = range(2, 6)
+Y_AHEAD = 3
+P1_ON_VECTOR = (0, 4, 5)
 P2_SPLIT = 256
+FIRST_WIDTH = 256
 
 KB = 1024
-AT_W1_EARLY = 9 * KB
-AT_W1_LAST = 20 * KB
-AT_Y_PICKED = 9 * KB
-AT_X_PICKED = [23 * KB, 0]
-AT_Z2 = 15 * KB
-AT_Z1 = 16 * KB
+AT_W1_RAW = 0
+AT_Y_PICKED = 0
+AT_W1 = 20 * KB
+AT_X2_FIRST = 16 * KB
+AT_X_SECOND = 32 * KB
+AT_Z2 = 26 * KB
+AT_Z1 = 26 * KB
 
 
 def tile_list_crack_hedge_tilt_kernel(tc, tab_words, tab_scales, offs, pos1, pos2, pos3, w1,
@@ -75,7 +76,8 @@ def tile_list_crack_hedge_tilt_kernel(tc, tab_words, tab_scales, offs, pos1, pos
         w2_cols = list(zip(W2_EDGES, W2_EDGES[1:]))
         w2_w = [held([P, 2 * 2 * (hi - lo)], U8, "w2_w%d" % lo) for lo, hi in w2_cols]
         w2_s = held([P, 2 * H], U8, "w2_s")
-        w1_raw = [[held([P, PACK * PASS], F32, "w1_raw%d%d" % (b, a)) for a in range(2)] for b in range(2)]
+        w1_raw = [[placed([P, PACK * PASS], F32, "w1_raw01", AT_W1_RAW) if (b, a) == (0, 1) else
+                   held([P, PACK * PASS], F32, "w1_raw%d%d" % (b, a)) for a in range(2)] for b in range(2)]
         w3_w = held([P, 2 * N], I32, "w3_w")
         w3_s = held([P, N], U8, "w3_s")
         cg_sb = held([P, TILES], F32, "cg_sb")
@@ -83,11 +85,11 @@ def tile_list_crack_hedge_tilt_kernel(tc, tab_words, tab_scales, offs, pos1, pos
         cg_sign = held([P, TILES], F32, "cg_sign")
         rl_sb = held([P, N_TILES], F32, "rl_sb")
 
-        nc.vector.memset(w2_s[:].bitcast(I32), 0)
+        nc.gpsimd.memset(w2_s[:].bitcast(I32), 0)
         nc.vector.memset(tab_s[32:64, :].bitcast(I32), 0)
         nc.vector.memset(tab_s[64:128, :].bitcast(I32), 0)
-        nc.vector.memset(v_s[:].bitcast(I32), 0)
-        nc.vector.memset(w3_s[:].bitcast(I32), 0)
+        nc.gpsimd.memset(v_s[:].bitcast(I32), 0)
+        nc.gpsimd.memset(w3_s[:].bitcast(I32), 0)
 
         def load_words(a):
             nc.sync.dma_start(tab_w[a][:], tab_words[a].rearrange("p t i -> p (t i)").bitcast(I32))
@@ -114,23 +116,24 @@ def tile_list_crack_hedge_tilt_kernel(tc, tab_words, tab_scales, offs, pos1, pos
             nc.sync.dma_start(v_s[32 * q:32 * q + 4, :].bitcast(I32).rearrange("p (a c) -> p a c", a=2),
                               gathered_s[8 * q:8 * q + 8, :].bitcast(I32))
         load_w2(nc.sync, 1)
-        nc.sync.dma_start(cg_sb[:].rearrange("p (b t) -> p b t", b=2), cg.rearrange("(b p t) -> p b t", b=2, t=PACK))
-        load_w1(0, 0)
         nc.sync.dma_start(pos3_sb[:], pos3)
+        load_w1(0, 0)
+        nc.sync.dma_start(cg_sb[:].rearrange("p (b t) -> p b t", b=2), cg.rearrange("(b p t) -> p b t", b=2, t=PACK))
         load_w2(nc.sync, 2)
         load_w1(0, 1)
-        nc.sync.dma_start(pos1_sb[:], pos1)
-        nc.sync.dma_start(pos2_sb[:], pos2)
+        load_w2(nc.sync, 3)
         load_w1(1, 0)
         load_w1(1, 1)
+        nc.sync.dma_start(pos1_sb[:], pos1)
+        nc.sync.dma_start(pos2_sb[:], pos2)
 
         nc.gpsimd.tensor_scalar(cg_step[:], cg_sb[:], 0.0, 2.0, ALU.is_ge, ALU.mult)
         nc.gpsimd.tensor_scalar(cg_sign[:], cg_step[:], -1.0, 1.0, ALU.add, ALU.mult)
 
-        for a in range(2):
-            for h in range(2):
-                nc.vector.tensor_copy(v_w[a][:, BANK * h:BANK * (h + 1)].bitcast(U32),
-                                      tab_w[a][:].bitcast(U32).indirect(offs_sb[:, BANK * h // 16:BANK * (h + 1) // 16]))
+        for a, width in enumerate([BANK, FIRST_WIDTH]):
+            for lo in range(0, S, width):
+                nc.vector.tensor_copy(v_w[a][:, lo:lo + width].bitcast(U32),
+                                      tab_w[a][:].bitcast(U32).indirect(offs_sb[:, lo // 16:(lo + width) // 16]))
 
         def pick(on_scalar, dst, win, places):
             if on_scalar:
@@ -145,41 +148,35 @@ def tile_list_crack_hedge_tilt_kernel(tc, tab_words, tab_scales, offs, pos1, pos
             nc.vector.quantize_mx(out=codes[:].bitcast(E4M3), scales=plane[:], in_=values)
             return codes, plane
 
-        def prepare_w1():
-            parts = [(b, a) for b in range(2) for a in range(2)]
-            size = PACK * PASS
-            early = placed([P, 3 * size], BF16, "w1_early", AT_W1_EARLY)
-            for e, (b, a) in enumerate(parts[:3]):
-                nc.vector.tensor_copy(early[:, size * e:size * (e + 1)].rearrange("p (t m j) -> p m j t", t=PACK, j=PACK),
-                                      w1_raw[b][a][:].rearrange("p (j m t) -> p m j t", t=PACK, j=PACK))
-            operands = {}
-            for e, part in enumerate(parts[:3]):
-                operands[part] = quantize("w1_%d%d" % part, early[:, size * e:size * (e + 1)])
-            b, a = parts[3]
-            last = placed([P, size], BF16, "w1_last", AT_W1_LAST)
-            nc.gpsimd.tensor_scalar(last[:].rearrange("p (t m j) -> p m t j", t=PACK, j=PACK),
+        size = PACK * PASS
+
+        def round_on_vector(dst, b, a):
+            nc.vector.tensor_copy(dst.rearrange("p (t m j) -> p m j t", t=PACK, j=PACK),
+                                  w1_raw[b][a][:].rearrange("p (j m t) -> p m j t", t=PACK, j=PACK))
+
+        def round_on_gpsimd(dst, b, a):
+            nc.gpsimd.tensor_scalar(dst.rearrange("p (t m j) -> p m t j", t=PACK, j=PACK),
                                     w1_raw[b][a][:].rearrange("p (j m t) -> p m t j", t=PACK, j=PACK),
                                     1.0, 0.0, ALU.mult, ALU.add)
-            operands[b, a] = quantize("w1_%d%d" % (b, a), last[:])
-            return operands
 
-        def table_operand(h, a):
-            return dict(rhs=v_w[a][:, BANK * h:BANK * (h + 1)].bitcast(E4M3),
-                        rhs_scale=v_s[:, S * a + BANK * h:S * a + BANK * (h + 1)], start=(a == 0), stop=(a == 1))
+        def table_operand(cols, a):
+            return dict(rhs=v_w[a][:, cols].bitcast(E4M3), rhs_scale=v_s[:, S * a + cols.start:S * a + cols.stop],
+                        start=(a == 0), stop=(a == 1))
 
-        def y_pass(acc, i, h, a):
+        def y_pass(acc, i, cols, a):
             part = sum(1 for edge in W2_EDGES[1:] if edge <= P * i)
             lo, hi = w2_cols[part]
             word = (hi - lo) * a + P * i - lo
             byte = H * a + P * i
-            nc.tensor.matmul_mx(out=acc[:], lhsT=w2_w[part][:, 2 * word:2 * (word + P)].bitcast(E2M1),
-                                lhsT_scale=w2_s[:, byte:byte + P], **table_operand(h, a))
+            nc.tensor.matmul_mx(out=acc, lhsT=w2_w[part][:, 2 * word:2 * (word + P)].bitcast(E2M1),
+                                lhsT_scale=w2_s[:, byte:byte + P], **table_operand(cols, a))
 
-        def x_pass(acc, i, h, a):
+        def x_pass(acc, i, cols, a):
             b, t = divmod(i, PACK)
-            codes, plane = w1_mx[b, a]
-            nc.tensor.matmul_mx(out=acc[:], lhsT=codes[:, P * t:P * (t + 1)].bitcast(E4M3),
-                                lhsT_scale=plane[:, P * t:P * (t + 1)], **table_operand(h, a))
+            codes, plane, first = w1_mx[b, a]
+            word = first + P * t
+            nc.tensor.matmul_mx(out=acc, lhsT=codes[:, word:word + P].bitcast(E4M3),
+                                lhsT_scale=plane[:, word:word + P], **table_operand(cols, a))
 
         def o_pass(acc, n, b, z, cols, start, stop):
             word = N * b + P * n
@@ -189,37 +186,53 @@ def tile_list_crack_hedge_tilt_kernel(tc, tab_words, tab_scales, offs, pos1, pos
 
         z2_rows = [held([P, PACK * M], BF16, "z2_rows%d" % b) for b in range(2)]
 
+        y_picked = []
+
         def pick_y(i):
             b, quarter = divmod(i, PACK)
             if i < Y_AHEAD:
-                picked = held([P, M], BF16, "y_picked%d" % i)
-            else:
-                picked = placed([P, M], BF16, "y_picked%d" % i, AT_Y_PICKED + KB * (LAST - i))
-            pick(i >= Y_ON_SCALAR, picked[:], y_win[i], pos3_sb[:])
+                y_picked.append(held([P, M], BF16, "y_picked%d" % i)[:])
+            elif i == Y_AHEAD:
+                group = placed([P, M * (TILES - i)], BF16, "y_picked%d" % i, AT_Y_PICKED)
+                y_picked.extend(group[:, M * e:M * (e + 1)] for e in range(TILES - i))
+            pick(i == LAST, y_picked[i], y_win[i], pos3_sb[:])
             nc.sync.dma_start(z2_rows[b][32 * quarter:32 * (quarter + 1), :].bitcast(I32).rearrange("p (j c) -> p j c", j=PACK),
-                              picked[:].bitcast(I32))
+                              y_picked[i].bitcast(I32))
 
-        first_banks = [[bank(2 * i + h) for h in range(2)] for i in range(2)]
+        def fill_window(g, one_pass, i, **scale):
+            win = window()
+            for h in range(2):
+                acc = bank((2 * g + h) % BANKS)
+                cols = slice(BANK * h, BANK * (h + 1))
+                for a in range(2):
+                    one_pass(acc[:], i, cols, a)
+                nc.scalar.activation(win[:, cols], acc[:], ACT.Copy, **scale)
+            return win
+
+        first_cols = [slice(lo, lo + FIRST_WIDTH) for lo in range(0, S, FIRST_WIDTH)]
+        first_banks = [[bank(2 * q + i) for i in range(2)] for q in range(len(first_cols))]
         y_win = [window() for i in range(2)]
-        for h in range(2):
+        for q, cols in enumerate(first_cols):
             for i in range(2):
-                y_pass(first_banks[i][h], i, h, 0)
-            for i in range(2):
-                y_pass(first_banks[i][h], i, h, 1)
-                nc.scalar.copy(y_win[i][:, BANK * h:BANK * (h + 1)], first_banks[i][h][:])
-        for i in range(2, TILES + 1):
-            if i < TILES:
-                y_win.append(window())
-                for h in range(2):
-                    acc = bank((2 * i + h) % BANKS)
-                    for a in range(2):
-                        y_pass(acc, i, h, a)
-                    nc.scalar.copy(y_win[i][:, BANK * h:BANK * (h + 1)], acc[:])
-            if i == 2:
-                w1_mx = prepare_w1()
-            if i % 2 == 0:
-                pick_y(i - 2)
-                pick_y(i - 1)
+                for a in range(2):
+                    y_pass(first_banks[q][i][:, 0:FIRST_WIDTH], i, cols, a)
+                nc.scalar.copy(y_win[i][:, cols], first_banks[q][i][:, 0:FIRST_WIDTH])
+        for i in range(2, TILES):
+            y_win.append(fill_window(i - 2, y_pass, i))
+
+        w1_mx = {}
+        w1_first = [held([P, size], BF16, "w1_00"), placed([P, size], BF16, "w1_01", AT_W1)]
+        round_on_gpsimd(w1_first[0][:], 0, 0)
+        for i in range(Y_AHEAD):
+            pick_y(i)
+        round_on_vector(w1_first[1][:], 0, 1)
+        for a in range(2):
+            w1_mx[0, a] = quantize("w1_0%d" % a, w1_first[a][:]) + (0,)
+        w1_second = placed([P, 2 * size], BF16, "w1_1", AT_W1)
+        for a in range(2):
+            round_on_gpsimd(w1_second[:, size * a:size * (a + 1)], 1, a)
+        for i in range(Y_AHEAD, TILES):
+            pick_y(i)
 
         nc.sync.dma_start(w3_w[:].rearrange("p (a c) -> p a c", a=2),
                           w3_words.rearrange("a p c i -> p a (c i)").bitcast(I32))
@@ -229,23 +242,21 @@ def tile_list_crack_hedge_tilt_kernel(tc, tab_words, tab_scales, offs, pos1, pos
             nc.sync.dma_start(rl_sb[:], rl.rearrange("(n p) -> p n", p=P))
 
         def picked_tile(b):
-            both = placed([P, 2 * PACK * M], F32, "x_picked%d" % b, AT_X_PICKED[b])
+            if b == 0:
+                return held([P, PACK * M], F32, "x1_first")[:], placed([P, PACK * M], F32, "x2_first", AT_X2_FIRST)[:]
+            both = placed([P, 2 * PACK * M], F32, "x_second", AT_X_SECOND)
             return both[:, 0:PACK * M], both[:, PACK * M:2 * PACK * M]
 
         def x_window(i):
-            win = window()
-            for h in range(2):
-                acc = bank((2 * i + h) % BANKS)
-                for a in range(2):
-                    x_pass(acc, i, h, a)
-                nc.scalar.activation(win[:, BANK * h:BANK * (h + 1)], acc[:], ACT.Copy, scale=cg_sign[:, i:i + 1])
-            return win
+            return fill_window(TILES - 2 + i, x_pass, i, scale=cg_sign[:, i:i + 1])
 
-        def pick_x(i, lo, hi):
+        def pick_p1(i, lo, hi):
             b, t = divmod(i, PACK)
-            x1, x2 = x_picked[b]
-            pick(i not in P1_ON_VECTOR, x1[:, M * t + lo:M * t + hi], x_win[i], pos1_sb[:, lo // 16:hi // 16])
-            pick(i == LAST and lo >= P2_SPLIT, x2[:, M * t + lo:M * t + hi], x_win[i], pos2_sb[:, lo // 16:hi // 16])
+            pick(i not in P1_ON_VECTOR, x_picked[b][0][:, M * t + lo:M * t + hi], x_win[i], pos1_sb[:, lo // 16:hi // 16])
+
+        def pick_p2(i, lo, hi):
+            b, t = divmod(i, PACK)
+            pick(i == LAST and lo >= P2_SPLIT, x_picked[b][1][:, M * t + lo:M * t + hi], x_win[i], pos2_sb[:, lo // 16:hi // 16])
 
         def scaled_abs(i, lo, hi):
             b, t = divmod(i, PACK)
@@ -266,19 +277,28 @@ def tile_list_crack_hedge_tilt_kernel(tc, tab_words, tab_scales, offs, pos1, pos
                                         z2_rows[b][:].rearrange("p (t m) -> p m t", t=PACK), 1.0, 0.0, ALU.mult, ALU.add)
             return both[:]
 
+        x_win = [x_window(i) for i in range(PACK)]
         x_picked = [picked_tile(0)]
-        x_win = [x_window(0)]
-        for i in range(LAST):
-            if i == PACK:
-                scaled_abs(i - 1, 0, M)
+        pick_p1(0, 0, M)
+        codes, plane = quantize("w1_1", w1_second[:])
+        for a in range(2):
+            w1_mx[1, a] = (codes, plane, PASS * a)
+        z2_woven = weave_z2()
+        for i in range(1, PACK):
+            pick_p1(i, 0, M)
+            scaled_abs(i - 1, 0, M)
+        x_win.append(x_window(PACK))
+        scaled_abs(PACK - 1, 0, M)
+        for i in range(PACK):
+            pick_p2(i, 0, M)
+        z2 = quantize("z2", z2_woven)
+        z1_rounded = form_z1(nc.gpsimd, placed([P, PACK * M], BF16, "z1_first", AT_Z1)[:], 0, 0, M)
+        x_picked.append(picked_tile(1))
+        for i in range(PACK, LAST):
             x_win.append(x_window(i + 1))
-            if i == PACK - 1:
-                z2 = quantize("z2", weave_z2())
-                x_picked.append(picked_tile(1))
-            if i == PACK + 1:
-                z1_first = quantize("z1_0", form_z1(nc.gpsimd, placed([P, PACK * M], BF16, "z1_first", AT_Z1)[:], 0, 0, M))
-            pick_x(i, 0, M)
-            if i >= 1 and i != PACK:
+            pick_p1(i, 0, M)
+            pick_p2(i, 0, M)
+            if i > PACK:
                 scaled_abs(i - 1, 0, M)
         scaled_abs(LAST - 1, 0, M)
 
@@ -287,12 +307,18 @@ def tile_list_crack_hedge_tilt_kernel(tc, tab_words, tab_scales, offs, pos1, pos
 
         o2_banks = []
         for n in range(N_TILES):
-            o2_banks.append(bank(BANKS - N_TILES + n))
+            o2_banks.append(bank(n))
             for b in range(2):
                 o_pass(o2_banks[n][:], n, b, z2, slice(M * b, M * (b + 1)), b == 0, b == 1)
 
+        for lo, hi in spans:
+            pick_p1(LAST, lo, hi)
+            pick_p2(LAST, lo, hi)
+            scaled_abs(LAST, lo, hi)
+        z1_first = quantize("z1_0", z1_rounded)
+
         o1 = []
-        free_banks = list(range(BANKS - N_TILES))
+        free_banks = list(range(N_TILES, BANKS))
         for lo, hi in spans:
             width = hi - lo
             share = BANK // width
@@ -323,9 +349,6 @@ def tile_list_crack_hedge_tilt_kernel(tc, tab_words, tab_scales, offs, pos1, pos
                 dst = out[P * group[0]:P * (group[-1] + 1), lo:hi].rearrange("(e p) m -> p e m", p=P)
                 nc.sync.dma_start(dst, tilt[:].rearrange("p (e m) -> p e m", e=len(group)))
 
-        for lo, hi in spans:
-            pick_x(LAST, lo, hi)
-            scaled_abs(LAST, lo, hi)
         for half in range(2):
             cols = slice(M // 2 * half, M // 2 * (half + 1))
             for n in range(N_TILES):

@@ -28,19 +28,18 @@ WINDOWS = TILES
 PIECES = [256, 128, 128]
 W2_EDGES = [0, 2 * P, 4 * P, 6 * P, H]
 
-Y_AHEAD = 3
+Y_AHEAD = 4
 P1_ON_VECTOR = (0, 4, 5)
 P2_SPLIT = 256
 FIRST_WIDTH = 256
 
 KB = 1024
-AT_W1_RAW = 0
-AT_Y_PICKED = 0
-AT_W1 = 20 * KB
-AT_X2_FIRST = 16 * KB
-AT_X_SECOND = 32 * KB
-AT_Z2 = 26 * KB
-AT_Z1 = 26 * KB
+AT_W1 = [8 * KB, 14 * KB]
+AT_Y_PICKED = 6 * KB
+AT_Z2 = 20 * KB
+AT_Z1 = 20 * KB
+AT_X2_FIRST = 10 * KB
+AT_X_SECOND = 26 * KB
 
 
 def tile_list_crack_hedge_tilt_kernel(tc, tab_words, tab_scales, offs, pos1, pos2, pos3, w1,
@@ -76,8 +75,7 @@ def tile_list_crack_hedge_tilt_kernel(tc, tab_words, tab_scales, offs, pos1, pos
         w2_cols = list(zip(W2_EDGES, W2_EDGES[1:]))
         w2_w = [held([P, 2 * 2 * (hi - lo)], U8, "w2_w%d" % lo) for lo, hi in w2_cols]
         w2_s = held([P, 2 * H], U8, "w2_s")
-        w1_raw = [[placed([P, PACK * PASS], F32, "w1_raw01", AT_W1_RAW) if (b, a) == (0, 1) else
-                   held([P, PACK * PASS], F32, "w1_raw%d%d" % (b, a)) for a in range(2)] for b in range(2)]
+        w1_raw = [[held([P, PACK * PASS], F32, "w1_raw%d%d" % (b, a)) for a in range(2)] for b in range(2)]
         w3_w = held([P, 2 * N], I32, "w3_w")
         w3_s = held([P, N], U8, "w3_s")
         cg_sb = held([P, TILES], F32, "cg_sb")
@@ -150,14 +148,13 @@ def tile_list_crack_hedge_tilt_kernel(tc, tab_words, tab_scales, offs, pos1, pos
 
         size = PACK * PASS
 
-        def round_on_vector(dst, b, a):
-            nc.vector.tensor_copy(dst.rearrange("p (t m j) -> p m j t", t=PACK, j=PACK),
-                                  w1_raw[b][a][:].rearrange("p (j m t) -> p m j t", t=PACK, j=PACK))
-
-        def round_on_gpsimd(dst, b, a):
-            nc.gpsimd.tensor_scalar(dst.rearrange("p (t m j) -> p m t j", t=PACK, j=PACK),
-                                    w1_raw[b][a][:].rearrange("p (j m t) -> p m t j", t=PACK, j=PACK),
-                                    1.0, 0.0, ALU.mult, ALU.add)
+        def round_w1(b):
+            group = placed([P, 2 * size], BF16, "w1_%d" % b, AT_W1[b])
+            for a in range(2):
+                nc.gpsimd.tensor_scalar(group[:, size * a:size * (a + 1)].rearrange("p (t m j) -> p m t j", t=PACK, j=PACK),
+                                        w1_raw[b][a][:].rearrange("p (j m t) -> p m t j", t=PACK, j=PACK),
+                                        1.0, 0.0, ALU.mult, ALU.add)
+            return group[:]
 
         def table_operand(cols, a):
             return dict(rhs=v_w[a][:, cols].bitcast(E4M3), rhs_scale=v_s[:, S * a + cols.start:S * a + cols.stop],
@@ -173,8 +170,8 @@ def tile_list_crack_hedge_tilt_kernel(tc, tab_words, tab_scales, offs, pos1, pos
 
         def x_pass(acc, i, cols, a):
             b, t = divmod(i, PACK)
-            codes, plane, first = w1_mx[b, a]
-            word = first + P * t
+            codes, plane = w1_mx[b]
+            word = PASS * a + P * t
             nc.tensor.matmul_mx(out=acc, lhsT=codes[:, word:word + P].bitcast(E4M3),
                                 lhsT_scale=plane[:, word:word + P], **table_operand(cols, a))
 
@@ -195,7 +192,7 @@ def tile_list_crack_hedge_tilt_kernel(tc, tab_words, tab_scales, offs, pos1, pos
             elif i == Y_AHEAD:
                 group = placed([P, M * (TILES - i)], BF16, "y_picked%d" % i, AT_Y_PICKED)
                 y_picked.extend(group[:, M * e:M * (e + 1)] for e in range(TILES - i))
-            pick(i == LAST, y_picked[i], y_win[i], pos3_sb[:])
+            pick(False, y_picked[i], y_win[i], pos3_sb[:])
             nc.sync.dma_start(z2_rows[b][32 * quarter:32 * (quarter + 1), :].bitcast(I32).rearrange("p (j c) -> p j c", j=PACK),
                               y_picked[i].bitcast(I32))
 
@@ -220,17 +217,11 @@ def tile_list_crack_hedge_tilt_kernel(tc, tab_words, tab_scales, offs, pos1, pos
         for i in range(2, TILES):
             y_win.append(fill_window(i - 2, y_pass, i))
 
-        w1_mx = {}
-        w1_first = [held([P, size], BF16, "w1_00"), placed([P, size], BF16, "w1_01", AT_W1)]
-        round_on_gpsimd(w1_first[0][:], 0, 0)
+        w1_first = round_w1(0)
         for i in range(Y_AHEAD):
             pick_y(i)
-        round_on_vector(w1_first[1][:], 0, 1)
-        for a in range(2):
-            w1_mx[0, a] = quantize("w1_0%d" % a, w1_first[a][:]) + (0,)
-        w1_second = placed([P, 2 * size], BF16, "w1_1", AT_W1)
-        for a in range(2):
-            round_on_gpsimd(w1_second[:, size * a:size * (a + 1)], 1, a)
+        w1_mx = [quantize("w1_0", w1_first)]
+        w1_second = round_w1(1)
         for i in range(Y_AHEAD, TILES):
             pick_y(i)
 
@@ -280,9 +271,7 @@ def tile_list_crack_hedge_tilt_kernel(tc, tab_words, tab_scales, offs, pos1, pos
         x_win = [x_window(i) for i in range(PACK)]
         x_picked = [picked_tile(0)]
         pick_p1(0, 0, M)
-        codes, plane = quantize("w1_1", w1_second[:])
-        for a in range(2):
-            w1_mx[1, a] = (codes, plane, PASS * a)
+        w1_mx.append(quantize("w1_1", w1_second))
         z2_woven = weave_z2()
         for i in range(1, PACK):
             pick_p1(i, 0, M)

@@ -24,12 +24,13 @@ BANKS = 8
 TILES = H // P
 N_TILES = N // P
 LAST = TILES - 1
+QUADRANTS = (0, 2, 1, 3)
 WINDOWS = TILES
 PIECES = [256, 128, 128]
 W2_EDGES = [0, 2 * P, 4 * P, 6 * P, H]
 
 Y_AHEAD = 4
-P1_ON_VECTOR = (0, 4, 5)
+P1_ON_VECTOR = (0, 4)
 P2_SPLIT = 256
 FIRST_WIDTH = 256
 
@@ -76,7 +77,6 @@ def tile_list_crack_hedge_tilt_kernel(tc, tab_words, tab_scales, offs, pos1, pos
         w2_w = [held([P, 2 * 2 * (hi - lo)], U8, "w2_w%d" % lo) for lo, hi in w2_cols]
         w2_s = held([P, 2 * H], U8, "w2_s")
         w1_raw = [[held([P, PACK * PASS], F32, "w1_raw%d%d" % (b, a)) for a in range(2)] for b in range(2)]
-        w3_w = held([P, 2 * N], I32, "w3_w")
         w3_s = held([P, N], U8, "w3_s")
         cg_sb = held([P, TILES], F32, "cg_sb")
         cg_step = held([P, TILES], F32, "cg_step")
@@ -105,12 +105,12 @@ def tile_list_crack_hedge_tilt_kernel(tc, tab_words, tab_scales, offs, pos1, pos
         nc.sync.dma_start(tab_s[0:32, :].bitcast(I32), tab_scales.bitcast(I32).rearrange("a s c -> s a c"))
         load_words(0)
         load_w2(nc.scalar, 0)
-        for q in range(4):
+        for q in QUADRANTS:
             nc.scalar.dma_start(w2_s[32 * q:32 * q + 4, :].bitcast(I32).rearrange("p (a c) -> p a c", a=2),
                                 w2_scales[:, 4 * q:4 * q + 4, :].bitcast(I32).rearrange("a s c -> s a c"))
         load_words(1)
         nc.vector.tensor_copy(gathered_s[:], tab_s[:].indirect(offs_sb[:]))
-        for q in range(4):
+        for q in QUADRANTS:
             nc.sync.dma_start(v_s[32 * q:32 * q + 4, :].bitcast(I32).rearrange("p (a c) -> p a c", a=2),
                               gathered_s[8 * q:8 * q + 8, :].bitcast(I32))
         load_w2(nc.sync, 1)
@@ -225,9 +225,10 @@ def tile_list_crack_hedge_tilt_kernel(tc, tab_words, tab_scales, offs, pos1, pos
         for i in range(Y_AHEAD, TILES):
             pick_y(i)
 
+        w3_w = placed([P, 2 * N], I32, "w3_w", AT_Y_PICKED)
         nc.sync.dma_start(w3_w[:].rearrange("p (a c) -> p a c", a=2),
                           w3_words.rearrange("a p c i -> p a (c i)").bitcast(I32))
-        for q in range(4):
+        for q in QUADRANTS:
             nc.sync.dma_start(w3_s[32 * q:32 * q + 8, :].bitcast(I32), w3_scales[:, 4 * q:4 * q + 4, :].bitcast(I32))
         with nc.allow_non_contiguous_dma(reason="one ratio for each partition"):
             nc.sync.dma_start(rl_sb[:], rl.rearrange("(n p) -> p n", p=P))

@@ -27,20 +27,22 @@ LAST = TILES - 1
 QUADRANTS = (0, 2, 1, 3)
 WINDOWS = TILES
 PIECES = [256, 128, 128]
-W2_EDGES = [0, 2 * P, 4 * P, 6 * P, H]
+W2_EDGES = [0, 4 * P, 6 * P, H]
 
-Y_AHEAD = 4
-P1_ON_VECTOR = (0, 4)
+Y_AHEAD = 5
+P1_ON_VECTOR = (0, 1, 4)
 P2_SPLIT = 256
 FIRST_WIDTH = 256
 
 KB = 1024
-AT_W1 = [8 * KB, 14 * KB]
-AT_Y_PICKED = 6 * KB
-AT_Z2 = 20 * KB
-AT_Z1 = 20 * KB
-AT_X2_FIRST = 10 * KB
-AT_X_SECOND = 26 * KB
+AT_W1_RAW = [0, 8 * KB]
+AT_Z2_ROWS = 40 * KB
+AT_W1 = [[24 * KB, 28 * KB], [30 * KB, 26 * KB]]
+AT_Y_PICKED = 23 * KB
+AT_X2_FIRST = 32 * KB
+AT_Z2 = [24 * KB, 28 * KB]
+AT_X_SECOND = 10 * KB
+AT_Z1 = 28 * KB
 
 
 def tile_list_crack_hedge_tilt_kernel(tc, tab_words, tab_scales, offs, pos1, pos2, pos3, w1,
@@ -75,19 +77,21 @@ def tile_list_crack_hedge_tilt_kernel(tc, tab_words, tab_scales, offs, pos1, pos
         v_s = held([P, 2 * S], U8, "v_s")
         w2_cols = list(zip(W2_EDGES, W2_EDGES[1:]))
         w2_w = [held([P, 2 * 2 * (hi - lo)], U8, "w2_w%d" % lo) for lo, hi in w2_cols]
-        w2_s = held([P, 2 * H], U8, "w2_s")
-        w1_raw = [[held([P, PACK * PASS], F32, "w1_raw%d%d" % (b, a)) for a in range(2)] for b in range(2)]
+        w2_s = [held([P, H], U8, "w2_s%d" % b) for b in range(2)]
+        w1_raw = [[held([P, PACK * PASS], F32, "w1_raw%d0" % b), placed([P, PACK * PASS], F32, "w1_raw%d1" % b, AT_W1_RAW[b])]
+                  for b in range(2)]
         w3_s = held([P, N], U8, "w3_s")
         cg_sb = held([P, TILES], F32, "cg_sb")
         cg_step = held([P, TILES], F32, "cg_step")
         cg_sign = held([P, TILES], F32, "cg_sign")
         rl_sb = held([P, N_TILES], F32, "rl_sb")
 
-        nc.gpsimd.memset(w2_s[:].bitcast(I32), 0)
+        nc.vector.memset(w2_s[0][:].bitcast(I32), 0)
         nc.vector.memset(tab_s[32:64, :].bitcast(I32), 0)
         nc.vector.memset(tab_s[64:128, :].bitcast(I32), 0)
-        nc.gpsimd.memset(v_s[:].bitcast(I32), 0)
-        nc.gpsimd.memset(w3_s[:].bitcast(I32), 0)
+        nc.vector.memset(v_s[:].bitcast(I32), 0)
+        nc.vector.memset(w2_s[1][:].bitcast(I32), 0)
+        nc.vector.memset(w3_s[:].bitcast(I32), 0)
 
         def load_words(a):
             nc.sync.dma_start(tab_w[a][:], tab_words[a].rearrange("p t i -> p (t i)").bitcast(I32))
@@ -101,25 +105,28 @@ def tile_list_crack_hedge_tilt_kernel(tc, tab_words, tab_scales, offs, pos1, pos
             queue.dma_start(w2_w[part][:].bitcast(I32).rearrange("p (a c) -> p a c", a=2),
                             w2_words[:, :, 2 * lo:2 * hi].bitcast(I32).rearrange("a p c -> p a c"))
 
+        def load_w2_scales(queue, b):
+            for q in QUADRANTS:
+                queue.dma_start(w2_s[b][32 * q:32 * q + 4, :].bitcast(I32).rearrange("p (a c) -> p a c", a=2),
+                                w2_scales[:, 4 * q:4 * q + 4, PASS * b:PASS * (b + 1)].bitcast(I32).rearrange("a s c -> s a c"))
+
         nc.sync.dma_start(offs_sb[:], offs)
         nc.sync.dma_start(tab_s[0:32, :].bitcast(I32), tab_scales.bitcast(I32).rearrange("a s c -> s a c"))
         load_words(0)
-        load_w2(nc.scalar, 0)
-        for q in QUADRANTS:
-            nc.scalar.dma_start(w2_s[32 * q:32 * q + 4, :].bitcast(I32).rearrange("p (a c) -> p a c", a=2),
-                                w2_scales[:, 4 * q:4 * q + 4, :].bitcast(I32).rearrange("a s c -> s a c"))
+        nc.sync.dma_start(pos3_sb[:], pos3)
         load_words(1)
+        load_w2_scales(nc.scalar, 0)
+        load_w2(nc.sync, 0)
         nc.vector.tensor_copy(gathered_s[:], tab_s[:].indirect(offs_sb[:]))
         for q in QUADRANTS:
             nc.sync.dma_start(v_s[32 * q:32 * q + 4, :].bitcast(I32).rearrange("p (a c) -> p a c", a=2),
                               gathered_s[8 * q:8 * q + 8, :].bitcast(I32))
-        load_w2(nc.sync, 1)
-        nc.sync.dma_start(pos3_sb[:], pos3)
         load_w1(0, 0)
+        load_w2_scales(nc.sync, 1)
+        load_w2(nc.sync, 1)
         nc.sync.dma_start(cg_sb[:].rearrange("p (b t) -> p b t", b=2), cg.rearrange("(b p t) -> p b t", b=2, t=PACK))
-        load_w2(nc.sync, 2)
         load_w1(0, 1)
-        load_w2(nc.sync, 3)
+        load_w2(nc.sync, 2)
         load_w1(1, 0)
         load_w1(1, 1)
         nc.sync.dma_start(pos1_sb[:], pos1)
@@ -139,9 +146,9 @@ def tile_list_crack_hedge_tilt_kernel(tc, tab_words, tab_scales, offs, pos1, pos
             else:
                 nc.vector.tensor_copy(dst, win[:].indirect(places))
 
-        def quantize(name, values):
+        def quantize(name, values, offset=None):
             width = values.shape[1] // PACK
-            codes = held([P, width], U32, name + "_w")
+            codes = held([P, width], U32, name + "_w") if offset is None else placed([P, width], U32, name + "_w", offset)
             plane = held([P, width], U8, name + "_s")
             nc.vector.quantize_mx(out=codes[:].bitcast(E4M3), scales=plane[:], in_=values)
             return codes, plane
@@ -149,12 +156,15 @@ def tile_list_crack_hedge_tilt_kernel(tc, tab_words, tab_scales, offs, pos1, pos
         size = PACK * PASS
 
         def round_w1(b):
-            group = placed([P, 2 * size], BF16, "w1_%d" % b, AT_W1[b])
+            parts = [placed([P, size], BF16, "w1_%d%d" % (b, a), AT_W1[b][a]) for a in range(2)]
             for a in range(2):
-                nc.gpsimd.tensor_scalar(group[:, size * a:size * (a + 1)].rearrange("p (t m j) -> p m t j", t=PACK, j=PACK),
-                                        w1_raw[b][a][:].rearrange("p (j m t) -> p m t j", t=PACK, j=PACK),
+                nc.gpsimd.tensor_scalar(parts[a][:].rearrange("p (t m j) -> p m j t", t=PACK, j=PACK),
+                                        w1_raw[b][a][:].rearrange("p (j m t) -> p m j t", t=PACK, j=PACK),
                                         1.0, 0.0, ALU.mult, ALU.add)
-            return group[:]
+            return parts
+
+        def quantize_pair(name, pair, offset):
+            return [quantize(name + "0", pair[0][:], offset), quantize(name + "1", pair[1][:])]
 
         def table_operand(cols, a):
             return dict(rhs=v_w[a][:, cols].bitcast(E4M3), rhs_scale=v_s[:, S * a + cols.start:S * a + cols.stop],
@@ -164,14 +174,15 @@ def tile_list_crack_hedge_tilt_kernel(tc, tab_words, tab_scales, offs, pos1, pos
             part = sum(1 for edge in W2_EDGES[1:] if edge <= P * i)
             lo, hi = w2_cols[part]
             word = (hi - lo) * a + P * i - lo
-            byte = H * a + P * i
+            b, t = divmod(i, PACK)
+            byte = PASS * a + P * t
             nc.tensor.matmul_mx(out=acc, lhsT=w2_w[part][:, 2 * word:2 * (word + P)].bitcast(E2M1),
-                                lhsT_scale=w2_s[:, byte:byte + P], **table_operand(cols, a))
+                                lhsT_scale=w2_s[b][:, byte:byte + P], **table_operand(cols, a))
 
         def x_pass(acc, i, cols, a):
             b, t = divmod(i, PACK)
-            codes, plane = w1_mx[b]
-            word = PASS * a + P * t
+            codes, plane = w1_mx[b][a]
+            word = P * t
             nc.tensor.matmul_mx(out=acc, lhsT=codes[:, word:word + P].bitcast(E4M3),
                                 lhsT_scale=plane[:, word:word + P], **table_operand(cols, a))
 
@@ -181,18 +192,18 @@ def tile_list_crack_hedge_tilt_kernel(tc, tab_words, tab_scales, offs, pos1, pos
             nc.tensor.matmul_mx(out=acc, lhsT=w3_w[:, word:word + P].bitcast(E4M3), lhsT_scale=w3_s[4 * b:, P * n:P * (n + 1)],
                                 rhs=codes[:, cols].bitcast(E4M3), rhs_scale=plane[:, cols], start=start, stop=stop)
 
-        z2_rows = [held([P, PACK * M], BF16, "z2_rows%d" % b) for b in range(2)]
+        z2_rows = [held([P, PACK * M], BF16, "z2_rows0"), placed([P, PACK * M], BF16, "z2_rows1", AT_Z2_ROWS)]
 
         y_picked = []
 
         def pick_y(i):
             b, quarter = divmod(i, PACK)
-            if i < Y_AHEAD:
+            if i < Y_AHEAD or i == LAST:
                 y_picked.append(held([P, M], BF16, "y_picked%d" % i)[:])
             elif i == Y_AHEAD:
-                group = placed([P, M * (TILES - i)], BF16, "y_picked%d" % i, AT_Y_PICKED)
-                y_picked.extend(group[:, M * e:M * (e + 1)] for e in range(TILES - i))
-            pick(False, y_picked[i], y_win[i], pos3_sb[:])
+                group = placed([P, M * (LAST - i)], BF16, "y_picked%d" % i, AT_Y_PICKED)
+                y_picked.extend(group[:, M * e:M * (e + 1)] for e in range(LAST - i))
+            pick(i == LAST, y_picked[i], y_win[i], pos3_sb[:])
             nc.sync.dma_start(z2_rows[b][32 * quarter:32 * (quarter + 1), :].bitcast(I32).rearrange("p (j c) -> p j c", j=PACK),
                               y_picked[i].bitcast(I32))
 
@@ -220,12 +231,12 @@ def tile_list_crack_hedge_tilt_kernel(tc, tab_words, tab_scales, offs, pos1, pos
         w1_first = round_w1(0)
         for i in range(Y_AHEAD):
             pick_y(i)
-        w1_mx = [quantize("w1_0", w1_first)]
+        w1_mx = [quantize_pair("w1_0", w1_first, AT_W1_RAW[0])]
         w1_second = round_w1(1)
         for i in range(Y_AHEAD, TILES):
             pick_y(i)
 
-        w3_w = placed([P, 2 * N], I32, "w3_w", AT_Y_PICKED)
+        w3_w = held([P, 2 * N], I32, "w3_w")
         nc.sync.dma_start(w3_w[:].rearrange("p (a c) -> p a c", a=2),
                           w3_words.rearrange("a p c i -> p a (c i)").bitcast(I32))
         for q in QUADRANTS:
@@ -263,25 +274,27 @@ def tile_list_crack_hedge_tilt_kernel(tc, tab_words, tab_scales, offs, pos1, pos
             return dst
 
         def weave_z2():
-            both = placed([P, 2 * PACK * M], BF16, "z2_woven", AT_Z2)
+            halves = [placed([P, PACK * M], BF16, "z2_woven%d" % b, AT_Z2[b]) for b in range(2)]
             for b in range(2):
-                nc.gpsimd.tensor_scalar(both[:, PACK * M * b:PACK * M * (b + 1)].rearrange("p (m t) -> p m t", t=PACK),
+                nc.gpsimd.tensor_scalar(halves[b][:].rearrange("p (m t) -> p m t", t=PACK),
                                         z2_rows[b][:].rearrange("p (t m) -> p m t", t=PACK), 1.0, 0.0, ALU.mult, ALU.add)
-            return both[:]
+            return halves
 
         x_win = [x_window(i) for i in range(PACK)]
         x_picked = [picked_tile(0)]
-        pick_p1(0, 0, M)
-        w1_mx.append(quantize("w1_1", w1_second))
-        z2_woven = weave_z2()
-        for i in range(1, PACK):
+        for i in range(2):
             pick_p1(i, 0, M)
-            scaled_abs(i - 1, 0, M)
+        w1_mx.append(quantize_pair("w1_1", w1_second, AT_W1_RAW[1]))
+        z2_woven = weave_z2()
+        for i in range(2, PACK):
+            pick_p1(i, 0, M)
+        for i in range(PACK - 1):
+            scaled_abs(i, 0, M)
         x_win.append(x_window(PACK))
         scaled_abs(PACK - 1, 0, M)
         for i in range(PACK):
             pick_p2(i, 0, M)
-        z2 = quantize("z2", z2_woven)
+        z2 = quantize_pair("z2_", z2_woven, AT_Z2_ROWS)
         z1_rounded = form_z1(nc.gpsimd, placed([P, PACK * M], BF16, "z1_first", AT_Z1)[:], 0, 0, M)
         x_picked.append(picked_tile(1))
         for i in range(PACK, LAST):
@@ -299,24 +312,28 @@ def tile_list_crack_hedge_tilt_kernel(tc, tab_words, tab_scales, offs, pos1, pos
         for n in range(N_TILES):
             o2_banks.append(bank(n))
             for b in range(2):
-                o_pass(o2_banks[n][:], n, b, z2, slice(M * b, M * (b + 1)), b == 0, b == 1)
+                o_pass(o2_banks[n][:], n, b, z2[b], slice(0, M), b == 0, b == 1)
 
         for lo, hi in spans:
             pick_p1(LAST, lo, hi)
             pick_p2(LAST, lo, hi)
             scaled_abs(LAST, lo, hi)
-        z1_first = quantize("z1_0", z1_rounded)
-
         o1 = []
         free_banks = list(range(N_TILES, BANKS))
-        for lo, hi in spans:
-            width = hi - lo
-            share = BANK // width
-            banks = [bank(free_banks.pop(0)) for g in range(N_TILES // share)]
-            o1.append([banks[n // share][:, width * (n % share):width * (n % share + 1)] for n in range(N_TILES)])
-            for n in range(N_TILES):
-                o_pass(o1[-1][n], n, 0, z1_first, slice(lo, hi), n % share == 0, False)
 
+        def open_o1(pieces):
+            first, last = spans[pieces[0]][0], spans[pieces[-1]][1]
+            z1_first = quantize("z1_0%d" % pieces[0], z1_rounded[:, PACK * first:PACK * last])
+            for u in pieces:
+                lo, hi = spans[u]
+                width = hi - lo
+                share = BANK // width
+                banks = [bank(free_banks.pop(0)) for g in range(N_TILES // share)]
+                o1.append([banks[n // share][:, width * (n % share):width * (n % share + 1)] for n in range(N_TILES)])
+                for n in range(N_TILES):
+                    o_pass(o1[u][n], n, 0, z1_first, slice(lo - first, hi - first), n % share == 0, False)
+
+        open_o1([0])
         o2 = [held([P, M], F32, "o2_%d" % n) for n in range(N_TILES)]
 
         def close_o1(u):
@@ -349,5 +366,7 @@ def tile_list_crack_hedge_tilt_kernel(tc, tab_words, tab_scales, offs, pos1, pos
                 z1_second.append(form_z1(nc.vector, held([P, PACK * PIECES[s]], BF16, "z1_second%d" % s)[:], 1, *spans[s]))
             if 0 <= s - 1 < len(PIECES):
                 close_o1(s - 1)
+            if s == 1:
+                open_o1([1, 2])
             if 0 <= s - 2 < len(PIECES):
                 finish(s - 2)

@@ -27,21 +27,20 @@ LAST = TILES - 1
 QUADRANTS = (0, 2, 1, 3)
 WINDOWS = TILES
 PIECES = [256, 128, 128]
-W2_EDGES = [0, 4 * P, 6 * P, H]
+W2_EDGES = [0, 4 * P, H]
 
-Y_AHEAD = 5
+Y_AHEAD = 4
 P1_ON_VECTOR = (0, 1, 4)
 P2_SPLIT = 256
 FIRST_WIDTH = 256
 
 KB = 1024
 AT_W1_RAW = [0, 8 * KB]
-AT_Z2_ROWS = 40 * KB
+AT_Z2_ROWS = 48 * KB
 AT_W1 = [[24 * KB, 28 * KB], [30 * KB, 26 * KB]]
-AT_Y_PICKED = 23 * KB
-AT_X2_FIRST = 32 * KB
+AT_Y_PICKED = 22 * KB
 AT_Z2 = [24 * KB, 28 * KB]
-AT_X_SECOND = 10 * KB
+AT_X = [32 * KB, 10 * KB]
 AT_Z1 = 28 * KB
 
 
@@ -89,9 +88,9 @@ def tile_list_crack_hedge_tilt_kernel(tc, tab_words, tab_scales, offs, pos1, pos
         nc.vector.memset(w2_s[0][:].bitcast(I32), 0)
         nc.vector.memset(tab_s[32:64, :].bitcast(I32), 0)
         nc.vector.memset(tab_s[64:128, :].bitcast(I32), 0)
-        nc.vector.memset(v_s[:].bitcast(I32), 0)
-        nc.vector.memset(w2_s[1][:].bitcast(I32), 0)
-        nc.vector.memset(w3_s[:].bitcast(I32), 0)
+        nc.gpsimd.memset(v_s[:].bitcast(I32), 0)
+        nc.gpsimd.memset(w2_s[1][:].bitcast(I32), 0)
+        nc.gpsimd.memset(w3_s[:].bitcast(I32), 0)
 
         def load_words(a):
             nc.sync.dma_start(tab_w[a][:], tab_words[a].rearrange("p t i -> p (t i)").bitcast(I32))
@@ -122,11 +121,10 @@ def tile_list_crack_hedge_tilt_kernel(tc, tab_words, tab_scales, offs, pos1, pos
             nc.sync.dma_start(v_s[32 * q:32 * q + 4, :].bitcast(I32).rearrange("p (a c) -> p a c", a=2),
                               gathered_s[8 * q:8 * q + 8, :].bitcast(I32))
         load_w1(0, 0)
-        load_w2_scales(nc.sync, 1)
-        load_w2(nc.sync, 1)
         nc.sync.dma_start(cg_sb[:].rearrange("p (b t) -> p b t", b=2), cg.rearrange("(b p t) -> p b t", b=2, t=PACK))
         load_w1(0, 1)
-        load_w2(nc.sync, 2)
+        load_w2_scales(nc.sync, 1)
+        load_w2(nc.sync, 1)
         load_w1(1, 0)
         load_w1(1, 1)
         nc.sync.dma_start(pos1_sb[:], pos1)
@@ -158,8 +156,8 @@ def tile_list_crack_hedge_tilt_kernel(tc, tab_words, tab_scales, offs, pos1, pos
         def round_w1(b):
             parts = [placed([P, size], BF16, "w1_%d%d" % (b, a), AT_W1[b][a]) for a in range(2)]
             for a in range(2):
-                nc.gpsimd.tensor_scalar(parts[a][:].rearrange("p (t m j) -> p m j t", t=PACK, j=PACK),
-                                        w1_raw[b][a][:].rearrange("p (j m t) -> p m j t", t=PACK, j=PACK),
+                nc.gpsimd.tensor_scalar(parts[a][:].rearrange("p (t m j) -> p m t j", t=PACK, j=PACK),
+                                        w1_raw[b][a][:].rearrange("p (j m t) -> p m t j", t=PACK, j=PACK),
                                         1.0, 0.0, ALU.mult, ALU.add)
             return parts
 
@@ -220,11 +218,11 @@ def tile_list_crack_hedge_tilt_kernel(tc, tab_words, tab_scales, offs, pos1, pos
         first_cols = [slice(lo, lo + FIRST_WIDTH) for lo in range(0, S, FIRST_WIDTH)]
         first_banks = [[bank(2 * q + i) for i in range(2)] for q in range(len(first_cols))]
         y_win = [window() for i in range(2)]
-        for q, cols in enumerate(first_cols):
-            for i in range(2):
-                for a in range(2):
-                    y_pass(first_banks[q][i][:, 0:FIRST_WIDTH], i, cols, a)
-                nc.scalar.copy(y_win[i][:, cols], first_banks[q][i][:, 0:FIRST_WIDTH])
+        for i, q in [(0, 0), (0, 1), (0, 2), (1, 0), (0, 3), (1, 1), (1, 2), (1, 3)]:
+            cols = first_cols[q]
+            for a in range(2):
+                y_pass(first_banks[q][i][:, 0:FIRST_WIDTH], i, cols, a)
+            nc.scalar.copy(y_win[i][:, cols], first_banks[q][i][:, 0:FIRST_WIDTH])
         for i in range(2, TILES):
             y_win.append(fill_window(i - 2, y_pass, i))
 
@@ -244,10 +242,10 @@ def tile_list_crack_hedge_tilt_kernel(tc, tab_words, tab_scales, offs, pos1, pos
         with nc.allow_non_contiguous_dma(reason="one ratio for each partition"):
             nc.sync.dma_start(rl_sb[:], rl.rearrange("(n p) -> p n", p=P))
 
+        p1_raw = {(0, 0): held([P, M], F32, "p1_raw")[:]}
+
         def picked_tile(b):
-            if b == 0:
-                return held([P, PACK * M], F32, "x1_first")[:], placed([P, PACK * M], F32, "x2_first", AT_X2_FIRST)[:]
-            both = placed([P, 2 * PACK * M], F32, "x_second", AT_X_SECOND)
+            both = placed([P, 2 * PACK * M], F32, "x_picked%d" % b, AT_X[b])
             return both[:, 0:PACK * M], both[:, PACK * M:2 * PACK * M]
 
         def x_window(i):
@@ -255,7 +253,8 @@ def tile_list_crack_hedge_tilt_kernel(tc, tab_words, tab_scales, offs, pos1, pos
 
         def pick_p1(i, lo, hi):
             b, t = divmod(i, PACK)
-            pick(i not in P1_ON_VECTOR, x_picked[b][0][:, M * t + lo:M * t + hi], x_win[i], pos1_sb[:, lo // 16:hi // 16])
+            dst = p1_raw.setdefault((i, lo), x_picked[b][0][:, M * t + lo:M * t + hi])
+            pick(i not in P1_ON_VECTOR and (i, lo) != (LAST, 0), dst, x_win[i], pos1_sb[:, lo // 16:hi // 16])
 
         def pick_p2(i, lo, hi):
             b, t = divmod(i, PACK)
@@ -263,8 +262,7 @@ def tile_list_crack_hedge_tilt_kernel(tc, tab_words, tab_scales, offs, pos1, pos
 
         def scaled_abs(i, lo, hi):
             b, t = divmod(i, PACK)
-            values = x_picked[b][0][:, M * t + lo:M * t + hi]
-            nc.scalar.activation(values, values, ACT.Abs, scale=cg_sb[:, i:i + 1])
+            nc.scalar.activation(x_picked[b][0][:, M * t + lo:M * t + hi], p1_raw[i, lo], ACT.Abs, scale=cg_sb[:, i:i + 1])
 
         def form_z1(engine, dst, b, lo, hi):
             def walk(tiles):
@@ -282,16 +280,14 @@ def tile_list_crack_hedge_tilt_kernel(tc, tab_words, tab_scales, offs, pos1, pos
 
         x_win = [x_window(i) for i in range(PACK)]
         x_picked = [picked_tile(0)]
-        for i in range(2):
-            pick_p1(i, 0, M)
+        pick_p1(0, 0, M)
         w1_mx.append(quantize_pair("w1_1", w1_second, AT_W1_RAW[1]))
         z2_woven = weave_z2()
-        for i in range(2, PACK):
+        for i in range(1, PACK):
             pick_p1(i, 0, M)
-        for i in range(PACK - 1):
+        for i in range(PACK):
             scaled_abs(i, 0, M)
         x_win.append(x_window(PACK))
-        scaled_abs(PACK - 1, 0, M)
         for i in range(PACK):
             pick_p2(i, 0, M)
         z2 = quantize_pair("z2_", z2_woven, AT_Z2_ROWS)
@@ -308,13 +304,18 @@ def tile_list_crack_hedge_tilt_kernel(tc, tab_words, tab_scales, offs, pos1, pos
         edges = [sum(PIECES[:u]) for u in range(len(PIECES) + 1)]
         spans = list(zip(edges, edges[1:]))
 
+        half = M // 2
+        halves = [(0, half), (half, M)]
         o2_banks = []
-        for n in range(N_TILES):
-            o2_banks.append(bank(n))
-            for b in range(2):
-                o_pass(o2_banks[n][:], n, b, z2[b], slice(0, M), b == 0, b == 1)
+        for g in range(N_TILES):
+            h, pair = divmod(g, 2)
+            o2_banks.append(bank(g))
+            for e in range(2):
+                for b in range(2):
+                    o_pass(o2_banks[g][:, half * e:half * (e + 1)], 2 * pair + e, b, z2[b], slice(*halves[h]),
+                           e + b == 0, e + b == 2)
 
-        for lo, hi in spans:
+        for lo, hi in halves:
             pick_p1(LAST, lo, hi)
             pick_p2(LAST, lo, hi)
             scaled_abs(LAST, lo, hi)
@@ -334,7 +335,12 @@ def tile_list_crack_hedge_tilt_kernel(tc, tab_words, tab_scales, offs, pos1, pos
                     o_pass(o1[u][n], n, 0, z1_first, slice(lo - first, hi - first), n % share == 0, False)
 
         open_o1([0])
-        o2 = [held([P, M], F32, "o2_%d" % n) for n in range(N_TILES)]
+        o2 = [held([P, BANK], F32, "o2_%d" % g) for g in range(N_TILES)]
+
+        def o2_part(n, lo, hi):
+            h = lo // half
+            first = half * (n % 2) + lo - half * h
+            return o2[2 * h + n // 2][:, first:first + hi - lo]
 
         def close_o1(u):
             lo, hi = spans[u]
@@ -351,15 +357,13 @@ def tile_list_crack_hedge_tilt_kernel(tc, tab_words, tab_scales, offs, pos1, pos
                 tilt = held([P, len(group) * width], F32, "tilt%d%d" % (u, group[0]))
                 for e, n in enumerate(group):
                     nc.vector.scalar_tensor_tensor(tilt[:, width * e:width * (e + 1)], o1[u][n], rl_sb[:, n:n + 1],
-                                                   o2[n][:, lo:hi], ALU.mult, ALU.subtract)
+                                                   o2_part(n, lo, hi), ALU.mult, ALU.subtract)
                 nc.scalar.activation(tilt[:], tilt[:], ACT.Tanh)
                 dst = out[P * group[0]:P * (group[-1] + 1), lo:hi].rearrange("(e p) m -> p e m", p=P)
                 nc.sync.dma_start(dst, tilt[:].rearrange("p (e m) -> p e m", e=len(group)))
 
-        for half in range(2):
-            cols = slice(M // 2 * half, M // 2 * (half + 1))
-            for n in range(N_TILES):
-                nc.scalar.copy(o2[n][:, cols], o2_banks[n][:, cols])
+        for g in range(N_TILES):
+            nc.scalar.copy(o2[g][:], o2_banks[g][:])
         z1_second = []
         for s in range(len(PIECES) + 2):
             if s < len(PIECES):

@@ -76,55 +76,54 @@ def tile_list_crack_hedge_tilt_kernel(tc, tab_words, tab_scales, offs, pos1, pos
         v_s = held([P, 2 * S], U8, "v_s")
         w2_cols = list(zip(W2_EDGES, W2_EDGES[1:]))
         w2_w = [held([P, 2 * 2 * (hi - lo)], U8, "w2_w%d" % lo) for lo, hi in w2_cols]
-        w2_s = [held([P, H], U8, "w2_s%d" % b) for b in range(2)]
-        w1_raw = [[held([P, PACK * PASS], F32, "w1_raw%d0" % b), placed([P, PACK * PASS], F32, "w1_raw%d1" % b, AT_W1_RAW[b])]
-                  for b in range(2)]
+        w2_s = held([P, 2 * H], U8, "w2_s")
         w3_s = held([P, N], U8, "w3_s")
         cg_sb = held([P, TILES], F32, "cg_sb")
         cg_step = held([P, TILES], F32, "cg_step")
         cg_sign = held([P, TILES], F32, "cg_sign")
         rl_sb = held([P, N_TILES], F32, "rl_sb")
 
-        nc.vector.memset(w2_s[0][:].bitcast(I32), 0)
+        nc.vector.memset(w2_s[:].bitcast(I32), 0)
         nc.vector.memset(tab_s[32:64, :].bitcast(I32), 0)
         nc.vector.memset(tab_s[64:128, :].bitcast(I32), 0)
-        nc.gpsimd.memset(v_s[:].bitcast(I32), 0)
-        nc.gpsimd.memset(w2_s[1][:].bitcast(I32), 0)
-        nc.gpsimd.memset(w3_s[:].bitcast(I32), 0)
+        nc.vector.memset(v_s[:].bitcast(I32), 0)
+        nc.vector.memset(w3_s[:].bitcast(I32), 0)
 
         def load_words(a):
             nc.sync.dma_start(tab_w[a][:], tab_words[a].rearrange("p t i -> p (t i)").bitcast(I32))
 
-        def load_w1(b, a):
-            src = w1[PASS * a:PASS * (a + 1), PASS * b:PASS * (b + 1)].rearrange("(p j) c -> p j c", j=PACK)
-            nc.sync.dma_start(w1_raw[b][a][:].rearrange("p (j c) -> p j c", j=PACK), src)
+        w1_raw = [[], []]
 
-        def load_w2(queue, part):
+        def load_w1(b, a, lo=0, hi=PASS):
+            shape, name = [P, PACK * (hi - lo)], "w1_raw%d%d_%d" % (b, a, lo)
+            raw = placed(shape, F32, name, AT_W1_RAW[b]) if (a, hi) == (1, PASS) else held(shape, F32, name)
+            src = w1[PASS * a:PASS * (a + 1), PASS * b + lo:PASS * b + hi].rearrange("(p j) c -> p j c", j=PACK)
+            nc.sync.dma_start(raw[:].rearrange("p (j c) -> p j c", j=PACK), src)
+            w1_raw[b].append((a, lo, raw))
+
+        def load_w2(part):
             lo, hi = w2_cols[part]
-            queue.dma_start(w2_w[part][:].bitcast(I32).rearrange("p (a c) -> p a c", a=2),
-                            w2_words[:, :, 2 * lo:2 * hi].bitcast(I32).rearrange("a p c -> p a c"))
-
-        def load_w2_scales(queue, b):
-            for q in QUADRANTS:
-                queue.dma_start(w2_s[b][32 * q:32 * q + 4, :].bitcast(I32).rearrange("p (a c) -> p a c", a=2),
-                                w2_scales[:, 4 * q:4 * q + 4, PASS * b:PASS * (b + 1)].bitcast(I32).rearrange("a s c -> s a c"))
+            nc.sync.dma_start(w2_w[part][:].bitcast(I32).rearrange("p (a c) -> p a c", a=2),
+                              w2_words[:, :, 2 * lo:2 * hi].bitcast(I32).rearrange("a p c -> p a c"))
 
         nc.sync.dma_start(offs_sb[:], offs)
         nc.sync.dma_start(tab_s[0:32, :].bitcast(I32), tab_scales.bitcast(I32).rearrange("a s c -> s a c"))
         load_words(0)
         nc.sync.dma_start(pos3_sb[:], pos3)
         load_words(1)
-        load_w2_scales(nc.scalar, 0)
-        load_w2(nc.sync, 0)
+        for q in QUADRANTS:
+            nc.scalar.dma_start(w2_s[32 * q:32 * q + 4, :].bitcast(I32).rearrange("p (a c) -> p a c", a=2),
+                                w2_scales[:, 4 * q:4 * q + 4, :].bitcast(I32).rearrange("a s c -> s a c"))
+        load_w2(0)
         nc.vector.tensor_copy(gathered_s[:], tab_s[:].indirect(offs_sb[:]))
         for q in QUADRANTS:
             nc.sync.dma_start(v_s[32 * q:32 * q + 4, :].bitcast(I32).rearrange("p (a c) -> p a c", a=2),
                               gathered_s[8 * q:8 * q + 8, :].bitcast(I32))
         load_w1(0, 0)
+        load_w2(1)
         nc.sync.dma_start(cg_sb[:].rearrange("p (b t) -> p b t", b=2), cg.rearrange("(b p t) -> p b t", b=2, t=PACK))
-        load_w1(0, 1)
-        load_w2_scales(nc.sync, 1)
-        load_w2(nc.sync, 1)
+        load_w1(0, 1, 0, PASS // 2)
+        load_w1(0, 1, PASS // 2, PASS)
         load_w1(1, 0)
         load_w1(1, 1)
         nc.sync.dma_start(pos1_sb[:], pos1)
@@ -155,10 +154,10 @@ def tile_list_crack_hedge_tilt_kernel(tc, tab_words, tab_scales, offs, pos1, pos
 
         def round_w1(b):
             parts = [placed([P, size], BF16, "w1_%d%d" % (b, a), AT_W1[b][a]) for a in range(2)]
-            for a in range(2):
-                nc.gpsimd.tensor_scalar(parts[a][:].rearrange("p (t m j) -> p m t j", t=PACK, j=PACK),
-                                        w1_raw[b][a][:].rearrange("p (j m t) -> p m t j", t=PACK, j=PACK),
-                                        1.0, 0.0, ALU.mult, ALU.add)
+            for a, lo, raw in w1_raw[b]:
+                first, count = lo // PACK, raw.shape[1] // (PACK * PACK)
+                nc.gpsimd.tensor_scalar(parts[a][:].rearrange("p (t m j) -> p m t j", t=PACK, j=PACK)[:, first:first + count],
+                                        raw[:].rearrange("p (j m t) -> p m t j", t=PACK, j=PACK), 1.0, 0.0, ALU.mult, ALU.add)
             return parts
 
         def quantize_pair(name, pair, offset):
@@ -172,10 +171,9 @@ def tile_list_crack_hedge_tilt_kernel(tc, tab_words, tab_scales, offs, pos1, pos
             part = sum(1 for edge in W2_EDGES[1:] if edge <= P * i)
             lo, hi = w2_cols[part]
             word = (hi - lo) * a + P * i - lo
-            b, t = divmod(i, PACK)
-            byte = PASS * a + P * t
+            byte = H * a + P * i
             nc.tensor.matmul_mx(out=acc, lhsT=w2_w[part][:, 2 * word:2 * (word + P)].bitcast(E2M1),
-                                lhsT_scale=w2_s[b][:, byte:byte + P], **table_operand(cols, a))
+                                lhsT_scale=w2_s[:, byte:byte + P], **table_operand(cols, a))
 
         def x_pass(acc, i, cols, a):
             b, t = divmod(i, PACK)

@@ -156,8 +156,8 @@ def tile_list_crack_hedge_tilt_kernel(tc, tab_words, tab_scales, offs, pos1, pos
             parts = [placed([P, size], BF16, "w1_%d%d" % (b, a), AT_W1[b][a]) for a in range(2)]
             for a, lo, raw in w1_raw[b]:
                 first, count = lo // PACK, raw.shape[1] // (PACK * PACK)
-                nc.gpsimd.tensor_scalar(parts[a][:].rearrange("p (t m j) -> p m t j", t=PACK, j=PACK)[:, first:first + count],
-                                        raw[:].rearrange("p (j m t) -> p m t j", t=PACK, j=PACK), 1.0, 0.0, ALU.mult, ALU.add)
+                nc.gpsimd.tensor_scalar(parts[a][:].rearrange("p (t m j) -> p m j t", t=PACK, j=PACK)[:, first:first + count],
+                                        raw[:].rearrange("p (j m t) -> p m j t", t=PACK, j=PACK), 1.0, 0.0, ALU.mult, ALU.add)
             return parts
 
         def quantize_pair(name, pair, offset):

from contextlib import ExitStack

import concourse.mybir as mybir

K, H, N, T, S, M = 1024, 1024, 512, 2048, 1024, 512
FLOPS = 2 * K * H * S * 2 + 2 * H * N * M * 2

F32 = mybir.dt.float32
BF16 = mybir.dt.bfloat16
I32 = mybir.dt.int32
U32 = mybir.dt.uint32
U16 = mybir.dt.uint16
U8 = mybir.dt.uint8
E4M3 = mybir.dt.float8_e4m3fn_x4
E2M1 = mybir.dt.float4_e2m1fn_x4
ALU = mybir.AluOpType
ACT = mybir.ActivationFunctionType

P = 128
PACK = 4
PASS = P * PACK
BANK = 512
BANKS = 8
TILES = H // P
N_TILES = N // P
LAST = TILES - 1
QUADRANTS = (0, 2, 1, 3)
WINDOWS = TILES
PIECES = [256, 128, 128]
W2_EDGES = [0, 4 * P, H]

Y_AHEAD = 4
P1_ON_VECTOR = (0, 1, 4)
P2_SPLIT = 256
FIRST_WIDTH = 256

KB = 1024
AT_W1_RAW = [0, 8 * KB]
AT_Z2_ROWS = 48 * KB
AT_W1 = [[24 * KB, 28 * KB], [30 * KB, 26 * KB]]
AT_Y_PICKED = 22 * KB
AT_Z2 = [24 * KB, 28 * KB]
AT_X = [32 * KB, 10 * KB]
AT_Z1 = 28 * KB


def tile_list_crack_hedge_tilt_kernel(tc, tab_words, tab_scales, offs, pos1, pos2, pos3, w1,
                                                    w2_words, w2_scales, w3_words, w3_scales, cg, rl, out):
    nc = tc.nc
    with ExitStack() as ctx:
        keep = ctx.enter_context(tc.tile_pool(name="keep", bufs=1))
        ring = ctx.enter_context(tc.tile_pool(name="ring", bufs=WINDOWS))
        staged = ctx.enter_context(tc.tile_pool(name="staged", bufs=1))
        psum = ctx.enter_context(tc.psum_pool(name="psum", bufs=1))

        def held(shape, dtype, name):
            return keep.tile(shape, dtype, name=name, align_bytes=64)

        def placed(shape, dtype, name, offset):
            return staged.tile(shape, dtype, name=name, align_bytes=64, offset=offset)

        def bank(index):
            return psum.tile([P, BANK], F32, name="bank", tag="bank%d" % index)

        def window():
            return ring.tile([P, S], F32, name="window", tag="window", align_bytes=64)

        offs_sb = keep.tile([P, S // 16], U16, name="offs_sb")
        pos1_sb = keep.tile([P, M // 16], U16, name="pos1_sb")
        pos2_sb = keep.tile([P, M // 16], U16, name="pos2_sb")
        pos3_sb = keep.tile([P, M // 16], U16, name="pos3_sb")
        tab_w = [held([P, T], I32, "tab_w%d" % a) for a in range(2)]
        tab_s = held([P, T], U8, "tab_s")
        v_w = [held([P, S], I32, "v_w%d" % a) for a in range(2)]
        gathered_s = held([P, S], U8, "gathered_s")
        v_s = held([P, 2 * S], U8, "v_s")
        w2_cols = list(zip(W2_EDGES, W2_EDGES[1:]))
        w2_w = [held([P, 2 * 2 * (hi - lo)], U8, "w2_w%d" % lo) for lo, hi in w2_cols]
        w2_s = held([P, 2 * H], U8, "w2_s")
        w3_s = held([P, N], U8, "w3_s")
        cg_sb = held([P, TILES], F32, "cg_sb")
        cg_step = held([P, TILES], F32, "cg_step")
        cg_sign = held([P, TILES], F32, "cg_sign")
        rl_sb = held([P, N_TILES], F32, "rl_sb")

        nc.vector.memset(w2_s[:].bitcast(I32), 0)
        nc.vector.memset(tab_s[32:64, :].bitcast(I32), 0)
        nc.vector.memset(tab_s[64:128, :].bitcast(I32), 0)
        nc.vector.memset(v_s[:].bitcast(I32), 0)
        nc.vector.memset(w3_s[:].bitcast(I32), 0)

        def load_words(a):
            nc.sync.dma_start(tab_w[a][:], tab_words[a].rearrange("p t i -> p (t i)").bitcast(I32))

        w1_raw = [[], []]

        def load_w1(b, a, lo=0, hi=PASS):
            shape, name = [P, PACK * (hi - lo)], "w1_raw%d%d_%d" % (b, a, lo)
            raw = placed(shape, F32, name, AT_W1_RAW[b]) if (a, hi) == (1, PASS) else held(shape, F32, name)
            src = w1[PASS * a:PASS * (a + 1), PASS * b + lo:PASS * b + hi].rearrange("(p j) c -> p j c", j=PACK)
            nc.sync.dma_start(raw[:].rearrange("p (j c) -> p j c", j=PACK), src)
            w1_raw[b].append((a, lo, raw))

        def load_w2(part):
            lo, hi = w2_cols[part]
            nc.sync.dma_start(w2_w[part][:].bitcast(I32).rearrange("p (a c) -> p a c", a=2),
                              w2_words[:, :, 2 * lo:2 * hi].bitcast(I32).rearrange("a p c -> p a c"))

        nc.sync.dma_start(offs_sb[:], offs)
        nc.sync.dma_start(tab_s[0:32, :].bitcast(I32), tab_scales.bitcast(I32).rearrange("a s c -> s a c"))
        load_words(0)
        nc.sync.dma_start(pos3_sb[:], pos3)
        load_words(1)
        for q in QUADRANTS:
            nc.scalar.dma_start(w2_s[32 * q:32 * q + 4, :].bitcast(I32).rearrange("p (a c) -> p a c", a=2),
                                w2_scales[:, 4 * q:4 * q + 4, :].bitcast(I32).rearrange("a s c -> s a c"))
        load_w2(0)
        nc.vector.tensor_copy(gathered_s[:], tab_s[:].indirect(offs_sb[:]))
        for q in QUADRANTS:
            nc.sync.dma_start(v_s[32 * q:32 * q + 4, :].bitcast(I32).rearrange("p (a c) -> p a c", a=2),
                              gathered_s[8 * q:8 * q + 8, :].bitcast(I32))
        load_w1(0, 0)
        load_w2(1)
        nc.sync.dma_start(cg_sb[:].rearrange("p (b t) -> p b t", b=2), cg.rearrange("(b p t) -> p b t", b=2, t=PACK))
        load_w1(0, 1, 0, PASS // 2)
        load_w1(0, 1, PASS // 2, PASS)
        load_w1(1, 0)
        load_w1(1, 1)
        nc.sync.dma_start(pos1_sb[:], pos1)
        nc.sync.dma_start(pos2_sb[:], pos2)

        nc.gpsimd.tensor_scalar(cg_step[:], cg_sb[:], 0.0, 2.0, ALU.is_ge, ALU.mult)
        nc.gpsimd.tensor_scalar(cg_sign[:], cg_step[:], -1.0, 1.0, ALU.add, ALU.mult)

        for a, width in enumerate([BANK, FIRST_WIDTH]):
            for lo in range(0, S, width):
                nc.vector.tensor_copy(v_w[a][:, lo:lo + width].bitcast(U32),
                                      tab_w[a][:].bitcast(U32).indirect(offs_sb[:, lo // 16:(lo + width) // 16]))

        def pick(on_scalar, dst, win, places):
            if on_scalar:
                nc.scalar.activation(dst, win[:].indirect(places), ACT.Copy)
            else:
                nc.vector.tensor_copy(dst, win[:].indirect(places))

        def quantize(name, values, offset=None):
            width = values.shape[1] // PACK
            codes = held([P, width], U32, name + "_w") if offset is None else placed([P, width], U32, name + "_w", offset)
            plane = held([P, width], U8, name + "_s")
            nc.vector.quantize_mx(out=codes[:].bitcast(E4M3), scales=plane[:], in_=values)
            return codes, plane

        size = PACK * PASS

        def round_w1(b):
            parts = [placed([P, size], BF16, "w1_%d%d" % (b, a), AT_W1[b][a]) for a in range(2)]
            for a, lo, raw in w1_raw[b]:
                first, count = lo // PACK, raw.shape[1] // (PACK * PACK)
                nc.gpsimd.tensor_scalar(parts[a][:].rearrange("p (t m j) -> p m j t", t=PACK, j=PACK)[:, first:first + count],
                                        raw[:].rearrange("p (j m t) -> p m j t", t=PACK, j=PACK), 1.0, 0.0, ALU.mult, ALU.add)
            return parts

        def quantize_pair(name, pair, offset):
            return [quantize(name + "0", pair[0][:], offset), quantize(name + "1", pair[1][:])]

        def table_operand(cols, a):
            return dict(rhs=v_w[a][:, cols].bitcast(E4M3), rhs_scale=v_s[:, S * a + cols.start:S * a + cols.stop],
                        start=(a == 0), stop=(a == 1))

        def y_pass(acc, i, cols, a):
            part = sum(1 for edge in W2_EDGES[1:] if edge <= P * i)
            lo, hi = w2_cols[part]
            word = (hi - lo) * a + P * i - lo
            byte = H * a + P * i
            nc.tensor.matmul_mx(out=acc, lhsT=w2_w[part][:, 2 * word:2 * (word + P)].bitcast(E2M1),
                                lhsT_scale=w2_s[:, byte:byte + P], **table_operand(cols, a))

        def x_pass(acc, i, cols, a):
            b, t = divmod(i, PACK)
            codes, plane = w1_mx[b][a]
            word = P * t
            nc.tensor.matmul_mx(out=acc, lhsT=codes[:, word:word + P].bitcast(E4M3),
                                lhsT_scale=plane[:, word:word + P], **table_operand(cols, a))

        def o_pass(acc, n, b, z, cols, start, stop):
            word = N * b + P * n
            codes, plane = z
            nc.tensor.matmul_mx(out=acc, lhsT=w3_w[:, word:word + P].bitcast(E4M3), lhsT_scale=w3_s[4 * b:, P * n:P * (n + 1)],
                                rhs=codes[:, cols].bitcast(E4M3), rhs_scale=plane[:, cols], start=start, stop=stop)

        z2_rows = [held([P, PACK * M], BF16, "z2_rows0"), placed([P, PACK * M], BF16, "z2_rows1", AT_Z2_ROWS)]

        y_picked = []

        def pick_y(i):
            b, quarter = divmod(i, PACK)
            if i < Y_AHEAD or i == LAST:
                y_picked.append(held([P, M], BF16, "y_picked%d" % i)[:])
            elif i == Y_AHEAD:
                group = placed([P, M * (LAST - i)], BF16, "y_picked%d" % i, AT_Y_PICKED)
                y_picked.extend(group[:, M * e:M * (e + 1)] for e in range(LAST - i))
            pick(i == LAST, y_picked[i], y_win[i], pos3_sb[:])
            nc.sync.dma_start(z2_rows[b][32 * quarter:32 * (quarter + 1), :].bitcast(I32).rearrange("p (j c) -> p j c", j=PACK),
                              y_picked[i].bitcast(I32))

        def fill_window(g, one_pass, i, **scale):
            win = window()
            for h in range(2):
                acc = bank((2 * g + h) % BANKS)
                cols = slice(BANK * h, BANK * (h + 1))
                for a in range(2):
                    one_pass(acc[:], i, cols, a)
                nc.scalar.activation(win[:, cols], acc[:], ACT.Copy, **scale)
            return win

        first_cols = [slice(lo, lo + FIRST_WIDTH) for lo in range(0, S, FIRST_WIDTH)]
        first_banks = [[bank(2 * q + i) for i in range(2)] for q in range(len(first_cols))]
        y_win = [window() for i in range(2)]
        for i, q in [(0, 0), (0, 1), (0, 2), (1, 0), (0, 3), (1, 1), (1, 2), (1, 3)]:
            cols = first_cols[q]
            for a in range(2):
                y_pass(first_banks[q][i][:, 0:FIRST_WIDTH], i, cols, a)
            nc.scalar.copy(y_win[i][:, cols], first_banks[q][i][:, 0:FIRST_WIDTH])
        for i in range(2, TILES):
            y_win.append(fill_window(i - 2, y_pass, i))

        w1_first = round_w1(0)
        for i in range(Y_AHEAD):
            pick_y(i)
        w1_mx = [quantize_pair("w1_0", w1_first, AT_W1_RAW[0])]
        w1_second = round_w1(1)
        for i in range(Y_AHEAD, TILES):
            pick_y(i)

        w3_w = held([P, 2 * N], I32, "w3_w")
        nc.sync.dma_start(w3_w[:].rearrange("p (a c) -> p a c", a=2),
                          w3_words.rearrange("a p c i -> p a (c i)").bitcast(I32))
        for q in QUADRANTS:
            nc.sync.dma_start(w3_s[32 * q:32 * q + 8, :].bitcast(I32), w3_scales[:, 4 * q:4 * q + 4, :].bitcast(I32))
        with nc.allow_non_contiguous_dma(reason="one ratio for each partition"):
            nc.sync.dma_start(rl_sb[:], rl.rearrange("(n p) -> p n", p=P))

        p1_raw = {(0, 0): held([P, M], F32, "p1_raw")[:]}

        def picked_tile(b):
            both = placed([P, 2 * PACK * M], F32, "x_picked%d" % b, AT_X[b])
            return both[:, 0:PACK * M], both[:, PACK * M:2 * PACK * M]

        def x_window(i):
            return fill_window(TILES - 2 + i, x_pass, i, scale=cg_sign[:, i:i + 1])

        def pick_p1(i, lo, hi):
            b, t = divmod(i, PACK)
            dst = p1_raw.setdefault((i, lo), x_picked[b][0][:, M * t + lo:M * t + hi])
            pick(i not in P1_ON_VECTOR and (i, lo) != (LAST, 0), dst, x_win[i], pos1_sb[:, lo // 16:hi // 16])

        def pick_p2(i, lo, hi):
            b, t = divmod(i, PACK)
            pick(i == LAST and lo >= P2_SPLIT, x_picked[b][1][:, M * t + lo:M * t + hi], x_win[i], pos2_sb[:, lo // 16:hi // 16])

        def scaled_abs(i, lo, hi):
            b, t = divmod(i, PACK)
            nc.scalar.activation(x_picked[b][0][:, M * t + lo:M * t + hi], p1_raw[i, lo], ACT.Abs, scale=cg_sb[:, i:i + 1])

        def form_z1(engine, dst, b, lo, hi):
            def walk(tiles):
                return tiles.rearrange("p (t m) -> p t m", t=PACK)[:, :, lo:hi].rearrange("p t (c i) -> p c t i", i=2)
            x1, x2 = x_picked[b]
            engine.tensor_tensor(dst.rearrange("p (c i t) -> p c t i", t=PACK, i=2), walk(x1), walk(x2), ALU.mult)
            return dst

        def weave_z2():
            halves = [placed([P, PACK * M], BF16, "z2_woven%d" % b, AT_Z2[b]) for b in range(2)]
            for b in range(2):
                nc.gpsimd.tensor_scalar(halves[b][:].rearrange("p (m t) -> p m t", t=PACK),
                                        z2_rows[b][:].rearrange("p (t m) -> p m t", t=PACK), 1.0, 0.0, ALU.mult, ALU.add)
            return halves

        x_win = [x_window(i) for i in range(PACK)]
        x_picked = [picked_tile(0)]
        pick_p1(0, 0, M)
        w1_mx.append(quantize_pair("w1_1", w1_second, AT_W1_RAW[1]))
        z2_woven = weave_z2()
        for i in range(1, PACK):
            pick_p1(i, 0, M)
        for i in range(PACK):
            scaled_abs(i, 0, M)
        x_win.append(x_window(PACK))
        for i in range(PACK):
            pick_p2(i, 0, M)
        z2 = quantize_pair("z2_", z2_woven, AT_Z2_ROWS)
        z1_rounded = form_z1(nc.gpsimd, placed([P, PACK * M], BF16, "z1_first", AT_Z1)[:], 0, 0, M)
        x_picked.append(picked_tile(1))
        for i in range(PACK, LAST):
            x_win.append(x_window(i + 1))
            pick_p1(i, 0, M)
            pick_p2(i, 0, M)
            if i > PACK:
                scaled_abs(i - 1, 0, M)
        scaled_abs(LAST - 1, 0, M)

        edges = [sum(PIECES[:u]) for u in range(len(PIECES) + 1)]
        spans = list(zip(edges, edges[1:]))

        half = M // 2
        halves = [(0, half), (half, M)]
        o2_banks = []
        for g in range(N_TILES):
            h, pair = divmod(g, 2)
            o2_banks.append(bank(g))
            for e in range(2):
                for b in range(2):
                    o_pass(o2_banks[g][:, half * e:half * (e + 1)], 2 * pair + e, b, z2[b], slice(*halves[h]),
                           e + b == 0, e + b == 2)

        for lo, hi in halves:
            pick_p1(LAST, lo, hi)
            pick_p2(LAST, lo, hi)
            scaled_abs(LAST, lo, hi)
        o1 = []
        free_banks = list(range(N_TILES, BANKS))

        def open_o1(pieces):
            first, last = spans[pieces[0]][0], spans[pieces[-1]][1]
            z1_first = quantize("z1_0%d" % pieces[0], z1_rounded[:, PACK * first:PACK * last])
            for u in pieces:
                lo, hi = spans[u]
                width = hi - lo
                share = BANK // width
                banks = [bank(free_banks.pop(0)) for g in range(N_TILES // share)]
                o1.append([banks[n // share][:, width * (n % share):width * (n % share + 1)] for n in range(N_TILES)])
                for n in range(N_TILES):
                    o_pass(o1[u][n], n, 0, z1_first, slice(lo - first, hi - first), n % share == 0, False)

        open_o1([0])
        o2 = [held([P, BANK], F32, "o2_%d" % g) for g in range(N_TILES)]

        def o2_part(n, lo, hi):
            h = lo // half
            first = half * (n % 2) + lo - half * h
            return o2[2 * h + n // 2][:, first:first + hi - lo]

        def close_o1(u):
            lo, hi = spans[u]
            share = BANK // (hi - lo)
            z1_piece = quantize("z1_1%d" % u, z1_second[u])
            for n in range(N_TILES):
                o_pass(o1[u][n], n, 1, z1_piece, slice(0, hi - lo), False, n % share == share - 1)

        def finish(u):
            lo, hi = spans[u]
            width = hi - lo
            groups = [(0, 1), (2, 3)] if u + 1 < len(PIECES) else [(0, 1), (2,), (3,)]
            for group in groups:
                tilt = held([P, len(group) * width], F32, "tilt%d%d" % (u, group[0]))
                for e, n in enumerate(group):
                    nc.vector.scalar_tensor_tensor(tilt[:, width * e:width * (e + 1)], o1[u][n], rl_sb[:, n:n + 1],
                                                   o2_part(n, lo, hi), ALU.mult, ALU.subtract)
                nc.scalar.activation(tilt[:], tilt[:], ACT.Tanh)
                dst = out[P * group[0]:P * (group[-1] + 1), lo:hi].rearrange("(e p) m -> p e m", p=P)
                nc.sync.dma_start(dst, tilt[:].rearrange("p (e m) -> p e m", e=len(group)))

        for g in range(N_TILES):
            nc.scalar.copy(o2[g][:], o2_banks[g][:])
        z1_second = []
        for s in range(len(PIECES) + 2):
            if s < len(PIECES):
                z1_second.append(form_z1(nc.vector, held([P, PACK * PIECES[s]], BF16, "z1_second%d" % s)[:], 1, *spans[s]))
            if 0 <= s - 1 < len(PIECES):
                close_o1(s - 1)
            if s == 1:
                open_o1([1, 2])
            if 0 <= s - 2 < len(PIECES):
                finish(s - 2)
